import numpy as np
import ml_dtypes


def mxq(x, axis, fmt="e4m3"):
    dtype, down = {"e4m3": (ml_dtypes.float8_e4m3fn, 7), "e5m2": (ml_dtypes.float8_e5m2, 14)}[fmt]
    v = np.moveaxis(np.asarray(x, np.float32).astype(ml_dtypes.bfloat16).astype(np.float64), axis, -1)
    blocks = v.reshape(v.shape[:-1] + (-1, 32))
    amax = np.abs(blocks).max(-1, keepdims=True)
    byte = np.maximum(np.where(amax > 0, np.frexp(amax)[1] - 1 + 127, 0) - down, 1)
    scale = np.exp2(byte - 127.0)
    codes = (blocks / scale).astype(np.float32).astype(dtype).astype(np.float64)
    return np.moveaxis((codes * scale).reshape(v.shape), -1, axis)


WIDE = False


def mx_kscale(k):
    if not WIDE:
        return np.ones(k)
    levels = np.array([10, -10, 5, -5, 0])
    if k % 512:
        return np.exp2(np.random.permutation(np.resize(levels, k // 32))).repeat(32)
    a = np.empty((k // 512, 16))
    for p in range(k // 512):
        a[p, :8] = np.random.permutation(np.resize(levels, 8))
        for g in range(8):
            far = levels[np.abs(levels - a[p, g]) >= 10]
            a[p, g + 8] = far[np.random.randint(len(far))]
    return np.exp2(a.ravel()).repeat(32)


def f64(x):
    return np.asarray(x).astype(np.float64)


def striped(idx):
    return np.tile(idx.reshape(-1, 16).T, (8, 1)).astype(np.uint16)


def unstriped(offs):
    return offs[:16].T.reshape(-1).astype(np.int64)


E2M1 = np.array([0.0, 0.5, 1.0, 1.5, 2.0, 3.0, 4.0, 6.0, -0.0, -0.5, -1.0, -1.5, -2.0, -3.0, -4.0, -6.0])


def pack_weight(w, fmt):
    k, n = w.shape
    w = f64(np.asarray(w, np.float32).astype(ml_dtypes.bfloat16)).reshape(k // 32, 32, n)
    amax = np.abs(w).max(1)
    if fmt == "e4m3":
        byte = np.frexp(amax)[1] - 1 + 127 - 7
    else:
        mant, ex = np.frexp(amax / 6.0)
        byte = np.where(mant > 0.5, ex, ex - 1) + 127
    byte = np.clip(np.where(amax > 0, byte, 1), 1, 254)
    scaled = (w * np.exp2(127.0 - byte)[:, None, :]).reshape(k, n).astype(np.float32)
    by_word = np.ascontiguousarray(scaled.reshape(k // 512, 128, 4, n).transpose(0, 1, 3, 2))
    if fmt == "e4m3":
        words = by_word.astype(ml_dtypes.float8_e4m3fn).view(np.uint8)
    else:
        c = by_word.astype(ml_dtypes.float4_e2m1fn).view(np.uint8) & 0xF
        words = (c[..., 0::2] | (c[..., 1::2] << 4)).reshape(k // 512, 128, 2 * n)
    return np.ascontiguousarray(words), np.ascontiguousarray(byte.astype(np.uint8).reshape(k // 512, 16, n))


def unpack_weight(words, scales, fmt):
    g, _, n = scales.shape
    words = np.ascontiguousarray(words).reshape(g, 128, n, -1)
    if fmt == "e4m3":
        vals = words.view(ml_dtypes.float8_e4m3fn).astype(np.float64)
    else:
        nib = np.empty((g, 128, n, 4), np.uint8)
        nib[..., 0::2] = words & 0xF
        nib[..., 1::2] = words >> 4
        vals = E2M1[nib]
    vals = vals * np.repeat(np.exp2(scales.astype(np.float64) - 127.0), 8, axis=1)[..., None]
    return vals.transpose(0, 1, 3, 2).reshape(g * 512, n)


def d_silu(v):
    s = 1.0 / (1.0 + np.exp(-np.maximum(v, -700.0)))
    return s * (1.0 + v * (1.0 - s))


K, T, E, C, H, N = 512, 1024, 4, 256, 512, 1024


def by_expert(wq, xq):
    return np.concatenate([wq[e].T @ xq[:, e * C:(e + 1) * C] for e in range(E)], axis=1)


def setup_inputs():
    n = np.random.standard_normal
    s = mx_kscale(K)
    v = mx_kscale(N)
    u = mx_kscale(H)
    slot_token = np.random.permutation(T)[:E * C]
    w_slot = np.random.uniform(0.2, 1.0, E * C)
    x = pack_weight(n((K, T)) * s[:, None], "e4m3")
    dy = pack_weight(n((N, T)) * v[:, None], "e4m3")
    m1 = n((E, K, H))
    w1 = [pack_weight(m, "e4m3") for m in m1 / np.sqrt(K) / s[None, :, None]]
    w2t = [pack_weight(m, "e4m3") for m in n((E, N, H)) / np.sqrt(N) / v[None, :, None] * u]
    w1t = [pack_weight(m, "e4m3") for m in m1.transpose(0, 2, 1) / np.sqrt(H) / u[None, :, None]]
    return {
        "x_words": x[0],
        "x_scales": x[1],
        "dy_words": dy[0],
        "dy_scales": dy[1],
        "w1_words": np.stack([m[0] for m in w1]),
        "w1_scales": np.stack([m[1] for m in w1]),
        "w2t_words": np.stack([m[0] for m in w2t]),
        "w2t_scales": np.stack([m[1] for m in w2t]),
        "w1t_words": np.stack([m[0] for m in w1t]),
        "w1t_scales": np.stack([m[1] for m in w1t]),
        "gate": (np.tile(w_slot, (128, 1))).astype(np.float32),
        "offs": striped(slot_token),
    }


def reference(x_words, x_scales, dy_words, dy_scales, w1_words, w1_scales, w2t_words, w2t_scales, w1t_words, w1t_scales, gate, offs):
    w1 = np.stack([unpack_weight(w1_words[e], w1_scales[e], "e4m3") for e in range(E)])
    w2t = np.stack([unpack_weight(w2t_words[e], w2t_scales[e], "e4m3") for e in range(E)])
    w1t = np.stack([unpack_weight(w1t_words[e], w1t_scales[e], "e4m3") for e in range(E)])
    idx = unstriped(offs)
    xq = unpack_weight(x_words, x_scales, "e4m3")[:, idx]
    gq = unpack_weight(dy_words, dy_scales, "e4m3")[:, idx]
    dh = f64(gate[:1]) * by_expert(w2t, gq)
    a = by_expert(w1, xq)
    dx = by_expert(w1t, mxq(dh * d_silu(a), 0, "e4m3"))
    out = np.zeros((K, T))
    out[:, idx] = dx
    return out

@@ -1,0 +1,193 @@
+from contextlib import ExitStack
+
+import concourse.mybir as mybir
+from concourse.masks import make_identity
+
+K, T, E, C, H, N = 512, 1024, 4, 256, 512, 1024
+FLOPS = 2 * E * C * (K * H + N * H + H * K)
+
+F32 = mybir.dt.float32
+BF16 = mybir.dt.bfloat16
+I32 = mybir.dt.int32
+U32 = mybir.dt.uint32
+U16 = mybir.dt.uint16
+U8 = mybir.dt.uint8
+FP8X4 = mybir.dt.float8_e4m3fn_x4
+ACT = mybir.ActivationFunctionType
+ALU = mybir.AluOpType
+
+P = 128
+PACK = 4
+QUADS = 4
+SLOT_TILES = C // P
+K_TILES = K // P
+PASSES = N // (P * PACK)
+STRIPE = 16
+
+
+def tile_moe_rec_mlp_silu_kernel(tc, x_words, x_scales, dy_words, dy_scales, w1_words, w1_scales, w2t_words, w2t_scales, w1t_words, w1t_scales, gate, offs, out):
+    nc = tc.nc
+    with ExitStack() as ctx:
+        keep = ctx.enter_context(tc.tile_pool(name="keep", bufs=1))
+        work = ctx.enter_context(tc.tile_pool(name="work", bufs=3))
+        psum = ctx.enter_context(tc.psum_pool(name="psum", bufs=2))
+
+        offsets = keep.tile([P, T // STRIPE], U16, name="offsets")
+        nc.sync.dma_start(offsets[:], offs)
+
+        def scale_tile(name, width):
+            plane = keep.tile([P, width], U8, name=name, align_bytes=64)
+            nc.vector.memset(plane[:].bitcast(I32), 0)
+            return plane
+
+        def load_scales(plane, planes):
+            rows = planes.shape[0] * 4
+            for q in range(QUADS):
+                nc.sync.dma_start(plane[32 * q : 32 * q + rows, :].bitcast(I32), planes[:, 4 * q : 4 * q + 4, :].bitcast(I32))
+
+        def load_words(name, words):
+            tile = keep.tile([P, words.shape[1]], I32, name=name, align_bytes=64)
+            nc.sync.dma_start(tile[:], words.rearrange("p c d -> p (c d)").bitcast(I32))
+            return tile
+
+        xs = scale_tile("xs", T)
+        dys = scale_tile("dys", T)
+        w1s = scale_tile("w1s", H)
+        w2s = [scale_tile(f"w2s{h}", H) for h in range(2)]
+        w1ts = scale_tile("w1ts", K)
+        w2_planes = w2t_scales.rearrange("e s b i -> (e s) b i")
+
+        warm = keep.tile([P, 1], F32, name="warm")
+        warm_out = keep.tile([P, 1], F32, name="warm_out")
+        nc.vector.memset(warm[:], 0.0)
+        nc.scalar.activation(warm_out[:], warm[:], ACT.Silu)
+
+        ident = keep.tile([P, P], F32, name="ident")
+        make_identity(nc, ident[:])
+
+        w1, w2, w1t = {}, {}, {}
+
+        def load_front(e):
+            w1[e] = load_words(f"w1_{e}", w1_words[e, 0])
+            tile = keep.tile([P, PASSES, H], I32, name=f"w2_{e}", align_bytes=64)
+            nc.sync.dma_start(tile[:], w2t_words[e].rearrange("s p c d -> p s (c d)").bitcast(I32))
+            w2[e] = tile
+
+        def load_back(e):
+            w1t[e] = load_words(f"w1t_{e}", w1t_words[e, 0])
+
+        load_scales(xs, x_scales)
+        xw = load_words("xw", x_words[0])
+        load_scales(dys, dy_scales)
+        dyw = [load_words(f"dyw{s}", dy_words[s]) for s in range(PASSES)]
+        load_scales(w1s, w1_scales[:, 0])
+        load_scales(w2s[0], w2_planes[0:4])
+        load_front(0)
+        gate_rows = keep.tile([P, P], F32, name="gate_rows")
+        nc.sync.dma_start(gate_rows[:], gate[0:16, :].rearrange("a (c m) -> (a c) m", m=P))
+        load_front(1)
+        load_scales(w1ts, w1t_scales[:, 0])
+        load_scales(w2s[1], w2_planes[4:8])
+        load_back(0)
+        load_front(2)
+        load_back(1)
+        load_front(3)
+        load_back(2)
+        load_back(3)
+
+        gate_ps = psum.tile([P, 512], F32, name="gate_ps", tag="turn")
+        nc.tensor.transpose(gate_ps[:, 0:P], gate_rows[:], ident[:])
+        half_gate = keep.tile([P, E * SLOT_TILES], F32, name="half_gate")
+        nc.scalar.activation(half_gate[:], gate_ps[:, 0 : E * SLOT_TILES], ACT.Copy, scale=-0.5)
+
+        windows = [keep.tile([P, T], F32, name=f"window{j}") for j in range(K_TILES)]
+
+        def listed(e):
+            return offsets[:, e * C // STRIPE : (e + 1) * C // STRIPE]
+
+        got = {}
+
+        def gather(e):
+            def one(name, window, dtype):
+                tile = keep.tile([P, C], dtype, name=f"{name}_{e}", align_bytes=64)
+                nc.vector.tensor_copy(tile[:], window.indirect(listed(e)))
+                return tile
+
+            gxs = one("gxs", xs[:], U8)
+            gx = one("gx", xw[:].bitcast(U32), U32)
+            gds = one("gds", dys[:], U8)
+            gd = [one(f"gd{s}", dyw[s][:].bitcast(U32), U32) for s in range(PASSES)]
+            got[e] = (gx, gxs, gd, gds)
+
+        grouped = {}
+
+        def front(e):
+            gx, gxs, gd, gds = got[e]
+            turned = psum.tile([P, SLOT_TILES, 2, P], F32, name="turned", tag="turn")
+            for c in range(SLOT_TILES):
+                cols = slice(c * P, (c + 1) * P)
+                a_ps = psum.tile([P, H], F32, name="a_ps")
+                nc.tensor.matmul_mx(a_ps[:], lhsT=gx[:, cols].bitcast(FP8X4), lhsT_scale=gxs[:, cols],
+                                    rhs=w1[e][:].bitcast(FP8X4), rhs_scale=w1s[4 * e :, :], start=True, stop=True)
+                dh_ps = psum.tile([P, H], F32, name="dh_ps")
+                for s in range(PASSES):
+                    plane = (PASSES * e + s) % 4
+                    nc.tensor.matmul_mx(dh_ps[:], lhsT=gd[s][:, cols].bitcast(FP8X4), lhsT_scale=gds[4 * s :, cols],
+                                        rhs=w2[e][:, s, :].bitcast(FP8X4), rhs_scale=w2s[e // 2][4 * plane :, :],
+                                        start=(s == 0), stop=(s == PASSES - 1))
+                silu_neg = work.tile([P, H], F32, name="silu_neg")
+                nc.scalar.activation(silu_neg[:], a_ps[:], ACT.Silu, scale=-1.0)
+                tanh_half = work.tile([P, H], F32, name="tanh_half")
+                nc.scalar.activation(tanh_half[:], a_ps[:], ACT.Tanh, scale=0.5)
+                g = half_gate[:, e * SLOT_TILES + c : e * SLOT_TILES + c + 1]
+                gated = work.tile([P, H], F32, name="gated")
+                nc.scalar.activation(gated[:], tanh_half[:], ACT.Identity, bias=g, scale=g)
+                part = work.tile([P, H], F32, name="part")
+                nc.vector.scalar_tensor_tensor(part[:], silu_neg[:], 1.0, dh_ps[:], ALU.subtract, ALU.mult)
+                da = work.tile([P, H], BF16, name="da")
+                nc.vector.tensor_tensor(da[:], gated[:], part[:], ALU.mult)
+                pairs = da[:].bitcast(F32)
+                for u in range(2):
+                    nc.tensor.transpose(turned[:, c, u, :], pairs[:, u : H // 2 : 2], ident[:])
+            tile = work.tile([P, C * PACK], BF16, name="grouped", align_bytes=64)
+            nc.scalar.copy(tile[:].bitcast(F32).rearrange("p (c r u) -> p c r u", c=SLOT_TILES, u=2), turned[:].rearrange("p c u r -> p c r u"))
+            grouped[e] = tile
+
+        staged = {}
+
+        def back(e):
+            codes = work.tile([P, C], U32, name="codes", align_bytes=64)
+            scales = work.tile([P, C], U8, name="scales", align_bytes=64)
+            nc.vector.quantize_mx(out=codes[:].bitcast(FP8X4), scales=scales[:], in_=grouped[e][:])
+            for h in range(K_TILES // 2):
+                dx_ps = psum.tile([P, 2, C], F32, name="dx_ps")
+                for i in range(2):
+                    cols = slice((2 * h + i) * P, (2 * h + i + 1) * P)
+                    nc.tensor.matmul_mx(dx_ps[:, i, :], lhsT=w1t[e][:, cols].bitcast(FP8X4), lhsT_scale=w1ts[4 * e :, cols],
+                                        rhs=codes[:].bitcast(FP8X4), rhs_scale=scales[:], start=True, stop=True)
+                dx = keep.tile([P, 2, C], F32, name=f"dx_{e}_{h}")
+                nc.scalar.copy(dx[:], dx_ps[:])
+                staged[e, h] = dx
+
+        def scatter(e):
+            for j in range(K_TILES):
+                nc.vector.tensor_copy(windows[j][:].indirect(listed(e)), staged[e, j // 2][:, j % 2, :])
+                if e == E - 1:
+                    nc.sync.dma_start(out[j * P : (j + 1) * P, :], windows[j][:])
+
+        gather(0)
+        gather(1)
+        front(0)
+        gather(2)
+        back(0)
+        front(1)
+        gather(3)
+        back(1)
+        front(2)
+        scatter(0)
+        back(2)
+        front(3)
+        scatter(1)
+        back(3)
+        scatter(2)
+        scatter(3)

@@ -29,7 +29,8 @@ def tile_moe_rec_mlp_silu_kernel(tc, x_words, x_scales, dy_words, dy_scales, w1_
     nc = tc.nc
     with ExitStack() as ctx:
         keep = ctx.enter_context(tc.tile_pool(name="keep", bufs=1))
-        work = ctx.enter_context(tc.tile_pool(name="work", bufs=3))
+        work = ctx.enter_context(tc.tile_pool(name="work", bufs=4))
+        arena = ctx.enter_context(tc.tile_pool(name="arena", bufs=1))
         psum = ctx.enter_context(tc.psum_pool(name="psum", bufs=2))
 
         offsets = keep.tile([P, T // STRIPE], U16, name="offsets")
@@ -50,9 +51,8 @@ def tile_moe_rec_mlp_silu_kernel(tc, x_words, x_scales, dy_words, dy_scales, w1_
             nc.sync.dma_start(tile[:], words.rearrange("p c d -> p (c d)").bitcast(I32))
             return tile
 
-        xs = scale_tile("xs", T)
-        dys = scale_tile("dys", T)
         w1s = scale_tile("w1s", H)
+        dys = scale_tile("dys", T)
         w2s = [scale_tile(f"w2s{h}", H) for h in range(2)]
         w1ts = scale_tile("w1ts", K)
         w2_planes = w2t_scales.rearrange("e s b i -> (e s) b i")
@@ -62,13 +62,12 @@ def tile_moe_rec_mlp_silu_kernel(tc, x_words, x_scales, dy_words, dy_scales, w1_
         nc.vector.memset(warm[:], 0.0)
         nc.scalar.activation(warm_out[:], warm[:], ACT.Silu)
 
-        ident = keep.tile([P, P], F32, name="ident")
-        make_identity(nc, ident[:])
-
         w1, w2, w1t = {}, {}, {}
 
-        def load_front(e):
+        def load_w1(e):
             w1[e] = load_words(f"w1_{e}", w1_words[e, 0])
+
+        def load_w2(e):
             tile = keep.tile([P, PASSES, H], I32, name=f"w2_{e}", align_bytes=64)
             nc.sync.dma_start(tile[:], w2t_words[e].rearrange("s p c d -> p s (c d)").bitcast(I32))
             w2[e] = tile
@@ -76,22 +75,33 @@ def tile_moe_rec_mlp_silu_kernel(tc, x_words, x_scales, dy_words, dy_scales, w1_
         def load_back(e):
             w1t[e] = load_words(f"w1t_{e}", w1t_words[e, 0])
 
-        load_scales(xs, x_scales)
-        xw = load_words("xw", x_words[0])
-        load_scales(dys, dy_scales)
-        dyw = [load_words(f"dyw{s}", dy_words[s]) for s in range(PASSES)]
+        ident = keep.tile([P, P], F32, name="ident")
+        make_identity(nc, ident[:])
+
+        xs = keep.tile([P, T], U8, name="xs", align_bytes=64)
+        for q in range(QUADS):
+            rows = x_scales[:, 4 * q : 4 * q + 4, :].bitcast(I32)
+            nc.sync.dma_start(xs[32 * q : 32 * q + 32, :].bitcast(I32), rows.to_broadcast([8, 4, T // 4]))
         load_scales(w1s, w1_scales[:, 0])
-        load_scales(w2s[0], w2_planes[0:4])
-        load_front(0)
+        xw = load_words("xw", x_words[0])
+        load_w1(0)
         gate_rows = keep.tile([P, P], F32, name="gate_rows")
         nc.sync.dma_start(gate_rows[:], gate[0:16, :].rearrange("a (c m) -> (a c) m", m=P))
-        load_front(1)
-        load_scales(w1ts, w1t_scales[:, 0])
+        load_scales(dys, dy_scales)
+        dyw = [load_words("dyw0", dy_words[0])]
+        load_w1(1)
+        dyw.append(load_words("dyw1", dy_words[1]))
+        load_scales(w2s[0], w2_planes[0:4])
         load_scales(w2s[1], w2_planes[4:8])
+        load_w2(0)
+        load_w1(2)
+        load_w2(1)
+        load_w1(3)
+        load_scales(w1ts, w1t_scales[:, 0])
         load_back(0)
-        load_front(2)
+        load_w2(2)
+        load_w2(3)
         load_back(1)
-        load_front(3)
         load_back(2)
         load_back(3)
 
@@ -100,60 +110,64 @@ def tile_moe_rec_mlp_silu_kernel(tc, x_words, x_scales, dy_words, dy_scales, w1_
         half_gate = keep.tile([P, E * SLOT_TILES], F32, name="half_gate")
         nc.scalar.activation(half_gate[:], gate_ps[:, 0 : E * SLOT_TILES], ACT.Copy, scale=-0.5)
 
-        windows = [keep.tile([P, T], F32, name=f"window{j}") for j in range(K_TILES)]
+        def seat(e, c):
+            return (3 * e + c) * 8192 + 4096
 
-        def listed(e):
-            return offsets[:, e * C // STRIPE : (e + 1) * C // STRIPE]
+        def listed(experts):
+            return offsets[:, experts[0] * C // STRIPE : (experts[-1] + 1) * C // STRIPE]
 
-        got = {}
+        halves = ((0, 1), (2, 3))
 
-        def gather(e):
-            def one(name, window, dtype):
-                tile = keep.tile([P, C], dtype, name=f"{name}_{e}", align_bytes=64)
-                nc.vector.tensor_copy(tile[:], window.indirect(listed(e)))
-                return tile
+        def gather(name, window, dtype, half):
+            tile = keep.tile([P, 2 * C], dtype, name=f"{name}_{half}", align_bytes=64)
+            nc.vector.tensor_copy(tile[:], window.indirect(listed(halves[half])))
+            return tile
 
-            gxs = one("gxs", xs[:], U8)
-            gx = one("gx", xw[:].bitcast(U32), U32)
-            gds = one("gds", dys[:], U8)
-            gd = [one(f"gd{s}", dyw[s][:].bitcast(U32), U32) for s in range(PASSES)]
-            got[e] = (gx, gxs, gd, gds)
+        gxs, gx = [], []
+        for half in range(2):
+            gxs.append(gather("gxs", xs[:], U8, half))
+            gx.append(gather("gx", xw[:].bitcast(U32), U32, half))
+        gds = [gather("gds", dys[:], U8, half) for half in range(2)]
+        gd = [[gather(f"gd{s}", dyw[s][:].bitcast(U32), U32, half) for s in range(PASSES)] for half in range(2)]
 
         grouped = {}
 
         def front(e):
-            gx, gxs, gd, gds = got[e]
+            half, first = e // 2, e % 2 * C
             turned = psum.tile([P, SLOT_TILES, 2, P], F32, name="turned", tag="turn")
+            a_ps, part = {}, {}
             for c in range(SLOT_TILES):
-                cols = slice(c * P, (c + 1) * P)
-                a_ps = psum.tile([P, H], F32, name="a_ps")
-                nc.tensor.matmul_mx(a_ps[:], lhsT=gx[:, cols].bitcast(FP8X4), lhsT_scale=gxs[:, cols],
+                cols = slice(first + c * P, first + (c + 1) * P)
+                a_ps[c] = psum.tile([P, H], F32, name="a_ps")
+                nc.tensor.matmul_mx(a_ps[c][:], lhsT=gx[half][:, cols].bitcast(FP8X4), lhsT_scale=gxs[half][:, cols],
                                     rhs=w1[e][:].bitcast(FP8X4), rhs_scale=w1s[4 * e :, :], start=True, stop=True)
+                silu_neg = work.tile([P, H], F32, name="silu_neg", bufs=8)
+                nc.scalar.activation(silu_neg[:], a_ps[c][:], ACT.Silu, scale=-1.0)
                 dh_ps = psum.tile([P, H], F32, name="dh_ps")
                 for s in range(PASSES):
                     plane = (PASSES * e + s) % 4
-                    nc.tensor.matmul_mx(dh_ps[:], lhsT=gd[s][:, cols].bitcast(FP8X4), lhsT_scale=gds[4 * s :, cols],
+                    nc.tensor.matmul_mx(dh_ps[:], lhsT=gd[half][s][:, cols].bitcast(FP8X4), lhsT_scale=gds[half][4 * s :, cols],
                                         rhs=w2[e][:, s, :].bitcast(FP8X4), rhs_scale=w2s[e // 2][4 * plane :, :],
                                         start=(s == 0), stop=(s == PASSES - 1))
-                silu_neg = work.tile([P, H], F32, name="silu_neg")
-                nc.scalar.activation(silu_neg[:], a_ps[:], ACT.Silu, scale=-1.0)
+                part[c] = arena.tile([P, H], F32, name=f"part_{e}_{c}", offset=seat(e, c), align_bytes=64)
+                nc.vector.scalar_tensor_tensor(part[c][:], silu_neg[:], 1.0, dh_ps[:], ALU.subtract, ALU.mult)
+            for c in range(SLOT_TILES):
                 tanh_half = work.tile([P, H], F32, name="tanh_half")
-                nc.scalar.activation(tanh_half[:], a_ps[:], ACT.Tanh, scale=0.5)
+                nc.scalar.activation(tanh_half[:], a_ps[c][:], ACT.Tanh, scale=0.5)
                 g = half_gate[:, e * SLOT_TILES + c : e * SLOT_TILES + c + 1]
-                gated = work.tile([P, H], F32, name="gated")
+                gated = work.tile([P, H], F32, name="gated", bufs=8)
                 nc.scalar.activation(gated[:], tanh_half[:], ACT.Identity, bias=g, scale=g)
-                part = work.tile([P, H], F32, name="part")
-                nc.vector.scalar_tensor_tensor(part[:], silu_neg[:], 1.0, dh_ps[:], ALU.subtract, ALU.mult)
                 da = work.tile([P, H], BF16, name="da")
-                nc.vector.tensor_tensor(da[:], gated[:], part[:], ALU.mult)
+                nc.vector.tensor_tensor(da[:], gated[:], part[c][:], ALU.mult)
                 pairs = da[:].bitcast(F32)
                 for u in range(2):
                     nc.tensor.transpose(turned[:, c, u, :], pairs[:, u : H // 2 : 2], ident[:])
-            tile = work.tile([P, C * PACK], BF16, name="grouped", align_bytes=64)
+            tile = arena.tile([P, C * PACK], BF16, name=f"grouped_{e}", align_bytes=64, offset=seat(e, 2))
             nc.scalar.copy(tile[:].bitcast(F32).rearrange("p (c r u) -> p c r u", c=SLOT_TILES, u=2), turned[:].rearrange("p c u r -> p c r u"))
             grouped[e] = tile
 
-        staged = {}
+        staged = [keep.tile([P, 2, T], F32, name=f"staged{h}") for h in range(K_TILES // 2)]
+        sums = {}
 
         def back(e):
             codes = work.tile([P, C], U32, name="codes", align_bytes=64)
@@ -165,29 +179,34 @@ def tile_moe_rec_mlp_silu_kernel(tc, x_words, x_scales, dy_words, dy_scales, w1_
                     cols = slice((2 * h + i) * P, (2 * h + i + 1) * P)
                     nc.tensor.matmul_mx(dx_ps[:, i, :], lhsT=w1t[e][:, cols].bitcast(FP8X4), lhsT_scale=w1ts[4 * e :, cols],
                                         rhs=codes[:].bitcast(FP8X4), rhs_scale=scales[:], start=True, stop=True)
-                dx = keep.tile([P, 2, C], F32, name=f"dx_{e}_{h}")
-                nc.scalar.copy(dx[:], dx_ps[:])
-                staged[e, h] = dx
+                sums[e, h] = dx_ps
 
-        def scatter(e):
-            for j in range(K_TILES):
-                nc.vector.tensor_copy(windows[j][:].indirect(listed(e)), staged[e, j // 2][:, j % 2, :])
-                if e == E - 1:
-                    nc.sync.dma_start(out[j * P : (j + 1) * P, :], windows[j][:])
+        def stage(e):
+            for h in range(K_TILES // 2):
+                nc.scalar.copy(staged[h][:, :, e * C : (e + 1) * C], sums[e, h][:])
 
-        gather(0)
-        gather(1)
+        def scatter(j, window, experts):
+            source = staged[j // 2][:, j % 2, experts[0] * C : (experts[-1] + 1) * C]
+            nc.vector.tensor_copy(window[:].indirect(listed(experts)), source)
+            if experts[-1] == E - 1:
+                nc.sync.dma_start(out[j * P : (j + 1) * P, :], window[:, 0:T])
+
         front(0)
-        gather(2)
-        back(0)
         front(1)
-        gather(3)
-        back(1)
+        back(0)
+        stage(0)
         front(2)
-        scatter(0)
-        back(2)
+        back(1)
         front(3)
-        scatter(1)
+        stage(1)
+        back(2)
+        stage(2)
         back(3)
-        scatter(2)
-        scatter(3)
+        stage(3)
+        after = {1: seat(2, 0), 2: seat(3, 1), 3: seat(3, 2)}
+        windows = [keep.tile([P, T], F32, name="window0")]
+        for j in range(1, K_TILES):
+            windows.append(arena.tile([P, T], F32, name=f"window{j}", offset=after[j] + 64 - 4096, align_bytes=64))
+        for experts in ((0,), (1, 2, 3)):
+            for j in range(K_TILES):
+                scatter(j, windows[j], experts)

@@ -19,194 +19,217 @@ ALU = mybir.AluOpType
 P = 128
 PACK = 4
 QUADS = 4
+QUAD_ROWS = 4
+PLANES = 4
 SLOT_TILES = C // P
-K_TILES = K // P
-PASSES = N // (P * PACK)
+ROW_TILES = K // P
+DY_PASSES = N // (P * PACK)
 STRIPE = 16
+MX_ALIGN = 64
+HALVES = ((0, 1), (2, 3))
+SEAT_BYTES = 4 * T
+
+EARLY_EXPERTS = {0: (0,), 1: (0,), 3: (0, 1, 2), 2: (0, 1)}
+EARLY_AFTER = {0: (2, 0), 1: (1, 1), 3: (1, 0), 2: (3, 0)}
+LATE_ORDER = (1, 0, 3, 2)
 
 
-def tile_moe_rec_mlp_silu_kernel(tc, x_words, x_scales, dy_words, dy_scales, w1_words, w1_scales, w2t_words, w2t_scales, w1t_words, w1t_scales, gate, offs, out):
+def tile_moe_rec_mlp_silu_kernel(
+    tc, x_words, x_scales, dy_words, dy_scales, w1_words, w1_scales, w2t_words, w2t_scales, w1t_words, w1t_scales, gate, offs, out
+):
     nc = tc.nc
     with ExitStack() as ctx:
         keep = ctx.enter_context(tc.tile_pool(name="keep", bufs=1))
         work = ctx.enter_context(tc.tile_pool(name="work", bufs=4))
-        arena = ctx.enter_context(tc.tile_pool(name="arena", bufs=1))
+        seats = ctx.enter_context(tc.tile_pool(name="seats", bufs=1))
         psum = ctx.enter_context(tc.psum_pool(name="psum", bufs=2))
+
+        def seat(e, c):
+            return (SLOT_TILES * e + c) * SEAT_BYTES
 
         offsets = keep.tile([P, T // STRIPE], U16, name="offsets")
         nc.sync.dma_start(offsets[:], offs)
 
-        def scale_tile(name, width):
-            plane = keep.tile([P, width], U8, name=name, align_bytes=64)
-            nc.vector.memset(plane[:].bitcast(I32), 0)
-            return plane
+        def listed(experts):
+            return offsets[:, experts[0] * C // STRIPE : (experts[-1] + 1) * C // STRIPE]
 
-        def load_scales(plane, planes):
-            rows = planes.shape[0] * 4
-            for q in range(QUADS):
-                nc.sync.dma_start(plane[32 * q : 32 * q + rows, :].bitcast(I32), planes[:, 4 * q : 4 * q + 4, :].bitcast(I32))
-
-        def load_words(name, words):
-            tile = keep.tile([P, words.shape[1]], I32, name=name, align_bytes=64)
-            nc.sync.dma_start(tile[:], words.rearrange("p c d -> p (c d)").bitcast(I32))
+        def zeroed_planes(name, width):
+            tile = keep.tile([P, width], U8, name=name, align_bytes=MX_ALIGN)
+            nc.vector.memset(tile[:].bitcast(I32), 0)
             return tile
 
-        w1s = scale_tile("w1s", H)
-        dys = scale_tile("dys", T)
-        w2s = [scale_tile(f"w2s{h}", H) for h in range(2)]
-        w1ts = scale_tile("w1ts", K)
-        w2_planes = w2t_scales.rearrange("e s b i -> (e s) b i")
+        def load_planes(tile, planes):
+            rows = planes.shape[0] * QUAD_ROWS
+            for q in range(QUADS):
+                source = planes[:, QUAD_ROWS * q : QUAD_ROWS * (q + 1), :]
+                nc.sync.dma_start(tile[32 * q : 32 * q + rows, :].bitcast(I32), source.bitcast(I32))
 
-        warm = keep.tile([P, 1], F32, name="warm")
-        warm_out = keep.tile([P, 1], F32, name="warm_out")
-        nc.vector.memset(warm[:], 0.0)
-        nc.scalar.activation(warm_out[:], warm[:], ACT.Silu)
+        def load_pass(name, words):
+            tile = keep.tile([P, words.shape[1]], I32, name=name, align_bytes=MX_ALIGN)
+            nc.sync.dma_start(tile[:], words.rearrange("p c d -> p (c d)").bitcast(I32))
+            return tile[:]
 
-        w1, w2, w1t = {}, {}, {}
+        def load_passes(name, words):
+            tile = keep.tile([P, words.shape[0], words.shape[2]], I32, name=name, align_bytes=MX_ALIGN)
+            nc.sync.dma_start(tile[:], words.rearrange("j p c d -> p j (c d)").bitcast(I32))
+            return [tile[:, j, :] for j in range(words.shape[0])]
 
-        def load_w1(e):
-            w1[e] = load_words(f"w1_{e}", w1_words[e, 0])
+        w1_planes = zeroed_planes("w1_planes", H)
+        dy_planes = zeroed_planes("dy_planes", T)
+        w2_planes = [zeroed_planes(f"w2_planes{half}", H) for half in range(len(HALVES))]
+        w1t_planes = zeroed_planes("w1t_planes", K)
+        w2_scale_rows = w2t_scales.rearrange("e s b i -> (e s) b i")
+        w2_word_passes = w2t_words.rearrange("e s p i d -> (e s) p i d")
 
-        def load_w2(e):
-            tile = keep.tile([P, PASSES, H], I32, name=f"w2_{e}", align_bytes=64)
-            nc.sync.dma_start(tile[:], w2t_words[e].rearrange("s p c d -> p s (c d)").bitcast(I32))
-            w2[e] = tile
-
-        def load_back(e):
-            w1t[e] = load_words(f"w1t_{e}", w1t_words[e, 0])
+        zero = keep.tile([P, 1], F32, name="zero")
+        no_bias = keep.tile([P, 1], F32, name="no_bias")
+        nc.vector.memset(zero[:], 0.0)
+        nc.scalar.activation(no_bias[:], zero[:], ACT.Silu)
 
         ident = keep.tile([P, P], F32, name="ident")
         make_identity(nc, ident[:])
 
-        xs = keep.tile([P, T], U8, name="xs", align_bytes=64)
+        x_plane = keep.tile([P, T], U8, name="x_plane", align_bytes=MX_ALIGN)
         for q in range(QUADS):
-            rows = x_scales[:, 4 * q : 4 * q + 4, :].bitcast(I32)
-            nc.sync.dma_start(xs[32 * q : 32 * q + 32, :].bitcast(I32), rows.to_broadcast([8, 4, T // 4]))
-        load_scales(w1s, w1_scales[:, 0])
-        xw = load_words("xw", x_words[0])
-        load_w1(0)
+            source = x_scales[:, QUAD_ROWS * q : QUAD_ROWS * (q + 1), :].bitcast(I32)
+            nc.sync.dma_start(x_plane[32 * q : 32 * (q + 1), :].bitcast(I32), source.to_broadcast([32 // QUAD_ROWS, QUAD_ROWS, T // 4]))
         gate_rows = keep.tile([P, P], F32, name="gate_rows")
-        nc.sync.dma_start(gate_rows[:], gate[0:16, :].rearrange("a (c m) -> (a c) m", m=P))
-        load_scales(dys, dy_scales)
-        dyw = [load_words("dyw0", dy_words[0])]
-        load_w1(1)
-        dyw.append(load_words("dyw1", dy_words[1]))
-        load_scales(w2s[0], w2_planes[0:4])
-        load_scales(w2s[1], w2_planes[4:8])
-        load_w2(0)
-        load_w1(2)
-        load_w2(1)
-        load_w1(3)
-        load_scales(w1ts, w1t_scales[:, 0])
-        load_back(0)
-        load_w2(2)
-        load_w2(3)
-        load_back(1)
-        load_back(2)
-        load_back(3)
+        nc.sync.dma_start(gate_rows[:], gate[0 : P * P // T, :].rearrange("a (c m) -> (a c) m", m=P))
+        xw = load_pass("xw", x_words[0])
+        w1 = [load_pass("w1_0", w1_words[0, 0])]
+        load_planes(w1_planes, w1_scales[:, 0])
+        dyw = [load_pass("dyw0", dy_words[0])]
+        w1.append(load_pass("w1_1", w1_words[1, 0]))
+        load_planes(dy_planes, dy_scales)
+        w2 = load_passes("w2_0", w2_word_passes[0:DY_PASSES])
+        dyw.append(load_pass("dyw1", dy_words[1]))
+        load_planes(w2_planes[0], w2_scale_rows[0:PLANES])
+        w1.append(load_pass("w1_2", w1_words[2, 0]))
+        load_planes(w2_planes[1], w2_scale_rows[PLANES : 2 * PLANES])
+        w2.extend(load_passes("w2_12", w2_word_passes[DY_PASSES : 3 * DY_PASSES]))
+        w1t = [load_pass("w1t_0", w1t_words[0, 0])]
+        load_planes(w1t_planes, w1t_scales[:, 0])
+        w1.append(load_pass("w1_3", w1_words[3, 0]))
+        w2.extend(load_passes("w2_3", w2_word_passes[3 * DY_PASSES : 4 * DY_PASSES]))
+        w1t.append(load_pass("w1t_1", w1t_words[1, 0]))
+        w1t.extend(load_passes("w1t_23", w1t_words[2:4, 0]))
 
-        gate_ps = psum.tile([P, 512], F32, name="gate_ps", tag="turn")
+        gate_ps = psum.tile([P, H], F32, name="gate_ps", tag="turn", bufs=1)
         nc.tensor.transpose(gate_ps[:, 0:P], gate_rows[:], ident[:])
-        half_gate = keep.tile([P, E * SLOT_TILES], F32, name="half_gate")
-        nc.scalar.activation(half_gate[:], gate_ps[:, 0 : E * SLOT_TILES], ACT.Copy, scale=-0.5)
+        neg_half_gate = keep.tile([P, E * SLOT_TILES], F32, name="neg_half_gate")
+        nc.scalar.activation(neg_half_gate[:], gate_ps[:, 0 : E * SLOT_TILES], ACT.Copy, scale=-0.5)
 
-        def seat(e, c):
-            return (3 * e + c) * 8192 + 4096
-
-        def listed(experts):
-            return offsets[:, experts[0] * C // STRIPE : (experts[-1] + 1) * C // STRIPE]
-
-        halves = ((0, 1), (2, 3))
-
-        def gather(name, window, dtype, half):
-            tile = keep.tile([P, 2 * C], dtype, name=f"{name}_{half}", align_bytes=64)
-            nc.vector.tensor_copy(tile[:], window.indirect(listed(halves[half])))
+        def gather(tile, window, half):
+            nc.vector.tensor_copy(tile[:], window.indirect(listed(HALVES[half])))
             return tile
 
-        gxs, gx = [], []
-        for half in range(2):
-            gxs.append(gather("gxs", xs[:], U8, half))
-            gx.append(gather("gx", xw[:].bitcast(U32), U32, half))
-        gds = [gather("gds", dys[:], U8, half) for half in range(2)]
-        gd = [[gather(f"gd{s}", dyw[s][:].bitcast(U32), U32, half) for s in range(PASSES)] for half in range(2)]
+        def gathered(name, window, dtype, half):
+            return gather(keep.tile([P, 2 * C], dtype, name=f"{name}_{half}", align_bytes=MX_ALIGN), window, half)
 
-        grouped = {}
+        slot_x_plane, slot_x, slot_dy_planes, slot_dy = {}, {}, {}, {}
+        for half in range(len(HALVES)):
+            slot_x_plane[half] = gathered("slot_x_plane", x_plane[:], U8, half)
+            slot_x[half] = gathered("slot_x", xw.bitcast(U32), U32, half)
+        slot_dy[0, 0] = gathered("slot_dy0", dyw[0].bitcast(U32), U32, 0)
+        for half in range(len(HALVES)):
+            slot_dy_planes[half] = gathered("slot_dy_planes", dy_planes[:], U8, half)
+            slot_dy[half, 1] = gathered("slot_dy1", dyw[1].bitcast(U32), U32, half)
 
-        def front(e):
+        interleaved = {}
+
+        def make_da(e):
             half, first = e // 2, e % 2 * C
-            turned = psum.tile([P, SLOT_TILES, 2, P], F32, name="turned", tag="turn")
+            turned = psum.tile([P, SLOT_TILES, 2, P], F32, name="turned", tag="turn", bufs=1)
             a_ps, part = {}, {}
             for c in range(SLOT_TILES):
-                cols = slice(first + c * P, first + (c + 1) * P)
+                slots = slice(first + c * P, first + (c + 1) * P)
                 a_ps[c] = psum.tile([P, H], F32, name="a_ps")
-                nc.tensor.matmul_mx(a_ps[c][:], lhsT=gx[half][:, cols].bitcast(FP8X4), lhsT_scale=gxs[half][:, cols],
-                                    rhs=w1[e][:].bitcast(FP8X4), rhs_scale=w1s[4 * e :, :], start=True, stop=True)
-                silu_neg = work.tile([P, H], F32, name="silu_neg", bufs=8)
-                nc.scalar.activation(silu_neg[:], a_ps[c][:], ACT.Silu, scale=-1.0)
-                dh_ps = psum.tile([P, H], F32, name="dh_ps")
-                for s in range(PASSES):
-                    plane = (PASSES * e + s) % 4
-                    nc.tensor.matmul_mx(dh_ps[:], lhsT=gd[half][s][:, cols].bitcast(FP8X4), lhsT_scale=gds[half][4 * s :, cols],
-                                        rhs=w2[e][:, s, :].bitcast(FP8X4), rhs_scale=w2s[e // 2][4 * plane :, :],
-                                        start=(s == 0), stop=(s == PASSES - 1))
-                part[c] = arena.tile([P, H], F32, name=f"part_{e}_{c}", offset=seat(e, c), align_bytes=64)
+                nc.tensor.matmul_mx(
+                    a_ps[c][:],
+                    lhsT=slot_x[half][:, slots].bitcast(FP8X4),
+                    lhsT_scale=slot_x_plane[half][:, slots],
+                    rhs=w1[e].bitcast(FP8X4),
+                    rhs_scale=w1_planes[QUAD_ROWS * e :, :],
+                    start=True,
+                    stop=True,
+                )
+                silu_neg = work.tile([P, H], F32, name="silu_neg", bufs=E * SLOT_TILES)
+                nc.scalar.activation(silu_neg[:], a_ps[c][:], ACT.Silu, bias=no_bias[:], scale=-1.0)
+                dh_ps = psum.tile([P, H], F32, name="dh_ps", bufs=3)
+                for s in range(DY_PASSES):
+                    j = DY_PASSES * e + s
+                    nc.tensor.matmul_mx(
+                        dh_ps[:],
+                        lhsT=slot_dy[half, s][:, slots].bitcast(FP8X4),
+                        lhsT_scale=slot_dy_planes[half][QUAD_ROWS * s :, slots],
+                        rhs=w2[j].bitcast(FP8X4),
+                        rhs_scale=w2_planes[j // PLANES][QUAD_ROWS * (j % PLANES) :, :],
+                        start=(s == 0),
+                        stop=(s == DY_PASSES - 1),
+                    )
+                part[c] = seats.tile([P, H], F32, name=f"part_{e}_{c}", offset=seat(e, c), align_bytes=MX_ALIGN)
                 nc.vector.scalar_tensor_tensor(part[c][:], silu_neg[:], 1.0, dh_ps[:], ALU.subtract, ALU.mult)
             for c in range(SLOT_TILES):
                 tanh_half = work.tile([P, H], F32, name="tanh_half")
                 nc.scalar.activation(tanh_half[:], a_ps[c][:], ACT.Tanh, scale=0.5)
-                g = half_gate[:, e * SLOT_TILES + c : e * SLOT_TILES + c + 1]
-                gated = work.tile([P, H], F32, name="gated", bufs=8)
+                g = neg_half_gate[:, e * SLOT_TILES + c : e * SLOT_TILES + c + 1]
+                gated = work.tile([P, H], F32, name="gated", bufs=E * SLOT_TILES)
                 nc.scalar.activation(gated[:], tanh_half[:], ACT.Identity, bias=g, scale=g)
                 da = work.tile([P, H], BF16, name="da")
                 nc.vector.tensor_tensor(da[:], gated[:], part[c][:], ALU.mult)
                 pairs = da[:].bitcast(F32)
                 for u in range(2):
                     nc.tensor.transpose(turned[:, c, u, :], pairs[:, u : H // 2 : 2], ident[:])
-            tile = arena.tile([P, C * PACK], BF16, name=f"grouped_{e}", align_bytes=64, offset=seat(e, 2))
-            nc.scalar.copy(tile[:].bitcast(F32).rearrange("p (c r u) -> p c r u", c=SLOT_TILES, u=2), turned[:].rearrange("p c u r -> p c r u"))
-            grouped[e] = tile
+            interleaved[e] = keep.tile([P, C * PACK], BF16, name=f"interleaved_{e}", align_bytes=MX_ALIGN)
+            nc.scalar.copy(
+                interleaved[e][:].bitcast(F32).rearrange("p (c r u) -> p c r u", c=SLOT_TILES, u=2),
+                turned[:].rearrange("p c u r -> p c r u"),
+            )
 
-        staged = [keep.tile([P, 2, T], F32, name=f"staged{h}") for h in range(K_TILES // 2)]
-        sums = {}
+        staged = [keep.tile([P, 2, T], F32, name=f"staged{h}") for h in range(ROW_TILES // 2)]
 
-        def back(e):
-            codes = work.tile([P, C], U32, name="codes", align_bytes=64)
-            scales = work.tile([P, C], U8, name="scales", align_bytes=64)
-            nc.vector.quantize_mx(out=codes[:].bitcast(FP8X4), scales=scales[:], in_=grouped[e][:])
-            for h in range(K_TILES // 2):
+        def make_dx(e):
+            codes = work.tile([P, C], U32, name="codes", align_bytes=MX_ALIGN)
+            da_plane = work.tile([P, C], U8, name="da_plane", align_bytes=MX_ALIGN)
+            nc.vector.quantize_mx(out=codes[:].bitcast(FP8X4), scales=da_plane[:], in_=interleaved[e][:])
+            banks = []
+            for h in range(ROW_TILES // 2):
                 dx_ps = psum.tile([P, 2, C], F32, name="dx_ps")
                 for i in range(2):
-                    cols = slice((2 * h + i) * P, (2 * h + i + 1) * P)
-                    nc.tensor.matmul_mx(dx_ps[:, i, :], lhsT=w1t[e][:, cols].bitcast(FP8X4), lhsT_scale=w1ts[4 * e :, cols],
-                                        rhs=codes[:].bitcast(FP8X4), rhs_scale=scales[:], start=True, stop=True)
-                sums[e, h] = dx_ps
+                    rows = slice((2 * h + i) * P, (2 * h + i + 1) * P)
+                    nc.tensor.matmul_mx(
+                        dx_ps[:, i, :],
+                        lhsT=w1t[e][:, rows].bitcast(FP8X4),
+                        lhsT_scale=w1t_planes[QUAD_ROWS * e :, rows],
+                        rhs=codes[:].bitcast(FP8X4),
+                        rhs_scale=da_plane[:],
+                        start=True,
+                        stop=True,
+                    )
+                banks.append(dx_ps)
+            for h in range(ROW_TILES // 2):
+                nc.scalar.copy(staged[h][:, :, e * C : (e + 1) * C], banks[h][:])
 
-        def stage(e):
-            for h in range(K_TILES // 2):
-                nc.scalar.copy(staged[h][:, :, e * C : (e + 1) * C], sums[e, h][:])
+        make_da(0)
+        late = seats.tile([P, 2 * C], U32, name="slot_dy0_1", offset=seat(0, SLOT_TILES - 1), align_bytes=MX_ALIGN)
+        slot_dy[1, 0] = gather(late, dyw[0].bitcast(U32), 1)
+        make_da(1)
+        make_da(2)
+        make_dx(0)
+        make_da(3)
+        for e in range(1, E):
+            make_dx(e)
 
-        def scatter(j, window, experts):
-            source = staged[j // 2][:, j % 2, experts[0] * C : (experts[-1] + 1) * C]
-            nc.vector.tensor_copy(window[:].indirect(listed(experts)), source)
-            if experts[-1] == E - 1:
-                nc.sync.dma_start(out[j * P : (j + 1) * P, :], window[:, 0:T])
+        windows = [
+            seats.tile([P, T], F32, name=f"window{r}", offset=seat(*EARLY_AFTER[r]), align_bytes=MX_ALIGN) for r in range(ROW_TILES)
+        ]
 
-        front(0)
-        front(1)
-        back(0)
-        stage(0)
-        front(2)
-        back(1)
-        front(3)
-        stage(1)
-        back(2)
-        stage(2)
-        back(3)
-        stage(3)
-        after = {1: seat(2, 0), 2: seat(3, 1), 3: seat(3, 2)}
-        windows = [keep.tile([P, T], F32, name="window0")]
-        for j in range(1, K_TILES):
-            windows.append(arena.tile([P, T], F32, name=f"window{j}", offset=after[j] + 64 - 4096, align_bytes=64))
-        for experts in ((0,), (1, 2, 3)):
-            for j in range(K_TILES):
-                scatter(j, windows[j], experts)
+        def scatter(r, experts):
+            source = staged[r // 2][:, r % 2, experts[0] * C : (experts[-1] + 1) * C]
+            nc.vector.tensor_copy(windows[r][:].indirect(listed(experts)), source)
+
+        for r in EARLY_EXPERTS:
+            scatter(r, EARLY_EXPERTS[r])
+        for r in LATE_ORDER:
+            scatter(r, range(len(EARLY_EXPERTS[r]), E))
+            nc.sync.dma_start(out[r * P : (r + 1) * P, :], windows[r][:])

@@ -22,16 +22,15 @@ QUADS = 4
 QUAD_ROWS = 4
 PLANES = 4
 SLOT_TILES = C // P
+TILES = E * SLOT_TILES
 ROW_TILES = K // P
 DY_PASSES = N // (P * PACK)
 STRIPE = 16
 MX_ALIGN = 64
-HALVES = ((0, 1), (2, 3))
-SEAT_BYTES = 4 * T
-
-EARLY_EXPERTS = {0: (0,), 1: (0,), 3: (0, 1, 2), 2: (0, 1)}
-EARLY_AFTER = {0: (2, 0), 1: (1, 1), 3: (1, 0), 2: (3, 0)}
-LATE_ORDER = (1, 0, 3, 2)
+BANK = 2048
+KB = 1024
+MODES = "BBBBBBBB"
+AHEAD = 8
 
 
 def tile_moe_rec_mlp_silu_kernel(
@@ -40,29 +39,27 @@ def tile_moe_rec_mlp_silu_kernel(
     nc = tc.nc
     with ExitStack() as ctx:
         keep = ctx.enter_context(tc.tile_pool(name="keep", bufs=1))
-        work = ctx.enter_context(tc.tile_pool(name="work", bufs=4))
+        work = ctx.enter_context(tc.tile_pool(name="work", bufs=AHEAD))
         seats = ctx.enter_context(tc.tile_pool(name="seats", bufs=1))
-        psum = ctx.enter_context(tc.psum_pool(name="psum", bufs=2))
-
-        def seat(e, c):
-            return (SLOT_TILES * e + c) * SEAT_BYTES
+        psum = ctx.enter_context(tc.psum_pool(name="psum", bufs=3))
+        turns = ctx.enter_context(tc.psum_pool(name="turns", bufs=1))
 
         offsets = keep.tile([P, T // STRIPE], U16, name="offsets")
         nc.sync.dma_start(offsets[:], offs)
 
-        def listed(experts):
-            return offsets[:, experts[0] * C // STRIPE : (experts[-1] + 1) * C // STRIPE]
+        def listed(first, count):
+            return offsets[:, first // STRIPE : (first + count) // STRIPE]
 
-        def zeroed_planes(name, width):
+        def zeroed_planes(name, width, engine):
             tile = keep.tile([P, width], U8, name=name, align_bytes=MX_ALIGN)
-            nc.vector.memset(tile[:].bitcast(I32), 0)
+            engine.memset(tile[:].bitcast(I32), 0)
             return tile
 
-        def load_planes(tile, planes):
+        def load_planes(tile, planes, queue=nc.sync):
             rows = planes.shape[0] * QUAD_ROWS
             for q in range(QUADS):
                 source = planes[:, QUAD_ROWS * q : QUAD_ROWS * (q + 1), :]
-                nc.sync.dma_start(tile[32 * q : 32 * q + rows, :].bitcast(I32), source.bitcast(I32))
+                queue.dma_start(tile[32 * q : 32 * q + rows, :].bitcast(I32), source.bitcast(I32))
 
         def load_pass(name, words):
             tile = keep.tile([P, words.shape[1]], I32, name=name, align_bytes=MX_ALIGN)
@@ -74,10 +71,10 @@ def tile_moe_rec_mlp_silu_kernel(
             nc.sync.dma_start(tile[:], words.rearrange("j p c d -> p j (c d)").bitcast(I32))
             return [tile[:, j, :] for j in range(words.shape[0])]
 
-        w1_planes = zeroed_planes("w1_planes", H)
-        dy_planes = zeroed_planes("dy_planes", T)
-        w2_planes = [zeroed_planes(f"w2_planes{half}", H) for half in range(len(HALVES))]
-        w1t_planes = zeroed_planes("w1t_planes", K)
+        w1_planes = zeroed_planes("w1_planes", H, nc.gpsimd)
+        dy_planes = zeroed_planes("dy_planes", T, nc.gpsimd)
+        w2_planes = [zeroed_planes(f"w2_planes{half}", H, nc.vector) for half in range(2)]
+        w1t_planes = zeroed_planes("w1t_planes", K, nc.vector)
         w2_scale_rows = w2t_scales.rearrange("e s b i -> (e s) b i")
         w2_word_passes = w2t_words.rearrange("e s p i d -> (e s) p i d")
 
@@ -90,146 +87,177 @@ def tile_moe_rec_mlp_silu_kernel(
         make_identity(nc, ident[:])
 
         x_plane = keep.tile([P, T], U8, name="x_plane", align_bytes=MX_ALIGN)
-        for q in range(QUADS):
-            source = x_scales[:, QUAD_ROWS * q : QUAD_ROWS * (q + 1), :].bitcast(I32)
-            nc.sync.dma_start(x_plane[32 * q : 32 * (q + 1), :].bitcast(I32), source.to_broadcast([32 // QUAD_ROWS, QUAD_ROWS, T // 4]))
         gate_rows = keep.tile([P, P], F32, name="gate_rows")
+        w1, w2, w1t, dyw = {}, {}, {}, {}
+
+        def load_x_plane():
+            for q in range(QUADS):
+                source = x_scales[:, QUAD_ROWS * q : QUAD_ROWS * (q + 1), :].bitcast(I32)
+                nc.sync.dma_start(x_plane[32 * q : 32 * (q + 1), :].bitcast(I32), source.to_broadcast([32 // QUAD_ROWS, QUAD_ROWS, T // 4]))
+
+        def load_w2(e):
+            w2[2 * e], w2[2 * e + 1] = load_passes(f"w2_{e}", w2_word_passes[2 * e : 2 * e + 2])
+
+        load_x_plane()
         nc.sync.dma_start(gate_rows[:], gate[0 : P * P // T, :].rearrange("a (c m) -> (a c) m", m=P))
         xw = load_pass("xw", x_words[0])
-        w1 = [load_pass("w1_0", w1_words[0, 0])]
+        w1[0] = load_pass("w1_0", w1_words[0, 0])
         load_planes(w1_planes, w1_scales[:, 0])
-        dyw = [load_pass("dyw0", dy_words[0])]
-        w1.append(load_pass("w1_1", w1_words[1, 0]))
+        dyw[0] = load_pass("dyw0", dy_words[0])
+        dyw[1] = load_pass("dyw1", dy_words[1])
         load_planes(dy_planes, dy_scales)
-        w2 = load_passes("w2_0", w2_word_passes[0:DY_PASSES])
-        dyw.append(load_pass("dyw1", dy_words[1]))
+        load_w2(0)
         load_planes(w2_planes[0], w2_scale_rows[0:PLANES])
-        w1.append(load_pass("w1_2", w1_words[2, 0]))
-        load_planes(w2_planes[1], w2_scale_rows[PLANES : 2 * PLANES])
-        w2.extend(load_passes("w2_12", w2_word_passes[DY_PASSES : 3 * DY_PASSES]))
-        w1t = [load_pass("w1t_0", w1t_words[0, 0])]
+        w1[1] = load_pass("w1_1", w1_words[1, 0])
+        load_w2(1)
         load_planes(w1t_planes, w1t_scales[:, 0])
-        w1.append(load_pass("w1_3", w1_words[3, 0]))
-        w2.extend(load_passes("w2_3", w2_word_passes[3 * DY_PASSES : 4 * DY_PASSES]))
-        w1t.append(load_pass("w1t_1", w1t_words[1, 0]))
-        w1t.extend(load_passes("w1t_23", w1t_words[2:4, 0]))
+        w1t[0] = load_pass("w1t_0", w1t_words[0, 0])
+        w1[2] = load_pass("w1_2", w1_words[2, 0])
+        load_planes(w2_planes[1], w2_scale_rows[PLANES : 2 * PLANES])
+        load_w2(2)
+        w1t[1] = load_pass("w1t_1", w1t_words[1, 0])
+        w1[3] = load_pass("w1_3", w1_words[3, 0])
+        load_w2(3)
+        w1t[2], w1t[3] = load_passes("w1t_23", w1t_words[2:4, 0])
 
-        gate_ps = psum.tile([P, H], F32, name="gate_ps", tag="turn", bufs=1)
+        gate_ps = turns.tile([P, H], F32, name="gate_ps", offset=0)
         nc.tensor.transpose(gate_ps[:, 0:P], gate_rows[:], ident[:])
-        neg_half_gate = keep.tile([P, E * SLOT_TILES], F32, name="neg_half_gate")
-        nc.scalar.activation(neg_half_gate[:], gate_ps[:, 0 : E * SLOT_TILES], ACT.Copy, scale=-0.5)
+        neg_half_gate = keep.tile([P, TILES], F32, name="neg_half_gate")
+        nc.scalar.activation(neg_half_gate[:], gate_ps[:, 0:TILES], ACT.Copy, scale=-0.5)
 
-        def gather(tile, window, half):
-            nc.vector.tensor_copy(tile[:], window.indirect(listed(HALVES[half])))
-            return tile
+        def gathered(name, window, dtype, first, count, offset=None):
+            if offset is None:
+                tile = keep.tile([P, count], dtype, name=name, align_bytes=MX_ALIGN)
+            else:
+                tile = seats.tile([P, count], dtype, name=name, offset=offset, align_bytes=MX_ALIGN)
+            nc.vector.tensor_copy(tile[:], window.indirect(listed(first, count)))
+            return [tile[:, i * P : (i + 1) * P] for i in range(count // P)]
 
-        def gathered(name, window, dtype, half):
-            return gather(keep.tile([P, 2 * C], dtype, name=f"{name}_{half}", align_bytes=MX_ALIGN), window, half)
+        slot_x_plane, slot_x, slot_dy_planes, slot_dy0, slot_dy1 = [], [], [], [], []
+        slot_dy = [slot_dy0, slot_dy1]
+        dy0w, dy1w = dyw[0].bitcast(U32), dyw[1].bitcast(U32)
+        slot_x_plane.extend(gathered("slot_x_plane0", x_plane[:], U8, 0, 2 * C))
+        slot_x.extend(gathered("slot_x0", xw.bitcast(U32), U32, 0, 2 * C))
+        slot_x_plane.extend(gathered("slot_x_plane1", x_plane[:], U8, 2 * C, 2 * C))
+        slot_dy0.extend(gathered("slot_dy0_0", dy0w, U32, 0, C, offset=2 * KB))
+        slot_dy_planes.extend(gathered("slot_dy_planes0", dy_planes[:], U8, 0, 2 * C))
+        slot_dy1.extend(gathered("slot_dy1_0", dy1w, U32, 0, C, offset=3 * KB))
+        slot_dy0.extend(gathered("slot_dy0_1", dy0w, U32, C, C))
+        slot_dy1.extend(gathered("slot_dy1_1", dy1w, U32, C, C))
 
-        slot_x_plane, slot_x, slot_dy_planes, slot_dy = {}, {}, {}, {}
-        for half in range(len(HALVES)):
-            slot_x_plane[half] = gathered("slot_x_plane", x_plane[:], U8, half)
-            slot_x[half] = gathered("slot_x", xw.bitcast(U32), U32, half)
-        slot_dy[0, 0] = gathered("slot_dy0", dyw[0].bitcast(U32), U32, 0)
-        for half in range(len(HALVES)):
-            slot_dy_planes[half] = gathered("slot_dy_planes", dy_planes[:], U8, half)
-            slot_dy[half, 1] = gathered("slot_dy1", dyw[1].bitcast(U32), U32, half)
+        staged = [keep.tile([P, ROW_TILES, P], F32, name=f"staged{j}") for j in range(TILES)]
+        joint = keep.tile([P, 2, 2 * P], F32, name="joint")
+        windows = [keep.tile([P, T], F32, name=f"window{r}") for r in range(ROW_TILES)]
+        interleaved, codes, da_plane = {}, {}, {}
 
-        interleaved = {}
-
-        def make_da(e):
-            half, first = e // 2, e % 2 * C
-            turned = psum.tile([P, SLOT_TILES, 2, P], F32, name="turned", tag="turn", bufs=1)
-            a_ps, part = {}, {}
-            for c in range(SLOT_TILES):
-                slots = slice(first + c * P, first + (c + 1) * P)
-                a_ps[c] = psum.tile([P, H], F32, name="a_ps")
+        def make_da(j):
+            e = j // SLOT_TILES
+            a_ps = psum.tile([P, H], F32, name="a_ps")
+            nc.tensor.matmul_mx(
+                a_ps[:],
+                lhsT=slot_x[j].bitcast(FP8X4),
+                lhsT_scale=slot_x_plane[j],
+                rhs=w1[e].bitcast(FP8X4),
+                rhs_scale=w1_planes[QUAD_ROWS * e :, :],
+                start=True,
+                stop=True,
+            )
+            silu_neg = work.tile([P, H], F32, name="silu_neg")
+            nc.scalar.activation(silu_neg[:], a_ps[:], ACT.Silu, bias=no_bias[:], scale=-1.0)
+            tanh_half = work.tile([P, H], F32, name="tanh_half")
+            nc.scalar.activation(tanh_half[:], a_ps[:], ACT.Tanh, scale=0.5)
+            g = neg_half_gate[:, j : j + 1]
+            gated = work.tile([P, H], F32, name="gated")
+            if MODES[j] == "B":
+                nc.scalar.activation(gated[:], tanh_half[:], ACT.Identity, bias=g, scale=g)
+            else:
+                nc.scalar.activation(gated[:], tanh_half[:], ACT.Copy, bias=1.0)
+                less = work.tile([P, H], F32, name="less")
+                nc.scalar.activation(less[:], silu_neg[:], ACT.Copy, bias=-1.0)
+                slope = work.tile([P, H], F32, name="slope")
+                nc.gpsimd.tensor_tensor(slope[:], gated[:], less[:], ALU.mult)
+            dh_ps = psum.tile([P, H], F32, name="dh_ps")
+            for s in range(DY_PASSES):
+                n = DY_PASSES * e + s
                 nc.tensor.matmul_mx(
-                    a_ps[c][:],
-                    lhsT=slot_x[half][:, slots].bitcast(FP8X4),
-                    lhsT_scale=slot_x_plane[half][:, slots],
-                    rhs=w1[e].bitcast(FP8X4),
-                    rhs_scale=w1_planes[QUAD_ROWS * e :, :],
+                    dh_ps[:],
+                    lhsT=slot_dy[s][j].bitcast(FP8X4),
+                    lhsT_scale=slot_dy_planes[j][QUAD_ROWS * s :, :],
+                    rhs=w2[n].bitcast(FP8X4),
+                    rhs_scale=w2_planes[n // PLANES][QUAD_ROWS * (n % PLANES) :, :],
+                    start=(s == 0),
+                    stop=(s == DY_PASSES - 1),
+                )
+            da = work.tile([P, H], BF16, name="da")
+            if MODES[j] == "B":
+                part = work.tile([P, H], F32, name="part")
+                nc.vector.scalar_tensor_tensor(part[:], silu_neg[:], 1.0, dh_ps[:], ALU.subtract, ALU.mult)
+                nc.gpsimd.tensor_tensor(da[:], gated[:], part[:], ALU.mult)
+            elif MODES[j] == "D":
+                nc.vector.scalar_tensor_tensor(da[:], slope[:], g, dh_ps[:], ALU.mult, ALU.mult)
+            else:
+                part = work.tile([P, H], F32, name="part")
+                nc.scalar.activation(part[:], dh_ps[:], ACT.Copy, scale=g)
+                nc.gpsimd.tensor_tensor(da[:], slope[:], part[:], ALU.mult)
+            turned = turns.tile([P, 2, P], F32, name=f"turned{j}", offset=j % 2 * BANK)
+            pairs = da[:].bitcast(F32)
+            for u in range(2):
+                nc.tensor.transpose(turned[:, u, :], pairs[:, u : H // 2 : 2], ident[:])
+            interleaved[j] = seats.tile([P, P * PACK], BF16, name=f"interleaved{j}", offset=(5 + j) * KB, align_bytes=MX_ALIGN)
+            nc.scalar.copy(
+                interleaved[j][:].bitcast(F32).rearrange("p (r u) -> p r u", u=2),
+                turned[:].rearrange("p u r -> p r u"),
+            )
+            codes[j] = keep.tile([P, P], U32, name=f"codes{j}", align_bytes=MX_ALIGN)
+            da_plane[j] = keep.tile([P, P], U8, name=f"da_plane{j}", align_bytes=MX_ALIGN)
+            nc.vector.quantize_mx(out=codes[j][:].bitcast(FP8X4), scales=da_plane[j][:], in_=interleaved[j][:])
+
+        def make_dx(j):
+            e = j // SLOT_TILES
+            dx_ps = turns.tile([P, ROW_TILES, P], F32, name=f"dx_ps{j}", offset=(j + 1) % 2 * BANK)
+            for r in range(ROW_TILES):
+                rows = slice(r * P, (r + 1) * P)
+                nc.tensor.matmul_mx(
+                    dx_ps[:, r, :],
+                    lhsT=w1t[e][:, rows].bitcast(FP8X4),
+                    lhsT_scale=w1t_planes[QUAD_ROWS * e :, rows],
+                    rhs=codes[j][:].bitcast(FP8X4),
+                    rhs_scale=da_plane[j][:],
                     start=True,
                     stop=True,
                 )
-                silu_neg = work.tile([P, H], F32, name="silu_neg", bufs=E * SLOT_TILES)
-                nc.scalar.activation(silu_neg[:], a_ps[c][:], ACT.Silu, bias=no_bias[:], scale=-1.0)
-                dh_ps = psum.tile([P, H], F32, name="dh_ps", bufs=3)
-                for s in range(DY_PASSES):
-                    j = DY_PASSES * e + s
-                    nc.tensor.matmul_mx(
-                        dh_ps[:],
-                        lhsT=slot_dy[half, s][:, slots].bitcast(FP8X4),
-                        lhsT_scale=slot_dy_planes[half][QUAD_ROWS * s :, slots],
-                        rhs=w2[j].bitcast(FP8X4),
-                        rhs_scale=w2_planes[j // PLANES][QUAD_ROWS * (j % PLANES) :, :],
-                        start=(s == 0),
-                        stop=(s == DY_PASSES - 1),
-                    )
-                part[c] = seats.tile([P, H], F32, name=f"part_{e}_{c}", offset=seat(e, c), align_bytes=MX_ALIGN)
-                nc.vector.scalar_tensor_tensor(part[c][:], silu_neg[:], 1.0, dh_ps[:], ALU.subtract, ALU.mult)
-            for c in range(SLOT_TILES):
-                tanh_half = work.tile([P, H], F32, name="tanh_half")
-                nc.scalar.activation(tanh_half[:], a_ps[c][:], ACT.Tanh, scale=0.5)
-                g = neg_half_gate[:, e * SLOT_TILES + c : e * SLOT_TILES + c + 1]
-                gated = work.tile([P, H], F32, name="gated", bufs=E * SLOT_TILES)
-                nc.scalar.activation(gated[:], tanh_half[:], ACT.Identity, bias=g, scale=g)
-                da = work.tile([P, H], BF16, name="da")
-                nc.vector.tensor_tensor(da[:], gated[:], part[c][:], ALU.mult)
-                pairs = da[:].bitcast(F32)
-                for u in range(2):
-                    nc.tensor.transpose(turned[:, c, u, :], pairs[:, u : H // 2 : 2], ident[:])
-            interleaved[e] = keep.tile([P, C * PACK], BF16, name=f"interleaved_{e}", align_bytes=MX_ALIGN)
-            nc.scalar.copy(
-                interleaved[e][:].bitcast(F32).rearrange("p (c r u) -> p c r u", c=SLOT_TILES, u=2),
-                turned[:].rearrange("p c u r -> p c r u"),
-            )
+            if j < TILES - 2:
+                nc.scalar.copy(staged[j][:], dx_ps[:])
+            else:
+                nc.scalar.copy(staged[j][:, 0:2, :], dx_ps[:, 0:2, :])
+                nc.scalar.copy(joint[:, :, j % 2 * P : (j % 2 + 1) * P], dx_ps[:, 2:4, :])
 
-        staged = [keep.tile([P, 2, T], F32, name=f"staged{h}") for h in range(ROW_TILES // 2)]
+        def scatter(r, first, count):
+            nc.vector.tensor_copy(windows[r][:].indirect(listed(first * P, count * P)), staged[first][:, r, :] if count == 1 else joint[:, r - 2, :])
 
-        def make_dx(e):
-            codes = work.tile([P, C], U32, name="codes", align_bytes=MX_ALIGN)
-            da_plane = work.tile([P, C], U8, name="da_plane", align_bytes=MX_ALIGN)
-            nc.vector.quantize_mx(out=codes[:].bitcast(FP8X4), scales=da_plane[:], in_=interleaved[e][:])
-            banks = []
-            for h in range(ROW_TILES // 2):
-                dx_ps = psum.tile([P, 2, C], F32, name="dx_ps")
-                for i in range(2):
-                    rows = slice((2 * h + i) * P, (2 * h + i + 1) * P)
-                    nc.tensor.matmul_mx(
-                        dx_ps[:, i, :],
-                        lhsT=w1t[e][:, rows].bitcast(FP8X4),
-                        lhsT_scale=w1t_planes[QUAD_ROWS * e :, rows],
-                        rhs=codes[:].bitcast(FP8X4),
-                        rhs_scale=da_plane[:],
-                        start=True,
-                        stop=True,
-                    )
-                banks.append(dx_ps)
-            for h in range(ROW_TILES // 2):
-                nc.scalar.copy(staged[h][:, :, e * C : (e + 1) * C], banks[h][:])
+        def store(r):
+            nc.sync.dma_start(out[r * P : (r + 1) * P, :], windows[r][:])
 
         make_da(0)
-        late = seats.tile([P, 2 * C], U32, name="slot_dy0_1", offset=seat(0, SLOT_TILES - 1), align_bytes=MX_ALIGN)
-        slot_dy[1, 0] = gather(late, dyw[0].bitcast(U32), 1)
         make_da(1)
-        make_da(2)
-        make_dx(0)
-        make_da(3)
-        for e in range(1, E):
-            make_dx(e)
-
-        windows = [
-            seats.tile([P, T], F32, name=f"window{r}", offset=seat(*EARLY_AFTER[r]), align_bytes=MX_ALIGN) for r in range(ROW_TILES)
-        ]
-
-        def scatter(r, experts):
-            source = staged[r // 2][:, r % 2, experts[0] * C : (experts[-1] + 1) * C]
-            nc.vector.tensor_copy(windows[r][:].indirect(listed(experts)), source)
-
-        for r in EARLY_EXPERTS:
-            scatter(r, EARLY_EXPERTS[r])
-        for r in LATE_ORDER:
-            scatter(r, range(len(EARLY_EXPERTS[r]), E))
-            nc.sync.dma_start(out[r * P : (r + 1) * P, :], windows[r][:])
+        slot_x.extend(gathered("slot_x1", xw.bitcast(U32), U32, 2 * C, 2 * C, offset=MX_ALIGN))
+        slot_dy_planes.extend(gathered("slot_dy_planes1", dy_planes[:], U8, 2 * C, 2 * C, offset=2 * KB + 2 * MX_ALIGN))
+        slot_dy0.extend(gathered("slot_dy0_2", dy0w, U32, 2 * C, C, offset=2 * KB + 11 * MX_ALIGN))
+        slot_dy1.extend(gathered("slot_dy1_2", dy1w, U32, 2 * C, C, offset=3 * KB + 12 * MX_ALIGN))
+        slot_dy0.extend(gathered("slot_dy0_3", dy0w, U32, 3 * C, C, offset=5 * KB + 0))
+        slot_dy1.extend(gathered("slot_dy1_3", dy1w, U32, 3 * C, C, offset=6 * KB))
+        for j in range(TILES - 2):
+            make_dx(j)
+            make_da(j + 2)
+            for r in range(ROW_TILES):
+                scatter(r, j, 1)
+        make_dx(TILES - 2)
+        for r in range(2):
+            scatter(r, TILES - 2, 1)
+        make_dx(TILES - 1)
+        for r in range(2):
+            scatter(r, TILES - 1, 1)
+            store(r)
+        for r in range(2, ROW_TILES):
+            scatter(r, TILES - 2, 2)
+            store(r)

@@ -30,6 +30,7 @@ MX_ALIGN = 64
 BANK = 2048
 KB = 1024
 MODES = "BBBBBBBB"
+HOLD = 3
 AHEAD = 8
 
 
@@ -71,6 +72,7 @@ def tile_moe_rec_mlp_silu_kernel(
             nc.sync.dma_start(tile[:], words.rearrange("j p c d -> p j (c d)").bitcast(I32))
             return [tile[:, j, :] for j in range(words.shape[0])]
 
+        x_plane = zeroed_planes("x_plane", T, nc.gpsimd)
         w1_planes = zeroed_planes("w1_planes", H, nc.gpsimd)
         dy_planes = zeroed_planes("dy_planes", T, nc.gpsimd)
         w2_planes = [zeroed_planes(f"w2_planes{half}", H, nc.vector) for half in range(2)]
@@ -86,19 +88,13 @@ def tile_moe_rec_mlp_silu_kernel(
         ident = keep.tile([P, P], F32, name="ident")
         make_identity(nc, ident[:])
 
-        x_plane = keep.tile([P, T], U8, name="x_plane", align_bytes=MX_ALIGN)
         gate_rows = keep.tile([P, P], F32, name="gate_rows")
         w1, w2, w1t, dyw = {}, {}, {}, {}
-
-        def load_x_plane():
-            for q in range(QUADS):
-                source = x_scales[:, QUAD_ROWS * q : QUAD_ROWS * (q + 1), :].bitcast(I32)
-                nc.sync.dma_start(x_plane[32 * q : 32 * (q + 1), :].bitcast(I32), source.to_broadcast([32 // QUAD_ROWS, QUAD_ROWS, T // 4]))
 
         def load_w2(e):
             w2[2 * e], w2[2 * e + 1] = load_passes(f"w2_{e}", w2_word_passes[2 * e : 2 * e + 2])
 
-        load_x_plane()
+        load_planes(x_plane, x_scales)
         nc.sync.dma_start(gate_rows[:], gate[0 : P * P // T, :].rearrange("a (c m) -> (a c) m", m=P))
         xw = load_pass("xw", x_words[0])
         w1[0] = load_pass("w1_0", w1_words[0, 0])
@@ -138,12 +134,11 @@ def tile_moe_rec_mlp_silu_kernel(
         dy0w, dy1w = dyw[0].bitcast(U32), dyw[1].bitcast(U32)
         slot_x_plane.extend(gathered("slot_x_plane0", x_plane[:], U8, 0, 2 * C))
         slot_x.extend(gathered("slot_x0", xw.bitcast(U32), U32, 0, 2 * C))
-        slot_x_plane.extend(gathered("slot_x_plane1", x_plane[:], U8, 2 * C, 2 * C))
+        slot_x.extend(gathered("slot_x1", xw.bitcast(U32), U32, 2 * C, 2 * C))
         slot_dy0.extend(gathered("slot_dy0_0", dy0w, U32, 0, C, offset=2 * KB))
-        slot_dy_planes.extend(gathered("slot_dy_planes0", dy_planes[:], U8, 0, 2 * C))
         slot_dy1.extend(gathered("slot_dy1_0", dy1w, U32, 0, C, offset=3 * KB))
-        slot_dy0.extend(gathered("slot_dy0_1", dy0w, U32, C, C))
-        slot_dy1.extend(gathered("slot_dy1_1", dy1w, U32, C, C))
+        slot_dy_planes.extend(gathered("slot_dy_planes0", dy_planes[:], U8, 0, C))
+        slot_dy_planes.extend(gathered("slot_dy_planes123", dy_planes[:], U8, C, 3 * C))
 
         staged = [keep.tile([P, ROW_TILES, P], F32, name=f"staged{j}") for j in range(TILES)]
         joint = keep.tile([P, 2, 2 * P], F32, name="joint")
@@ -171,10 +166,16 @@ def tile_moe_rec_mlp_silu_kernel(
             if MODES[j] == "B":
                 nc.scalar.activation(gated[:], tanh_half[:], ACT.Identity, bias=g, scale=g)
             else:
-                nc.scalar.activation(gated[:], tanh_half[:], ACT.Copy, bias=1.0)
+                if MODES[j] in "DC":
+                    nc.scalar.activation(gated[:], tanh_half[:], ACT.Identity, bias=g, scale=g)
+                else:
+                    nc.gpsimd.tensor_scalar(gated[:], tanh_half[:], 1.0, g, ALU.add, ALU.mult)
                 less = work.tile([P, H], F32, name="less")
                 nc.scalar.activation(less[:], silu_neg[:], ACT.Copy, bias=-1.0)
-                slope = work.tile([P, H], F32, name="slope")
+                if j == 1:
+                    slope = seats.tile([P, H], F32, name="slope1", offset=14 * KB, align_bytes=MX_ALIGN)
+                else:
+                    slope = work.tile([P, H], F32, name="slope")
                 nc.gpsimd.tensor_tensor(slope[:], gated[:], less[:], ALU.mult)
             dh_ps = psum.tile([P, H], F32, name="dh_ps")
             for s in range(DY_PASSES):
@@ -190,25 +191,30 @@ def tile_moe_rec_mlp_silu_kernel(
                 )
             da = work.tile([P, H], BF16, name="da")
             if MODES[j] == "B":
-                part = work.tile([P, H], F32, name="part")
+                if j >= HOLD:
+                    part = seats.tile([P, H], F32, name=f"part{j}", offset=(18 + 3 * (j - HOLD)) * KB + 256, align_bytes=MX_ALIGN)
+                elif j == 2:
+                    part = seats.tile([P, H], F32, name="part2", offset=50 * KB + 512, align_bytes=MX_ALIGN)
+                else:
+                    part = work.tile([P, H], F32, name="part")
                 nc.vector.scalar_tensor_tensor(part[:], silu_neg[:], 1.0, dh_ps[:], ALU.subtract, ALU.mult)
                 nc.gpsimd.tensor_tensor(da[:], gated[:], part[:], ALU.mult)
             elif MODES[j] == "D":
-                nc.vector.scalar_tensor_tensor(da[:], slope[:], g, dh_ps[:], ALU.mult, ALU.mult)
+                nc.vector.tensor_tensor(da[:], slope[:], dh_ps[:], ALU.mult)
             else:
                 part = work.tile([P, H], F32, name="part")
-                nc.scalar.activation(part[:], dh_ps[:], ACT.Copy, scale=g)
+                nc.scalar.copy(part[:], dh_ps[:])
                 nc.gpsimd.tensor_tensor(da[:], slope[:], part[:], ALU.mult)
             turned = turns.tile([P, 2, P], F32, name=f"turned{j}", offset=j % 2 * BANK)
             pairs = da[:].bitcast(F32)
             for u in range(2):
                 nc.tensor.transpose(turned[:, u, :], pairs[:, u : H // 2 : 2], ident[:])
-            interleaved[j] = seats.tile([P, P * PACK], BF16, name=f"interleaved{j}", offset=(5 + j) * KB, align_bytes=MX_ALIGN)
+            interleaved[j] = seats.tile([P, P * PACK], BF16, name=f"interleaved{j}", offset=(48 + 4 * j) * KB, align_bytes=MX_ALIGN)
             nc.scalar.copy(
                 interleaved[j][:].bitcast(F32).rearrange("p (r u) -> p r u", u=2),
                 turned[:].rearrange("p u r -> p r u"),
             )
-            codes[j] = keep.tile([P, P], U32, name=f"codes{j}", align_bytes=MX_ALIGN)
+            codes[j] = seats.tile([P, P], U32, name=f"codes{j}", offset=(20 + 3 * j) * KB, align_bytes=MX_ALIGN)
             da_plane[j] = keep.tile([P, P], U8, name=f"da_plane{j}", align_bytes=MX_ALIGN)
             nc.vector.quantize_mx(out=codes[j][:].bitcast(FP8X4), scales=da_plane[j][:], in_=interleaved[j][:])
 
@@ -240,14 +246,16 @@ def tile_moe_rec_mlp_silu_kernel(
 
         make_da(0)
         make_da(1)
-        slot_x.extend(gathered("slot_x1", xw.bitcast(U32), U32, 2 * C, 2 * C, offset=MX_ALIGN))
-        slot_dy_planes.extend(gathered("slot_dy_planes1", dy_planes[:], U8, 2 * C, 2 * C, offset=2 * KB + 2 * MX_ALIGN))
-        slot_dy0.extend(gathered("slot_dy0_2", dy0w, U32, 2 * C, C, offset=2 * KB + 11 * MX_ALIGN))
+        slot_dy0.extend(gathered("slot_dy0_1", dy0w, U32, C, C, offset=KB + MX_ALIGN))
+        slot_dy1.extend(gathered("slot_dy1_1", dy1w, U32, C, C, offset=2 * KB + 11 * MX_ALIGN))
+        slot_x_plane.extend(gathered("slot_x_plane1", x_plane[:], U8, 2 * C, 2 * C, offset=2 * KB + 2 * MX_ALIGN))
         slot_dy1.extend(gathered("slot_dy1_2", dy1w, U32, 2 * C, C, offset=3 * KB + 12 * MX_ALIGN))
-        slot_dy0.extend(gathered("slot_dy0_3", dy0w, U32, 3 * C, C, offset=5 * KB + 0))
-        slot_dy1.extend(gathered("slot_dy1_3", dy1w, U32, 3 * C, C, offset=6 * KB))
+        late = gathered("slot_dy0_3", dy0w, U32, 3 * C, C, offset=48 * KB)
+        slot_dy1.extend(gathered("slot_dy1_3", dy1w, U32, 3 * C, C, offset=52 * KB + 512))
         for j in range(TILES - 2):
             make_dx(j)
+            if j == 0:
+                slot_dy0.extend(gathered("slot_dy0_2", dy0w, U32, 2 * C, C, offset=20 * KB + 256) + late)
             make_da(j + 2)
             for r in range(ROW_TILES):
                 scatter(r, j, 1)

@@ -72,7 +72,6 @@ def tile_moe_rec_mlp_silu_kernel(
             nc.sync.dma_start(tile[:], words.rearrange("j p c d -> p j (c d)").bitcast(I32))
             return [tile[:, j, :] for j in range(words.shape[0])]
 
-        x_plane = zeroed_planes("x_plane", T, nc.gpsimd)
         w1_planes = zeroed_planes("w1_planes", H, nc.gpsimd)
         dy_planes = zeroed_planes("dy_planes", T, nc.gpsimd)
         w2_planes = [zeroed_planes(f"w2_planes{half}", H, nc.vector) for half in range(2)]
@@ -88,13 +87,19 @@ def tile_moe_rec_mlp_silu_kernel(
         ident = keep.tile([P, P], F32, name="ident")
         make_identity(nc, ident[:])
 
+        x_plane = keep.tile([P, T], U8, name="x_plane", align_bytes=MX_ALIGN)
         gate_rows = keep.tile([P, P], F32, name="gate_rows")
         w1, w2, w1t, dyw = {}, {}, {}, {}
+
+        def load_x_plane():
+            for q in range(QUADS):
+                source = x_scales[:, QUAD_ROWS * q : QUAD_ROWS * (q + 1), :].bitcast(I32)
+                nc.sync.dma_start(x_plane[32 * q : 32 * (q + 1), :].bitcast(I32), source.to_broadcast([32 // QUAD_ROWS, QUAD_ROWS, T // 4]))
 
         def load_w2(e):
             w2[2 * e], w2[2 * e + 1] = load_passes(f"w2_{e}", w2_word_passes[2 * e : 2 * e + 2])
 
-        load_planes(x_plane, x_scales)
+        load_x_plane()
         nc.sync.dma_start(gate_rows[:], gate[0 : P * P // T, :].rearrange("a (c m) -> (a c) m", m=P))
         xw = load_pass("xw", x_words[0])
         w1[0] = load_pass("w1_0", w1_words[0, 0])
@@ -134,6 +139,7 @@ def tile_moe_rec_mlp_silu_kernel(
         dy0w, dy1w = dyw[0].bitcast(U32), dyw[1].bitcast(U32)
         slot_x_plane.extend(gathered("slot_x_plane0", x_plane[:], U8, 0, 2 * C))
         slot_x.extend(gathered("slot_x0", xw.bitcast(U32), U32, 0, 2 * C))
+        slot_x_plane.extend(gathered("slot_x_plane1", x_plane[:], U8, 2 * C, 2 * C))
         slot_x.extend(gathered("slot_x1", xw.bitcast(U32), U32, 2 * C, 2 * C))
         slot_dy0.extend(gathered("slot_dy0_0", dy0w, U32, 0, C, offset=2 * KB))
         slot_dy1.extend(gathered("slot_dy1_0", dy1w, U32, 0, C, offset=3 * KB))
@@ -209,7 +215,7 @@ def tile_moe_rec_mlp_silu_kernel(
             pairs = da[:].bitcast(F32)
             for u in range(2):
                 nc.tensor.transpose(turned[:, u, :], pairs[:, u : H // 2 : 2], ident[:])
-            interleaved[j] = seats.tile([P, P * PACK], BF16, name=f"interleaved{j}", offset=(48 + 4 * j) * KB, align_bytes=MX_ALIGN)
+            interleaved[j] = seats.tile([P, P * PACK], BF16, name=f"interleaved{j}", offset=(48 + 4 * j if j < 2 else 54 + j) * KB, align_bytes=MX_ALIGN)
             nc.scalar.copy(
                 interleaved[j][:].bitcast(F32).rearrange("p (r u) -> p r u", u=2),
                 turned[:].rearrange("p u r -> p r u"),
@@ -248,10 +254,9 @@ def tile_moe_rec_mlp_silu_kernel(
         make_da(1)
         slot_dy0.extend(gathered("slot_dy0_1", dy0w, U32, C, C, offset=KB + MX_ALIGN))
         slot_dy1.extend(gathered("slot_dy1_1", dy1w, U32, C, C, offset=2 * KB + 11 * MX_ALIGN))
-        slot_x_plane.extend(gathered("slot_x_plane1", x_plane[:], U8, 2 * C, 2 * C, offset=2 * KB + 2 * MX_ALIGN))
         slot_dy1.extend(gathered("slot_dy1_2", dy1w, U32, 2 * C, C, offset=3 * KB + 12 * MX_ALIGN))
-        late = gathered("slot_dy0_3", dy0w, U32, 3 * C, C, offset=48 * KB)
-        slot_dy1.extend(gathered("slot_dy1_3", dy1w, U32, 3 * C, C, offset=52 * KB + 512))
+        late = gathered("slot_dy0_3", dy0w, U32, 3 * C, C, offset=47 * KB + 512)
+        slot_dy1.extend(gathered("slot_dy1_3", dy1w, U32, 3 * C, C, offset=48 * KB + 512))
         for j in range(TILES - 2):
             make_dx(j)
             if j == 0:

@@ -29,8 +29,6 @@ STRIPE = 16
 MX_ALIGN = 64
 BANK = 2048
 KB = 1024
-MODES = "BBBBBBBB"
-HOLD = 3
 AHEAD = 8
 
 
@@ -146,12 +144,18 @@ def tile_moe_rec_mlp_silu_kernel(
         slot_dy_planes.extend(gathered("slot_dy_planes0", dy_planes[:], U8, 0, C))
         slot_dy_planes.extend(gathered("slot_dy_planes123", dy_planes[:], U8, C, 3 * C))
 
-        staged = [keep.tile([P, ROW_TILES, P], F32, name=f"staged{j}") for j in range(TILES)]
-        joint = keep.tile([P, 2, 2 * P], F32, name="joint")
-        windows = [keep.tile([P, T], F32, name=f"window{r}") for r in range(ROW_TILES)]
-        interleaved, codes, da_plane = {}, {}, {}
+        def placed(shape, dtype, name, offset):
+            if offset is None:
+                return keep.tile(shape, dtype, name=name, align_bytes=MX_ALIGN)
+            return seats.tile(shape, dtype, name=name, offset=offset, align_bytes=MX_ALIGN)
 
-        def make_da(j):
+        def period(p):
+            return (20 + 8 * p) * KB
+
+        windows = [keep.tile([P, T], F32, name=f"window{r}") for r in range(ROW_TILES)]
+        silu_neg, gated, part, codes, da_plane = {}, {}, {}, {}, {}
+
+        def factors(j):
             e = j // SLOT_TILES
             a_ps = psum.tile([P, H], F32, name="a_ps")
             nc.tensor.matmul_mx(
@@ -163,27 +167,17 @@ def tile_moe_rec_mlp_silu_kernel(
                 start=True,
                 stop=True,
             )
-            silu_neg = work.tile([P, H], F32, name="silu_neg")
-            nc.scalar.activation(silu_neg[:], a_ps[:], ACT.Silu, bias=no_bias[:], scale=-1.0)
+            silu_neg[j] = work.tile([P, H], F32, name="silu_neg")
+            nc.scalar.activation(silu_neg[j][:], a_ps[:], ACT.Silu, bias=no_bias[:], scale=-1.0)
             tanh_half = work.tile([P, H], F32, name="tanh_half")
             nc.scalar.activation(tanh_half[:], a_ps[:], ACT.Tanh, scale=0.5)
             g = neg_half_gate[:, j : j + 1]
-            gated = work.tile([P, H], F32, name="gated")
-            if MODES[j] == "B":
-                nc.scalar.activation(gated[:], tanh_half[:], ACT.Identity, bias=g, scale=g)
-            else:
-                if MODES[j] in "DC":
-                    nc.scalar.activation(gated[:], tanh_half[:], ACT.Identity, bias=g, scale=g)
-                else:
-                    nc.gpsimd.tensor_scalar(gated[:], tanh_half[:], 1.0, g, ALU.add, ALU.mult)
-                less = work.tile([P, H], F32, name="less")
-                nc.scalar.activation(less[:], silu_neg[:], ACT.Copy, bias=-1.0)
-                if j == 1:
-                    slope = seats.tile([P, H], F32, name="slope1", offset=14 * KB, align_bytes=MX_ALIGN)
-                else:
-                    slope = work.tile([P, H], F32, name="slope")
-                nc.gpsimd.tensor_tensor(slope[:], gated[:], less[:], ALU.mult)
-            dh_ps = psum.tile([P, H], F32, name="dh_ps")
+            gated[j] = work.tile([P, H], F32, name="gated")
+            nc.scalar.activation(gated[j][:], tanh_half[:], ACT.Identity, bias=g, scale=g)
+
+        def first(j, offset):
+            e = j // SLOT_TILES
+            dh_ps = psum.tile([P, H], F32, name="dh_ps", bufs=2)
             for s in range(DY_PASSES):
                 n = DY_PASSES * e + s
                 nc.tensor.matmul_mx(
@@ -195,42 +189,32 @@ def tile_moe_rec_mlp_silu_kernel(
                     start=(s == 0),
                     stop=(s == DY_PASSES - 1),
                 )
-            da = work.tile([P, H], BF16, name="da")
-            if MODES[j] == "B":
-                if j >= HOLD:
-                    part = seats.tile([P, H], F32, name=f"part{j}", offset=(18 + 3 * (j - HOLD)) * KB + 256, align_bytes=MX_ALIGN)
-                elif j == 2:
-                    part = seats.tile([P, H], F32, name="part2", offset=50 * KB + 512, align_bytes=MX_ALIGN)
-                else:
-                    part = work.tile([P, H], F32, name="part")
-                nc.vector.scalar_tensor_tensor(part[:], silu_neg[:], 1.0, dh_ps[:], ALU.subtract, ALU.mult)
-                nc.gpsimd.tensor_tensor(da[:], gated[:], part[:], ALU.mult)
-            elif MODES[j] == "D":
-                nc.vector.tensor_tensor(da[:], slope[:], dh_ps[:], ALU.mult)
-            else:
-                part = work.tile([P, H], F32, name="part")
-                nc.scalar.copy(part[:], dh_ps[:])
-                nc.gpsimd.tensor_tensor(da[:], slope[:], part[:], ALU.mult)
+            part[j] = placed([P, H], F32, f"part{j}", offset)
+            nc.vector.scalar_tensor_tensor(part[j][:], silu_neg[j][:], 1.0, dh_ps[:], ALU.subtract, ALU.mult)
+
+        def second(j, target):
+            da = work.tile([P, H], BF16, name="da", bufs=3)
+            nc.gpsimd.tensor_tensor(da[:], gated[j][:], part[j][:], ALU.mult)
             turned = turns.tile([P, 2, P], F32, name=f"turned{j}", offset=j % 2 * BANK)
             pairs = da[:].bitcast(F32)
             for u in range(2):
                 nc.tensor.transpose(turned[:, u, :], pairs[:, u : H // 2 : 2], ident[:])
-            interleaved[j] = seats.tile([P, P * PACK], BF16, name=f"interleaved{j}", offset=(48 + 4 * j if j < 2 else 54 + j) * KB, align_bytes=MX_ALIGN)
-            nc.scalar.copy(
-                interleaved[j][:].bitcast(F32).rearrange("p (r u) -> p r u", u=2),
-                turned[:].rearrange("p u r -> p r u"),
-            )
-            codes[j] = seats.tile([P, P], U32, name=f"codes{j}", offset=(20 + 3 * j) * KB, align_bytes=MX_ALIGN)
-            da_plane[j] = keep.tile([P, P], U8, name=f"da_plane{j}", align_bytes=MX_ALIGN)
-            nc.vector.quantize_mx(out=codes[j][:].bitcast(FP8X4), scales=da_plane[j][:], in_=interleaved[j][:])
+            nc.scalar.copy(target.bitcast(F32).rearrange("p (r u) -> p r u", u=2), turned[:].rearrange("p u r -> p r u"))
 
-        def make_dx(j):
+        def quantise(j, source, offset):
+            width = source.shape[1] // PACK
+            codes[j] = placed([P, width], U32, f"codes{j}", offset)
+            da_plane[j] = keep.tile([P, width], U8, name=f"da_plane{j}", align_bytes=MX_ALIGN)
+            nc.vector.quantize_mx(out=codes[j][:].bitcast(FP8X4), scales=da_plane[j][:], in_=source)
+
+        def make_dx(j, row_tiles, bank, offset=None):
             e = j // SLOT_TILES
-            dx_ps = turns.tile([P, ROW_TILES, P], F32, name=f"dx_ps{j}", offset=(j + 1) % 2 * BANK)
-            for r in range(ROW_TILES):
+            width = H // len(row_tiles)
+            dx_ps = turns.tile([P, len(row_tiles), width], F32, name=f"dx_ps{j}_{row_tiles[0]}", offset=bank * BANK)
+            for i, r in enumerate(row_tiles):
                 rows = slice(r * P, (r + 1) * P)
                 nc.tensor.matmul_mx(
-                    dx_ps[:, r, :],
+                    dx_ps[:, i, :],
                     lhsT=w1t[e][:, rows].bitcast(FP8X4),
                     lhsT_scale=w1t_planes[QUAD_ROWS * e :, rows],
                     rhs=codes[j][:].bitcast(FP8X4),
@@ -238,39 +222,56 @@ def tile_moe_rec_mlp_silu_kernel(
                     start=True,
                     stop=True,
                 )
-            if j < TILES - 2:
-                nc.scalar.copy(staged[j][:], dx_ps[:])
-            else:
-                nc.scalar.copy(staged[j][:, 0:2, :], dx_ps[:, 0:2, :])
-                nc.scalar.copy(joint[:, :, j % 2 * P : (j % 2 + 1) * P], dx_ps[:, 2:4, :])
+            staged = placed([P, len(row_tiles), width], F32, f"staged{j}_{row_tiles[0]}", offset)
+            nc.scalar.copy(staged[:], dx_ps[:])
+            return staged
 
-        def scatter(r, first, count):
-            nc.vector.tensor_copy(windows[r][:].indirect(listed(first * P, count * P)), staged[first][:, r, :] if count == 1 else joint[:, r - 2, :])
+        def scatter(r, j, source):
+            nc.vector.tensor_copy(windows[r][:].indirect(listed(j * P, source.shape[1])), source)
 
         def store(r):
             nc.sync.dma_start(out[r * P : (r + 1) * P, :], windows[r][:])
 
-        make_da(0)
-        make_da(1)
+        WIDE = P * PACK
+        for j in range(2):
+            factors(j)
+            first(j, None)
+            single = placed([P, WIDE], BF16, f"single{j}", (8 + 4 * j) * KB)
+            second(j, single[:])
+            quantise(j, single[:], 16 * KB if j == 0 else None)
         slot_dy0.extend(gathered("slot_dy0_1", dy0w, U32, C, C, offset=KB + MX_ALIGN))
         slot_dy1.extend(gathered("slot_dy1_1", dy1w, U32, C, C, offset=2 * KB + 11 * MX_ALIGN))
         slot_dy1.extend(gathered("slot_dy1_2", dy1w, U32, 2 * C, C, offset=3 * KB + 12 * MX_ALIGN))
-        late = gathered("slot_dy0_3", dy0w, U32, 3 * C, C, offset=47 * KB + 512)
-        slot_dy1.extend(gathered("slot_dy1_3", dy1w, U32, 3 * C, C, offset=48 * KB + 512))
-        for j in range(TILES - 2):
-            make_dx(j)
-            if j == 0:
-                slot_dy0.extend(gathered("slot_dy0_2", dy0w, U32, 2 * C, C, offset=20 * KB + 256) + late)
-            make_da(j + 2)
-            for r in range(ROW_TILES):
-                scatter(r, j, 1)
-        make_dx(TILES - 2)
-        for r in range(2):
-            scatter(r, TILES - 2, 1)
-        make_dx(TILES - 1)
-        for r in range(2):
-            scatter(r, TILES - 1, 1)
-            store(r)
-        for r in range(2, ROW_TILES):
-            scatter(r, TILES - 2, 2)
+        late = gathered("slot_dy0_3", dy0w, U32, 3 * C, C, offset=7 * KB + 512)
+        slot_dy1.extend(gathered("slot_dy1_3", dy1w, U32, 3 * C, C, offset=8 * KB + 512))
+        every = range(ROW_TILES)
+        staged = make_dx(0, every, 1)
+        slot_dy0.extend(gathered("slot_dy0_2", dy0w, U32, 2 * C, C, offset=16 * KB + 256) + late)
+        seat_first = {2: 10 * KB + 512, 3: 14 * KB + 256}
+        held = [(r, 0, staged[:, r, :]) for r in every]
+        for e in range(1, E):
+            pair = placed([P, 2 * WIDE], BF16, f"pair{e}", period(e) + 2 * KB)
+            for c in range(SLOT_TILES):
+                j = SLOT_TILES * e + c
+                factors(j)
+                first(j, seat_first[j])
+                second(j, pair[:, c * WIDE : (c + 1) * WIDE])
+            if e == 1:
+                staged = make_dx(1, every, 1)
+                waiting = [(r, 1, staged[:, r, :]) for r in every]
+            else:
+                staged = make_dx(SLOT_TILES * (e - 1), (2, 3), 1)
+                waiting = [(r, SLOT_TILES * (e - 1), staged[:, r - 2, :]) for r in (2, 3)]
+            for r, j, source in held:
+                scatter(r, j, source)
+            quantise(SLOT_TILES * e, pair[:], None)
+            seat_first[SLOT_TILES * e + 2] = period(e) + 256
+            seat_first[SLOT_TILES * e + 3] = period(e) + 4 * KB - 256
+            staged = make_dx(SLOT_TILES * e, (0, 1), 2)
+            held = waiting + [(r, SLOT_TILES * e, staged[:, r, :]) for r in (0, 1)]
+        staged = make_dx(TILES - 2, (2, 3), 0)
+        for r, j, source in held[0:2]:
+            scatter(r, j, source)
+        for r, j, source in held[2:4] + [(r, TILES - 2, staged[:, r - 2, :]) for r in (2, 3)]:
+            scatter(r, j, source)
             store(r)

@@ -21,15 +21,29 @@ PACK = 4
 QUADS = 4
 QUAD_ROWS = 4
 PLANES = 4
-SLOT_TILES = C // P
-TILES = E * SLOT_TILES
+PER_EXPERT = C // P
+GROUPS = E * PER_EXPERT
 ROW_TILES = K // P
+LOW_ROWS, HIGH_ROWS = (0, 1), (2, 3)
 DY_PASSES = N // (P * PACK)
 STRIPE = 16
 MX_ALIGN = 64
 BANK = 2048
 KB = 1024
-AHEAD = 8
+
+HOST_DY = (2 * KB, 6 * KB)
+HOST_INTERLEAVED_1 = 12 * KB
+HOST_CODES_0 = 16 * KB
+HOST_PAIR = {e: (22 + 8 * e) * KB for e in range(1, E)}
+LAP = 256
+
+
+def below(host, size):
+    return host + LAP - size
+
+
+def above(host, host_size):
+    return host + host_size - LAP
 
 
 def tile_moe_rec_mlp_silu_kernel(
@@ -38,27 +52,32 @@ def tile_moe_rec_mlp_silu_kernel(
     nc = tc.nc
     with ExitStack() as ctx:
         keep = ctx.enter_context(tc.tile_pool(name="keep", bufs=1))
-        work = ctx.enter_context(tc.tile_pool(name="work", bufs=AHEAD))
+        work = ctx.enter_context(tc.tile_pool(name="work", bufs=GROUPS))
         seats = ctx.enter_context(tc.tile_pool(name="seats", bufs=1))
         psum = ctx.enter_context(tc.psum_pool(name="psum", bufs=3))
-        turns = ctx.enter_context(tc.psum_pool(name="turns", bufs=1))
+        banks = ctx.enter_context(tc.psum_pool(name="banks", bufs=1))
 
         offsets = keep.tile([P, T // STRIPE], U16, name="offsets")
         nc.sync.dma_start(offsets[:], offs)
 
-        def listed(first, count):
-            return offsets[:, first // STRIPE : (first + count) // STRIPE]
+        def listed(first_slot, count):
+            return offsets[:, first_slot // STRIPE : (first_slot + count) // STRIPE]
+
+        def placed(shape, dtype, name, offset):
+            if offset is None:
+                return keep.tile(shape, dtype, name=name, align_bytes=MX_ALIGN)
+            return seats.tile(shape, dtype, name=name, offset=offset, align_bytes=MX_ALIGN)
 
         def zeroed_planes(name, width, engine):
             tile = keep.tile([P, width], U8, name=name, align_bytes=MX_ALIGN)
             engine.memset(tile[:].bitcast(I32), 0)
             return tile
 
-        def load_planes(tile, planes, queue=nc.sync):
+        def load_planes(tile, planes):
             rows = planes.shape[0] * QUAD_ROWS
             for q in range(QUADS):
                 source = planes[:, QUAD_ROWS * q : QUAD_ROWS * (q + 1), :]
-                queue.dma_start(tile[32 * q : 32 * q + rows, :].bitcast(I32), source.bitcast(I32))
+                nc.sync.dma_start(tile[32 * q : 32 * q + rows, :].bitcast(I32), source.bitcast(I32))
 
         def load_pass(name, words):
             tile = keep.tile([P, words.shape[1]], I32, name=name, align_bytes=MX_ALIGN)
@@ -72,10 +91,9 @@ def tile_moe_rec_mlp_silu_kernel(
 
         w1_planes = zeroed_planes("w1_planes", H, nc.gpsimd)
         dy_planes = zeroed_planes("dy_planes", T, nc.gpsimd)
-        w2_planes = [zeroed_planes(f"w2_planes{half}", H, nc.vector) for half in range(2)]
+        w2_planes = [zeroed_planes(f"w2_planes{half}", H, nc.vector) for half in range(E * DY_PASSES // PLANES)]
         w1t_planes = zeroed_planes("w1t_planes", K, nc.vector)
         w2_scale_rows = w2t_scales.rearrange("e s b i -> (e s) b i")
-        w2_word_passes = w2t_words.rearrange("e s p i d -> (e s) p i d")
 
         zero = keep.tile([P, 1], F32, name="zero")
         no_bias = keep.tile([P, 1], F32, name="no_bias")
@@ -86,77 +104,57 @@ def tile_moe_rec_mlp_silu_kernel(
         make_identity(nc, ident[:])
 
         x_plane = keep.tile([P, T], U8, name="x_plane", align_bytes=MX_ALIGN)
+        for q in range(QUADS):
+            source = x_scales[:, QUAD_ROWS * q : QUAD_ROWS * (q + 1), :].bitcast(I32)
+            nc.sync.dma_start(x_plane[32 * q : 32 * (q + 1), :].bitcast(I32), source.to_broadcast([32 // QUAD_ROWS, QUAD_ROWS, T // 4]))
         gate_rows = keep.tile([P, P], F32, name="gate_rows")
-        w1, w2, w1t, dyw = {}, {}, {}, {}
-
-        def load_x_plane():
-            for q in range(QUADS):
-                source = x_scales[:, QUAD_ROWS * q : QUAD_ROWS * (q + 1), :].bitcast(I32)
-                nc.sync.dma_start(x_plane[32 * q : 32 * (q + 1), :].bitcast(I32), source.to_broadcast([32 // QUAD_ROWS, QUAD_ROWS, T // 4]))
-
-        def load_w2(e):
-            w2[2 * e], w2[2 * e + 1] = load_passes(f"w2_{e}", w2_word_passes[2 * e : 2 * e + 2])
-
-        load_x_plane()
         nc.sync.dma_start(gate_rows[:], gate[0 : P * P // T, :].rearrange("a (c m) -> (a c) m", m=P))
-        xw = load_pass("xw", x_words[0])
-        w1[0] = load_pass("w1_0", w1_words[0, 0])
+        xw = load_pass("xw", x_words[0]).bitcast(U32)
+        w1 = [load_pass("w1_0", w1_words[0, 0])]
         load_planes(w1_planes, w1_scales[:, 0])
-        dyw[0] = load_pass("dyw0", dy_words[0])
-        dyw[1] = load_pass("dyw1", dy_words[1])
+        dyw = [load_pass(f"dyw{s}", dy_words[s]).bitcast(U32) for s in range(DY_PASSES)]
         load_planes(dy_planes, dy_scales)
-        load_w2(0)
+        w2 = load_passes("w2_0", w2t_words[0])
         load_planes(w2_planes[0], w2_scale_rows[0:PLANES])
-        w1[1] = load_pass("w1_1", w1_words[1, 0])
-        load_w2(1)
+        w1.append(load_pass("w1_1", w1_words[1, 0]))
+        w2.extend(load_passes("w2_1", w2t_words[1]))
         load_planes(w1t_planes, w1t_scales[:, 0])
-        w1t[0] = load_pass("w1t_0", w1t_words[0, 0])
-        w1[2] = load_pass("w1_2", w1_words[2, 0])
+        w1t = [load_pass("w1t_0", w1t_words[0, 0])]
+        w1.append(load_pass("w1_2", w1_words[2, 0]))
         load_planes(w2_planes[1], w2_scale_rows[PLANES : 2 * PLANES])
-        load_w2(2)
-        w1t[1] = load_pass("w1t_1", w1t_words[1, 0])
-        w1[3] = load_pass("w1_3", w1_words[3, 0])
-        load_w2(3)
-        w1t[2], w1t[3] = load_passes("w1t_23", w1t_words[2:4, 0])
+        w2.extend(load_passes("w2_2", w2t_words[2]))
+        w1t.append(load_pass("w1t_1", w1t_words[1, 0]))
+        w1.append(load_pass("w1_3", w1_words[3, 0]))
+        w2.extend(load_passes("w2_3", w2t_words[3]))
+        w1t.extend(load_passes("w1t_23", w1t_words[2:4, 0]))
 
-        gate_ps = turns.tile([P, H], F32, name="gate_ps", offset=0)
+        gate_ps = banks.tile([P, H], F32, name="gate_ps", offset=0)
         nc.tensor.transpose(gate_ps[:, 0:P], gate_rows[:], ident[:])
-        neg_half_gate = keep.tile([P, TILES], F32, name="neg_half_gate")
-        nc.scalar.activation(neg_half_gate[:], gate_ps[:, 0:TILES], ACT.Copy, scale=-0.5)
+        neg_half_gate = keep.tile([P, GROUPS], F32, name="neg_half_gate")
+        nc.scalar.activation(neg_half_gate[:], gate_ps[:, 0:GROUPS], ACT.Copy, scale=-0.5)
 
-        def gathered(name, window, dtype, first, count, offset=None):
-            if offset is None:
-                tile = keep.tile([P, count], dtype, name=name, align_bytes=MX_ALIGN)
-            else:
-                tile = seats.tile([P, count], dtype, name=name, offset=offset, align_bytes=MX_ALIGN)
-            nc.vector.tensor_copy(tile[:], window.indirect(listed(first, count)))
-            return [tile[:, i * P : (i + 1) * P] for i in range(count // P)]
+        slot_x_plane, slot_x, slot_dy_planes = {}, {}, {}
+        slot_dy = [{} for s in range(DY_PASSES)]
 
-        slot_x_plane, slot_x, slot_dy_planes, slot_dy0, slot_dy1 = [], [], [], [], []
-        slot_dy = [slot_dy0, slot_dy1]
-        dy0w, dy1w = dyw[0].bitcast(U32), dyw[1].bitcast(U32)
-        slot_x_plane.extend(gathered("slot_x_plane0", x_plane[:], U8, 0, 2 * C))
-        slot_x.extend(gathered("slot_x0", xw.bitcast(U32), U32, 0, 2 * C))
-        slot_x_plane.extend(gathered("slot_x_plane1", x_plane[:], U8, 2 * C, 2 * C))
-        slot_x.extend(gathered("slot_x1", xw.bitcast(U32), U32, 2 * C, 2 * C))
-        slot_dy0.extend(gathered("slot_dy0_0", dy0w, U32, 0, C, offset=2 * KB))
-        slot_dy1.extend(gathered("slot_dy1_0", dy1w, U32, 0, C, offset=3 * KB))
-        slot_dy_planes.extend(gathered("slot_dy_planes0", dy_planes[:], U8, 0, C))
-        slot_dy_planes.extend(gathered("slot_dy_planes123", dy_planes[:], U8, C, 3 * C))
+        def gather(into, name, window, dtype, experts, offset=None):
+            tile = placed([P, len(experts) * C], dtype, f"{name}_{experts[0]}", offset)
+            nc.vector.tensor_copy(tile[:], window.indirect(listed(experts[0] * C, len(experts) * C)))
+            for i in range(len(experts) * PER_EXPERT):
+                into[experts[0] * PER_EXPERT + i] = tile[:, i * P : (i + 1) * P]
 
-        def placed(shape, dtype, name, offset):
-            if offset is None:
-                return keep.tile(shape, dtype, name=name, align_bytes=MX_ALIGN)
-            return seats.tile(shape, dtype, name=name, offset=offset, align_bytes=MX_ALIGN)
-
-        def period(p):
-            return (20 + 8 * p) * KB
+        for experts in ((0, 1), (2, 3)):
+            gather(slot_x_plane, "slot_x_plane", x_plane[:], U8, experts)
+            gather(slot_x, "slot_x", xw, U32, experts)
+        for s in range(DY_PASSES):
+            gather(slot_dy[s], f"slot_dy{s}", dyw[s], U32, (0,), HOST_DY[s])
+        gather(slot_dy_planes, "slot_dy_planes", dy_planes[:], U8, (0,))
+        gather(slot_dy_planes, "slot_dy_planes", dy_planes[:], U8, (1, 2, 3))
 
         windows = [keep.tile([P, T], F32, name=f"window{r}") for r in range(ROW_TILES)]
-        silu_neg, gated, part, codes, da_plane = {}, {}, {}, {}, {}
+        codes, da_plane = {}, {}
 
-        def factors(j):
-            e = j // SLOT_TILES
+        def make_da(j, part_offset, interleaved):
+            e = j // PER_EXPERT
             a_ps = psum.tile([P, H], F32, name="a_ps")
             nc.tensor.matmul_mx(
                 a_ps[:],
@@ -167,16 +165,14 @@ def tile_moe_rec_mlp_silu_kernel(
                 start=True,
                 stop=True,
             )
-            silu_neg[j] = work.tile([P, H], F32, name="silu_neg")
-            nc.scalar.activation(silu_neg[j][:], a_ps[:], ACT.Silu, bias=no_bias[:], scale=-1.0)
+            silu_neg = work.tile([P, H], F32, name="silu_neg")
+            nc.scalar.activation(silu_neg[:], a_ps[:], ACT.Silu, bias=no_bias[:], scale=-1.0)
             tanh_half = work.tile([P, H], F32, name="tanh_half")
             nc.scalar.activation(tanh_half[:], a_ps[:], ACT.Tanh, scale=0.5)
             g = neg_half_gate[:, j : j + 1]
-            gated[j] = work.tile([P, H], F32, name="gated")
-            nc.scalar.activation(gated[j][:], tanh_half[:], ACT.Identity, bias=g, scale=g)
+            gated = work.tile([P, H], F32, name="gated")
+            nc.scalar.activation(gated[:], tanh_half[:], ACT.Identity, bias=g, scale=g)
 
-        def first(j, offset):
-            e = j // SLOT_TILES
             dh_ps = psum.tile([P, H], F32, name="dh_ps", bufs=2)
             for s in range(DY_PASSES):
                 n = DY_PASSES * e + s
@@ -189,28 +185,27 @@ def tile_moe_rec_mlp_silu_kernel(
                     start=(s == 0),
                     stop=(s == DY_PASSES - 1),
                 )
-            part[j] = placed([P, H], F32, f"part{j}", offset)
-            nc.vector.scalar_tensor_tensor(part[j][:], silu_neg[j][:], 1.0, dh_ps[:], ALU.subtract, ALU.mult)
+            part = placed([P, H], F32, f"part{j}", part_offset)
+            nc.vector.scalar_tensor_tensor(part[:], silu_neg[:], 1.0, dh_ps[:], ALU.subtract, ALU.mult)
 
-        def second(j, target):
             da = work.tile([P, H], BF16, name="da", bufs=3)
-            nc.gpsimd.tensor_tensor(da[:], gated[j][:], part[j][:], ALU.mult)
-            turned = turns.tile([P, 2, P], F32, name=f"turned{j}", offset=j % 2 * BANK)
+            nc.gpsimd.tensor_tensor(da[:], gated[:], part[:], ALU.mult)
+            turned = banks.tile([P, 2, P], F32, name=f"turned{j}", offset=j % 2 * BANK)
             pairs = da[:].bitcast(F32)
             for u in range(2):
                 nc.tensor.transpose(turned[:, u, :], pairs[:, u : H // 2 : 2], ident[:])
-            nc.scalar.copy(target.bitcast(F32).rearrange("p (r u) -> p r u", u=2), turned[:].rearrange("p u r -> p r u"))
+            nc.scalar.copy(interleaved.bitcast(F32).rearrange("p (m u) -> p m u", u=2), turned[:].rearrange("p u m -> p m u"))
 
-        def quantise(j, source, offset):
-            width = source.shape[1] // PACK
-            codes[j] = placed([P, width], U32, f"codes{j}", offset)
-            da_plane[j] = keep.tile([P, width], U8, name=f"da_plane{j}", align_bytes=MX_ALIGN)
-            nc.vector.quantize_mx(out=codes[j][:].bitcast(FP8X4), scales=da_plane[j][:], in_=source)
+        def quantise(j, interleaved, codes_offset=None):
+            slots = interleaved.shape[1] // PACK
+            codes[j] = placed([P, slots], U32, f"codes{j}", codes_offset)
+            da_plane[j] = keep.tile([P, slots], U8, name=f"da_plane{j}", align_bytes=MX_ALIGN)
+            nc.vector.quantize_mx(out=codes[j][:].bitcast(FP8X4), scales=da_plane[j][:], in_=interleaved)
 
-        def make_dx(j, row_tiles, bank, offset=None):
-            e = j // SLOT_TILES
-            width = H // len(row_tiles)
-            dx_ps = turns.tile([P, len(row_tiles), width], F32, name=f"dx_ps{j}_{row_tiles[0]}", offset=bank * BANK)
+        def make_dx(j, row_tiles, bank):
+            e = j // PER_EXPERT
+            slots = codes[j].shape[1]
+            dx_ps = banks.tile([P, len(row_tiles), slots], F32, name=f"dx_ps{j}_{row_tiles[0]}", offset=bank * BANK)
             for i, r in enumerate(row_tiles):
                 rows = slice(r * P, (r + 1) * P)
                 nc.tensor.matmul_mx(
@@ -222,56 +217,39 @@ def tile_moe_rec_mlp_silu_kernel(
                     start=True,
                     stop=True,
                 )
-            staged = placed([P, len(row_tiles), width], F32, f"staged{j}_{row_tiles[0]}", offset)
+            staged = keep.tile([P, len(row_tiles), slots], F32, name=f"staged{j}_{row_tiles[0]}", align_bytes=MX_ALIGN)
             nc.scalar.copy(staged[:], dx_ps[:])
-            return staged
+            return [(r, j, staged[:, i, :]) for i, r in enumerate(row_tiles)]
 
-        def scatter(r, j, source):
-            nc.vector.tensor_copy(windows[r][:].indirect(listed(j * P, source.shape[1])), source)
+        def scatter(r, j, values):
+            nc.vector.tensor_copy(windows[r][:].indirect(listed(j * P, values.shape[1])), values)
 
-        def store(r):
-            nc.sync.dma_start(out[r * P : (r + 1) * P, :], windows[r][:])
+        for j in range(PER_EXPERT):
+            interleaved = placed([P, H], BF16, f"interleaved{j}", HOST_INTERLEAVED_1 if j == 1 else None)
+            make_da(j, None, interleaved[:])
+            quantise(j, interleaved[:], HOST_CODES_0 if j == 0 else None)
+        gather(slot_dy[0], "slot_dy0", dyw[0], U32, (1,), below(HOST_DY[0], 4 * C))
+        gather(slot_dy[1], "slot_dy1", dyw[1], U32, (1,), above(HOST_DY[0], 4 * C))
+        gather(slot_dy[1], "slot_dy1", dyw[1], U32, (2, 3), above(HOST_DY[1], 4 * C))
+        gather(slot_dy[0], "slot_dy0", dyw[0], U32, (3,), below(HOST_DY[1], 4 * C))
+        ready = make_dx(0, range(ROW_TILES), 1)
+        gather(slot_dy[0], "slot_dy0", dyw[0], U32, (2,), above(HOST_CODES_0, 4 * P))
 
-        WIDE = P * PACK
-        for j in range(2):
-            factors(j)
-            first(j, None)
-            single = placed([P, WIDE], BF16, f"single{j}", (8 + 4 * j) * KB)
-            second(j, single[:])
-            quantise(j, single[:], 16 * KB if j == 0 else None)
-        slot_dy0.extend(gathered("slot_dy0_1", dy0w, U32, C, C, offset=KB + MX_ALIGN))
-        slot_dy1.extend(gathered("slot_dy1_1", dy1w, U32, C, C, offset=2 * KB + 11 * MX_ALIGN))
-        slot_dy1.extend(gathered("slot_dy1_2", dy1w, U32, 2 * C, C, offset=3 * KB + 12 * MX_ALIGN))
-        late = gathered("slot_dy0_3", dy0w, U32, 3 * C, C, offset=7 * KB + 512)
-        slot_dy1.extend(gathered("slot_dy1_3", dy1w, U32, 3 * C, C, offset=8 * KB + 512))
-        every = range(ROW_TILES)
-        staged = make_dx(0, every, 1)
-        slot_dy0.extend(gathered("slot_dy0_2", dy0w, U32, 2 * C, C, offset=16 * KB + 256) + late)
-        seat_first = {2: 10 * KB + 512, 3: 14 * KB + 256}
-        held = [(r, 0, staged[:, r, :]) for r in every]
+        part_offsets = (below(HOST_INTERLEAVED_1, 4 * H), below(HOST_CODES_0, 4 * H))
         for e in range(1, E):
-            pair = placed([P, 2 * WIDE], BF16, f"pair{e}", period(e) + 2 * KB)
-            for c in range(SLOT_TILES):
-                j = SLOT_TILES * e + c
-                factors(j)
-                first(j, seat_first[j])
-                second(j, pair[:, c * WIDE : (c + 1) * WIDE])
-            if e == 1:
-                staged = make_dx(1, every, 1)
-                waiting = [(r, 1, staged[:, r, :]) for r in every]
-            else:
-                staged = make_dx(SLOT_TILES * (e - 1), (2, 3), 1)
-                waiting = [(r, SLOT_TILES * (e - 1), staged[:, r - 2, :]) for r in (2, 3)]
-            for r, j, source in held:
-                scatter(r, j, source)
-            quantise(SLOT_TILES * e, pair[:], None)
-            seat_first[SLOT_TILES * e + 2] = period(e) + 256
-            seat_first[SLOT_TILES * e + 3] = period(e) + 4 * KB - 256
-            staged = make_dx(SLOT_TILES * e, (0, 1), 2)
-            held = waiting + [(r, SLOT_TILES * e, staged[:, r, :]) for r in (0, 1)]
-        staged = make_dx(TILES - 2, (2, 3), 0)
-        for r, j, source in held[0:2]:
-            scatter(r, j, source)
-        for r, j, source in held[2:4] + [(r, TILES - 2, staged[:, r - 2, :]) for r in (2, 3)]:
-            scatter(r, j, source)
-            store(r)
+            first = PER_EXPERT * e
+            pair = placed([P, PER_EXPERT * H], BF16, f"pair{e}", HOST_PAIR[e])
+            for c in range(PER_EXPERT):
+                make_da(first + c, part_offsets[c], pair[:, c * H : (c + 1) * H])
+            held = make_dx(1, range(ROW_TILES), 1) if e == 1 else make_dx(first - PER_EXPERT, HIGH_ROWS, 1)
+            for r, j, values in ready:
+                scatter(r, j, values)
+            quantise(first, pair[:])
+            part_offsets = (below(HOST_PAIR[e], 4 * H), above(HOST_PAIR[e], 2 * PER_EXPERT * H))
+            ready = held + make_dx(first, LOW_ROWS, 2)
+
+        last_group = GROUPS - PER_EXPERT
+        for r, j, values in ready + make_dx(last_group, HIGH_ROWS, 0):
+            scatter(r, j, values)
+            if j == last_group:
+                nc.sync.dma_start(out[r * P : (r + 1) * P, :], windows[r][:])

@@ -31,19 +31,23 @@ MX_ALIGN = 64
 BANK = 2048
 KB = 1024
 
-HOST_DY = (2 * KB, 6 * KB)
-HOST_INTERLEAVED_1 = 12 * KB
-HOST_CODES_0 = 16 * KB
-HOST_PAIR = {e: (22 + 8 * e) * KB for e in range(1, E)}
-LAP = 256
+A_BANKS = (0, 1, 2, 3, 4, 6, 3, 5)
+LAP = 64
+ROOM = 2 * KB
+HOSTS = ("right0", "slope1", "right3", "interleaved1", "interleaved2", "interleaved0", "part3", "da3", "da5", "da7", "dh5")
+XW = 3 * len(HOSTS) * ROOM
 
 
-def below(host, size):
-    return host + LAP - size
+def host(name):
+    return (3 * HOSTS.index(name) + 1) * ROOM
 
 
-def above(host, host_size):
-    return host + host_size - LAP
+def below(name, size):
+    return host(name) + LAP - size
+
+
+def above(name, host_size=ROOM):
+    return host(name) + host_size - LAP
 
 
 def tile_moe_rec_mlp_silu_kernel(
@@ -52,9 +56,7 @@ def tile_moe_rec_mlp_silu_kernel(
     nc = tc.nc
     with ExitStack() as ctx:
         keep = ctx.enter_context(tc.tile_pool(name="keep", bufs=1))
-        work = ctx.enter_context(tc.tile_pool(name="work", bufs=GROUPS))
         seats = ctx.enter_context(tc.tile_pool(name="seats", bufs=1))
-        psum = ctx.enter_context(tc.psum_pool(name="psum", bufs=3))
         banks = ctx.enter_context(tc.psum_pool(name="banks", bufs=1))
 
         offsets = keep.tile([P, T // STRIPE], U16, name="offsets")
@@ -79,8 +81,8 @@ def tile_moe_rec_mlp_silu_kernel(
                 source = planes[:, QUAD_ROWS * q : QUAD_ROWS * (q + 1), :]
                 nc.sync.dma_start(tile[32 * q : 32 * q + rows, :].bitcast(I32), source.bitcast(I32))
 
-        def load_pass(name, words):
-            tile = keep.tile([P, words.shape[1]], I32, name=name, align_bytes=MX_ALIGN)
+        def load_pass(name, words, offset=None):
+            tile = placed([P, words.shape[1]], I32, name, offset)
             nc.sync.dma_start(tile[:], words.rearrange("p c d -> p (c d)").bitcast(I32))
             return tile[:]
 
@@ -109,29 +111,29 @@ def tile_moe_rec_mlp_silu_kernel(
             nc.sync.dma_start(x_plane[32 * q : 32 * (q + 1), :].bitcast(I32), source.to_broadcast([32 // QUAD_ROWS, QUAD_ROWS, T // 4]))
         gate_rows = keep.tile([P, P], F32, name="gate_rows")
         nc.sync.dma_start(gate_rows[:], gate[0 : P * P // T, :].rearrange("a (c m) -> (a c) m", m=P))
-        xw = load_pass("xw", x_words[0]).bitcast(U32)
-        w1 = [load_pass("w1_0", w1_words[0, 0])]
+        xw = load_pass("xw", x_words[0], XW).bitcast(U32)
+        w1 = load_passes("w1_01", w1_words[0:2, 0])
         load_planes(w1_planes, w1_scales[:, 0])
         dyw = [load_pass(f"dyw{s}", dy_words[s]).bitcast(U32) for s in range(DY_PASSES)]
         load_planes(dy_planes, dy_scales)
         w2 = load_passes("w2_0", w2t_words[0])
         load_planes(w2_planes[0], w2_scale_rows[0:PLANES])
-        w1.append(load_pass("w1_1", w1_words[1, 0]))
+        w1.extend(load_passes("w1_23", w1_words[2:4, 0]))
         w2.extend(load_passes("w2_1", w2t_words[1]))
         load_planes(w1t_planes, w1t_scales[:, 0])
-        w1t = [load_pass("w1t_0", w1t_words[0, 0])]
-        w1.append(load_pass("w1_2", w1_words[2, 0]))
+        w1t = load_passes("w1t_01", w1t_words[0:2, 0])
         load_planes(w2_planes[1], w2_scale_rows[PLANES : 2 * PLANES])
         w2.extend(load_passes("w2_2", w2t_words[2]))
-        w1t.append(load_pass("w1t_1", w1t_words[1, 0]))
-        w1.append(load_pass("w1_3", w1_words[3, 0]))
         w2.extend(load_passes("w2_3", w2t_words[3]))
         w1t.extend(load_passes("w1t_23", w1t_words[2:4, 0]))
 
-        gate_ps = banks.tile([P, H], F32, name="gate_ps", offset=0)
+        def bank(shape, name, index):
+            return banks.tile(shape, F32, name=name, offset=index * BANK)
+
+        gate_ps = bank([P, H], "gate_ps", 7)
         nc.tensor.transpose(gate_ps[:, 0:P], gate_rows[:], ident[:])
-        neg_half_gate = keep.tile([P, GROUPS], F32, name="neg_half_gate")
-        nc.scalar.activation(neg_half_gate[:], gate_ps[:, 0:GROUPS], ACT.Copy, scale=-0.5)
+        half_gate = keep.tile([P, GROUPS], F32, name="half_gate")
+        nc.scalar.activation(half_gate[:], gate_ps[:, 0:GROUPS], ACT.Copy, scale=-0.5)
 
         slot_x_plane, slot_x, slot_dy_planes = {}, {}, {}
         slot_dy = [{} for s in range(DY_PASSES)]
@@ -142,20 +144,12 @@ def tile_moe_rec_mlp_silu_kernel(
             for i in range(len(experts) * PER_EXPERT):
                 into[experts[0] * PER_EXPERT + i] = tile[:, i * P : (i + 1) * P]
 
-        for experts in ((0, 1), (2, 3)):
-            gather(slot_x_plane, "slot_x_plane", x_plane[:], U8, experts)
-            gather(slot_x, "slot_x", xw, U32, experts)
-        for s in range(DY_PASSES):
-            gather(slot_dy[s], f"slot_dy{s}", dyw[s], U32, (0,), HOST_DY[s])
-        gather(slot_dy_planes, "slot_dy_planes", dy_planes[:], U8, (0,))
-        gather(slot_dy_planes, "slot_dy_planes", dy_planes[:], U8, (1, 2, 3))
-
         windows = [keep.tile([P, T], F32, name=f"window{r}") for r in range(ROW_TILES)]
-        codes, da_plane = {}, {}
+        left, right, slope, dh, da, codes, da_plane = {}, {}, {}, {}, {}, {}, {}
 
-        def make_da(j, part_offset, interleaved):
+        def factors(j, ahead=True, offset=None):
+            a_ps = bank([P, H], f"a_ps{j}", A_BANKS[j])
             e = j // PER_EXPERT
-            a_ps = psum.tile([P, H], F32, name="a_ps")
             nc.tensor.matmul_mx(
                 a_ps[:],
                 lhsT=slot_x[j].bitcast(FP8X4),
@@ -165,15 +159,24 @@ def tile_moe_rec_mlp_silu_kernel(
                 start=True,
                 stop=True,
             )
-            silu_neg = work.tile([P, H], F32, name="silu_neg")
-            nc.scalar.activation(silu_neg[:], a_ps[:], ACT.Silu, bias=no_bias[:], scale=-1.0)
-            tanh_half = work.tile([P, H], F32, name="tanh_half")
-            nc.scalar.activation(tanh_half[:], a_ps[:], ACT.Tanh, scale=0.5)
-            g = neg_half_gate[:, j : j + 1]
-            gated = work.tile([P, H], F32, name="gated")
-            nc.scalar.activation(gated[:], tanh_half[:], ACT.Identity, bias=g, scale=g)
+            left[j] = keep.tile([P, H], F32, name=f"left{j}")
+            nc.scalar.activation(left[j][:], a_ps[:], ACT.Silu, bias=no_bias[:], scale=-1.0)
+            right[j] = placed([P, H], F32, f"right{j}", offset)
+            nc.scalar.activation(right[j][:], a_ps[:], ACT.Tanh, scale=0.5)
+            if ahead:
+                nc.gpsimd.tensor_scalar(left[j][:], left[j][:], 1.0, -1.0, ALU.mult, ALU.add)
+            else:
+                g = half_gate[:, j : j + 1]
+                nc.gpsimd.tensor_scalar(left[j][:], left[j][:], -1.0, g, ALU.add, ALU.mult)
 
-            dh_ps = psum.tile([P, H], F32, name="dh_ps", bufs=2)
+        def make_slope(j, offset=None):
+            nc.scalar.activation(right[j][:], right[j][:], ACT.Copy, bias=1.0)
+            slope[j] = placed([P, H], F32, f"slope{j}", offset)
+            nc.gpsimd.tensor_tensor(slope[j][:], left[j][:], right[j][:], ALU.mult)
+
+        def make_dh(j, index):
+            e = j // PER_EXPERT
+            dh_ps = bank([P, H], f"dh_ps{j}", index)
             for s in range(DY_PASSES):
                 n = DY_PASSES * e + s
                 nc.tensor.matmul_mx(
@@ -185,71 +188,126 @@ def tile_moe_rec_mlp_silu_kernel(
                     start=(s == 0),
                     stop=(s == DY_PASSES - 1),
                 )
+            return dh_ps
+
+        def da_on_vector(j, index):
+            dh_ps = make_dh(j, index)
+            da[j] = keep.tile([P, H], BF16, name=f"da{j}")
+            nc.vector.scalar_tensor_tensor(da[j][:], dh_ps[:], half_gate[:, j : j + 1], slope[j][:], ALU.mult, ALU.mult)
+
+        def da_on_both(j, index, part_offset=None, da_offset=None):
+            dh_ps = make_dh(j, index)
             part = placed([P, H], F32, f"part{j}", part_offset)
-            nc.vector.scalar_tensor_tensor(part[:], silu_neg[:], 1.0, dh_ps[:], ALU.subtract, ALU.mult)
+            nc.vector.scalar_tensor_tensor(part[:], right[j][:], 1.0, dh_ps[:], ALU.add, ALU.mult)
+            da[j] = placed([P, H], BF16, f"da{j}", da_offset)
+            nc.gpsimd.tensor_tensor(da[j][:], left[j][:], part[:], ALU.mult)
 
-            da = work.tile([P, H], BF16, name="da", bufs=3)
-            nc.gpsimd.tensor_tensor(da[:], gated[:], part[:], ALU.mult)
-            turned = banks.tile([P, 2, P], F32, name=f"turned{j}", offset=j % 2 * BANK)
-            pairs = da[:].bitcast(F32)
-            for u in range(2):
-                nc.tensor.transpose(turned[:, u, :], pairs[:, u : H // 2 : 2], ident[:])
-            nc.scalar.copy(interleaved.bitcast(F32).rearrange("p (m u) -> p m u", u=2), turned[:].rearrange("p u m -> p m u"))
+        def stage_dh(j, index, offset=None):
+            dh_ps = make_dh(j, index)
+            dh[j] = placed([P, H], F32, f"dh{j}", offset)
+            nc.scalar.activation(dh[j][:], dh_ps[:], ACT.Copy, scale=half_gate[:, j : j + 1])
 
-        def quantise(j, interleaved, codes_offset=None):
-            slots = interleaved.shape[1] // PACK
-            codes[j] = placed([P, slots], U32, f"codes{j}", codes_offset)
-            da_plane[j] = keep.tile([P, slots], U8, name=f"da_plane{j}", align_bytes=MX_ALIGN)
-            nc.vector.quantize_mx(out=codes[j][:].bitcast(FP8X4), scales=da_plane[j][:], in_=interleaved)
+        def da_on_gpsimd(j, offset=None):
+            da[j] = placed([P, H], BF16, f"da{j}", offset)
+            nc.gpsimd.tensor_tensor(da[j][:], dh[j][:], slope[j][:], ALU.mult)
 
-        def make_dx(j, row_tiles, bank):
-            e = j // PER_EXPERT
-            slots = codes[j].shape[1]
-            dx_ps = banks.tile([P, len(row_tiles), slots], F32, name=f"dx_ps{j}_{row_tiles[0]}", offset=bank * BANK)
+        def interleave(e, index, offset=None):
+            turned = bank([P, PER_EXPERT, 2, P], f"turned{e}", index)
+            for c in range(PER_EXPERT):
+                pairs = da[PER_EXPERT * e + c][:].bitcast(F32)
+                for u in range(2):
+                    nc.tensor.transpose(turned[:, c, u, :], pairs[:, u : H // 2 : 2], ident[:])
+            interleaved = placed([P, PER_EXPERT * H], BF16, f"interleaved{e}", offset)
+            nc.scalar.copy(
+                interleaved[:].bitcast(F32).rearrange("p (c m u) -> p c m u", c=PER_EXPERT, u=2), turned[:].rearrange("p c u m -> p c m u")
+            )
+            return interleaved
+
+        def quantise(e, interleaved):
+            codes[e] = keep.tile([P, C], U32, name=f"codes{e}", align_bytes=MX_ALIGN)
+            da_plane[e] = keep.tile([P, C], U8, name=f"da_plane{e}", align_bytes=MX_ALIGN)
+            nc.vector.quantize_mx(out=codes[e][:].bitcast(FP8X4), scales=da_plane[e][:], in_=interleaved[:])
+
+        def make_dx(e, row_tiles, index, span=1):
+            dx_ps = bank([P, span * len(row_tiles), C], f"dx_ps{e}_{row_tiles[0]}", index)[:, 0 : len(row_tiles), :]
             for i, r in enumerate(row_tiles):
                 rows = slice(r * P, (r + 1) * P)
                 nc.tensor.matmul_mx(
                     dx_ps[:, i, :],
                     lhsT=w1t[e][:, rows].bitcast(FP8X4),
                     lhsT_scale=w1t_planes[QUAD_ROWS * e :, rows],
-                    rhs=codes[j][:].bitcast(FP8X4),
-                    rhs_scale=da_plane[j][:],
+                    rhs=codes[e][:].bitcast(FP8X4),
+                    rhs_scale=da_plane[e][:],
                     start=True,
                     stop=True,
                 )
-            staged = keep.tile([P, len(row_tiles), slots], F32, name=f"staged{j}_{row_tiles[0]}", align_bytes=MX_ALIGN)
-            nc.scalar.copy(staged[:], dx_ps[:])
-            return [(r, j, staged[:, i, :]) for i, r in enumerate(row_tiles)]
+            return dx_ps
 
-        def scatter(r, j, values):
-            nc.vector.tensor_copy(windows[r][:].indirect(listed(j * P, values.shape[1])), values)
+        def scatter_dx(e, row_tiles, dx_ps, offset=None):
+            staged = placed([P, len(row_tiles), C], F32, f"staged{e}_{row_tiles[0]}", offset)
+            nc.scalar.copy(staged[:], dx_ps)
+            for i, r in enumerate(row_tiles):
+                nc.vector.tensor_copy(windows[r][:].indirect(listed(e * C, C)), staged[:, i, :])
+                if e == E - 1:
+                    nc.sync.dma_start(out[r * P : (r + 1) * P, :], windows[r][:])
 
-        for j in range(PER_EXPERT):
-            interleaved = placed([P, H], BF16, f"interleaved{j}", HOST_INTERLEAVED_1 if j == 1 else None)
-            make_da(j, None, interleaved[:])
-            quantise(j, interleaved[:], HOST_CODES_0 if j == 0 else None)
-        gather(slot_dy[0], "slot_dy0", dyw[0], U32, (1,), below(HOST_DY[0], 4 * C))
-        gather(slot_dy[1], "slot_dy1", dyw[1], U32, (1,), above(HOST_DY[0], 4 * C))
-        gather(slot_dy[1], "slot_dy1", dyw[1], U32, (2, 3), above(HOST_DY[1], 4 * C))
-        gather(slot_dy[0], "slot_dy0", dyw[0], U32, (3,), below(HOST_DY[1], 4 * C))
-        ready = make_dx(0, range(ROW_TILES), 1)
-        gather(slot_dy[0], "slot_dy0", dyw[0], U32, (2,), above(HOST_CODES_0, 4 * P))
+        gather(slot_x_plane, "slot_x_plane", x_plane[:], U8, (0, 1))
+        gather(slot_x, "slot_x", xw, U32, (0, 1))
+        gather(slot_x, "slot_x", xw, U32, (2, 3))
+        gather(slot_x_plane, "slot_x_plane", x_plane[:], U8, (2, 3), XW + 4 * T - LAP)
+        for s in range(DY_PASSES):
+            gather(slot_dy[s], f"slot_dy{s}", dyw[s], U32, (0,))
+        gather(slot_dy_planes, "slot_dy_planes", dy_planes[:], U8, (0,))
+        gather(slot_dy_planes, "slot_dy_planes", dy_planes[:], U8, (1, 2, 3))
 
-        part_offsets = (below(HOST_INTERLEAVED_1, 4 * H), below(HOST_CODES_0, 4 * H))
-        for e in range(1, E):
-            first = PER_EXPERT * e
-            pair = placed([P, PER_EXPERT * H], BF16, f"pair{e}", HOST_PAIR[e])
-            for c in range(PER_EXPERT):
-                make_da(first + c, part_offsets[c], pair[:, c * H : (c + 1) * H])
-            held = make_dx(1, range(ROW_TILES), 1) if e == 1 else make_dx(first - PER_EXPERT, HIGH_ROWS, 1)
-            for r, j, values in ready:
-                scatter(r, j, values)
-            quantise(first, pair[:])
-            part_offsets = (below(HOST_PAIR[e], 4 * H), above(HOST_PAIR[e], 2 * PER_EXPERT * H))
-            ready = held + make_dx(first, LOW_ROWS, 2)
+        factors(0, False, host("right0"))
+        factors(1)
+        make_slope(1, host("slope1"))
+        factors(2, False)
+        factors(3, False, host("right3"))
+        factors(4)
+        factors(5)
+        da_on_both(0, 0)
+        da_on_vector(1, 1)
+        interleaved = interleave(0, 3, host("interleaved0"))
+        gather(slot_dy[0], "slot_dy0", dyw[0], U32, (1,), below("right0", 4 * C))
+        gather(slot_dy[1], "slot_dy1", dyw[1], U32, (1,), above("right0"))
+        gather(slot_dy[0], "slot_dy0", dyw[0], U32, (2, 3), above("slope1"))
+        quantise(0, interleaved)
+        make_slope(4)
+        low, high = make_dx(0, LOW_ROWS, 2, 2), make_dx(0, HIGH_ROWS, 5)
+        da_on_both(2, 0, None, above("interleaved0"))
+        da_on_both(3, 1, host("part3"), host("da3"))
+        make_slope(5, above("part3"))
+        gather(slot_dy[1], "slot_dy1", dyw[1], U32, (2, 3), above("right3"))
+        scatter_dx(0, LOW_ROWS, low, below("right3", ROOM))
+        factors(6)
+        interleaved = interleave(1, 2, host("interleaved1"))
+        scatter_dx(0, HIGH_ROWS, high, above("da3", 2 * H))
+        quantise(1, interleaved)
 
-        last_group = GROUPS - PER_EXPERT
-        for r, j, values in ready + make_dx(last_group, HIGH_ROWS, 0):
-            scatter(r, j, values)
-            if j == last_group:
-                nc.sync.dma_start(out[r * P : (r + 1) * P, :], windows[r][:])
+        stage_dh(4, 1)
+        stage_dh(5, 4, host("dh5"))
+        da_on_gpsimd(4, below("interleaved1", 2 * H))
+        da_on_gpsimd(5, host("da5"))
+        make_slope(6, above("dh5"))
+        low, high = make_dx(1, LOW_ROWS, 4, 2), make_dx(1, HIGH_ROWS, 1)
+        scatter_dx(1, LOW_ROWS, low)
+        factors(7)
+        interleaved = interleave(2, 4, host("interleaved2"))
+        scatter_dx(1, HIGH_ROWS, high, above("da5", 2 * H))
+        quantise(2, interleaved)
+
+        stage_dh(6, 4)
+        stage_dh(7, 1)
+        da_on_gpsimd(6, below("interleaved2", 2 * H))
+        make_slope(7, above("interleaved2"))
+        da_on_gpsimd(7, host("da7"))
+        low, high = make_dx(2, LOW_ROWS, 1), make_dx(2, HIGH_ROWS, 4)
+        scatter_dx(2, LOW_ROWS, low)
+        interleaved = interleave(3, 1)
+        scatter_dx(2, HIGH_ROWS, high, above("da7", 2 * H))
+        quantise(3, interleaved)
+        low, high = make_dx(3, LOW_ROWS, 0), make_dx(3, HIGH_ROWS, 6)
+        scatter_dx(3, LOW_ROWS, low)
+        scatter_dx(3, HIGH_ROWS, high)

@@ -34,7 +34,7 @@ KB = 1024
 A_BANKS = (0, 1, 2, 3, 4, 6, 3, 5)
 LAP = 64
 ROOM = 2 * KB
-HOSTS = ("right0", "slope1", "right3", "interleaved1", "interleaved2", "interleaved0", "part3", "da3", "da5", "da7", "dh5")
+HOSTS = ("slope0", "slope1", "right2", "interleaved1", "interleaved2", "interleaved0", "part3", "da3", "da5", "da7", "dh5")
 XW = 3 * len(HOSTS) * ROOM
 
 
@@ -260,27 +260,27 @@ def tile_moe_rec_mlp_silu_kernel(
         gather(slot_dy_planes, "slot_dy_planes", dy_planes[:], U8, (0,))
         gather(slot_dy_planes, "slot_dy_planes", dy_planes[:], U8, (1, 2, 3))
 
-        factors(0, False, host("right0"))
-        factors(1)
-        make_slope(1, host("slope1"))
-        factors(2, False)
-        factors(3, False, host("right3"))
-        factors(4)
-        factors(5)
-        da_on_both(0, 0)
+        for j in range(PER_EXPERT):
+            factors(j)
+            make_slope(j, host(f"slope{j}"))
+        factors(2, False, host("right2"))
+        factors(3, False)
+        da_on_vector(0, 0)
+        gather(slot_dy[1], "slot_dy1", dyw[1], U32, (1,), above("slope0"))
         da_on_vector(1, 1)
         interleaved = interleave(0, 3, host("interleaved0"))
-        gather(slot_dy[0], "slot_dy0", dyw[0], U32, (1,), below("right0", 4 * C))
-        gather(slot_dy[1], "slot_dy1", dyw[1], U32, (1,), above("right0"))
+        factors(4)
+        factors(5)
+        gather(slot_dy[0], "slot_dy0", dyw[0], U32, (1,), below("slope1", 4 * C))
         gather(slot_dy[0], "slot_dy0", dyw[0], U32, (2, 3), above("slope1"))
         quantise(0, interleaved)
-        make_slope(4)
-        low, high = make_dx(0, LOW_ROWS, 2, 2), make_dx(0, HIGH_ROWS, 5)
         da_on_both(2, 0, None, above("interleaved0"))
+        gather(slot_dy[1], "slot_dy1", dyw[1], U32, (2, 3), above("right2"))
         da_on_both(3, 1, host("part3"), host("da3"))
+        low, high = make_dx(0, LOW_ROWS, 2, 2), make_dx(0, HIGH_ROWS, 5)
+        scatter_dx(0, LOW_ROWS, low)
+        make_slope(4, below("part3", ROOM))
         make_slope(5, above("part3"))
-        gather(slot_dy[1], "slot_dy1", dyw[1], U32, (2, 3), above("right3"))
-        scatter_dx(0, LOW_ROWS, low, below("right3", ROOM))
         factors(6)
         interleaved = interleave(1, 2, host("interleaved1"))
         scatter_dx(0, HIGH_ROWS, high, above("da3", 2 * H))

@@ -147,7 +147,7 @@ def tile_moe_rec_mlp_silu_kernel(
         windows = [keep.tile([P, T], F32, name=f"window{r}") for r in range(ROW_TILES)]
         left, right, slope, dh, da, codes, da_plane = {}, {}, {}, {}, {}, {}, {}
 
-        def factors(j, ahead=True, offset=None):
+        def factors(j, offset=None):
             a_ps = bank([P, H], f"a_ps{j}", A_BANKS[j])
             e = j // PER_EXPERT
             nc.tensor.matmul_mx(
@@ -163,11 +163,11 @@ def tile_moe_rec_mlp_silu_kernel(
             nc.scalar.activation(left[j][:], a_ps[:], ACT.Silu, bias=no_bias[:], scale=-1.0)
             right[j] = placed([P, H], F32, f"right{j}", offset)
             nc.scalar.activation(right[j][:], a_ps[:], ACT.Tanh, scale=0.5)
-            if ahead:
-                nc.gpsimd.tensor_scalar(left[j][:], left[j][:], 1.0, -1.0, ALU.mult, ALU.add)
-            else:
-                g = half_gate[:, j : j + 1]
-                nc.gpsimd.tensor_scalar(left[j][:], left[j][:], -1.0, g, ALU.add, ALU.mult)
+
+        def gate_left(j, gated_offset=None):
+            silu_neg = left[j]
+            left[j] = placed([P, H], F32, f"gated{j}", gated_offset)
+            nc.gpsimd.tensor_scalar(left[j][:], silu_neg[:], -1.0, half_gate[:, j : j + 1], ALU.add, ALU.mult)
 
         def make_slope(j, offset=None):
             nc.scalar.activation(right[j][:], right[j][:], ACT.Copy, bias=1.0)
@@ -193,7 +193,7 @@ def tile_moe_rec_mlp_silu_kernel(
         def da_on_vector(j, index):
             dh_ps = make_dh(j, index)
             da[j] = keep.tile([P, H], BF16, name=f"da{j}")
-            nc.vector.scalar_tensor_tensor(da[j][:], dh_ps[:], half_gate[:, j : j + 1], slope[j][:], ALU.mult, ALU.mult)
+            nc.vector.tensor_tensor(da[j][:], slope[j][:], dh_ps[:], ALU.mult)
 
         def da_on_both(j, index, part_offset=None, da_offset=None):
             dh_ps = make_dh(j, index)
@@ -205,7 +205,7 @@ def tile_moe_rec_mlp_silu_kernel(
         def stage_dh(j, index, offset=None):
             dh_ps = make_dh(j, index)
             dh[j] = placed([P, H], F32, f"dh{j}", offset)
-            nc.scalar.activation(dh[j][:], dh_ps[:], ACT.Copy, scale=half_gate[:, j : j + 1])
+            nc.scalar.copy(dh[j][:], dh_ps[:])
 
         def da_on_gpsimd(j, offset=None):
             da[j] = placed([P, H], BF16, f"da{j}", offset)
@@ -262,45 +262,52 @@ def tile_moe_rec_mlp_silu_kernel(
 
         for j in range(PER_EXPERT):
             factors(j)
+            gate_left(j)
             make_slope(j, host(f"slope{j}"))
-        factors(2, False, host("right2"))
-        factors(3, False)
+        factors(2, host("right2"))
+        gate_left(2)
+        factors(3)
+        gate_left(3)
         da_on_vector(0, 0)
         gather(slot_dy[1], "slot_dy1", dyw[1], U32, (1,), above("slope0"))
         da_on_vector(1, 1)
         interleaved = interleave(0, 3, host("interleaved0"))
         factors(4)
+        gate_left(4)
         factors(5)
         gather(slot_dy[0], "slot_dy0", dyw[0], U32, (1,), below("slope1", 4 * C))
         gather(slot_dy[0], "slot_dy0", dyw[0], U32, (2, 3), above("slope1"))
         quantise(0, interleaved)
+        gate_left(5, below("interleaved0", ROOM))
         da_on_both(2, 0, None, above("interleaved0"))
         gather(slot_dy[1], "slot_dy1", dyw[1], U32, (2, 3), above("right2"))
         da_on_both(3, 1, host("part3"), host("da3"))
         low, high = make_dx(0, LOW_ROWS, 2, 2), make_dx(0, HIGH_ROWS, 5)
         scatter_dx(0, LOW_ROWS, low)
         make_slope(4, below("part3", ROOM))
-        make_slope(5, above("part3"))
         factors(6)
+        gate_left(6)
         interleaved = interleave(1, 2, host("interleaved1"))
         scatter_dx(0, HIGH_ROWS, high, above("da3", 2 * H))
         quantise(1, interleaved)
 
         stage_dh(4, 1)
         stage_dh(5, 4, host("dh5"))
-        da_on_gpsimd(4, below("interleaved1", 2 * H))
+        da_on_gpsimd(4, host("interleaved1") + ROOM // 4)
+        make_slope(5, above("interleaved1"))
         da_on_gpsimd(5, host("da5"))
         make_slope(6, above("dh5"))
         low, high = make_dx(1, LOW_ROWS, 4, 2), make_dx(1, HIGH_ROWS, 1)
         scatter_dx(1, LOW_ROWS, low)
         factors(7)
+        gate_left(7)
         interleaved = interleave(2, 4, host("interleaved2"))
         scatter_dx(1, HIGH_ROWS, high, above("da5", 2 * H))
         quantise(2, interleaved)
 
         stage_dh(6, 4)
         stage_dh(7, 1)
-        da_on_gpsimd(6, below("interleaved2", 2 * H))
+        da_on_gpsimd(6, host("interleaved2") + ROOM // 4)
         make_slope(7, above("interleaved2"))
         da_on_gpsimd(7, host("da7"))
         low, high = make_dx(2, LOW_ROWS, 1), make_dx(2, HIGH_ROWS, 4)

@@ -34,8 +34,7 @@ KB = 1024
 A_BANKS = (0, 1, 2, 3, 4, 6, 3, 5)
 LAP = 64
 ROOM = 2 * KB
-HOSTS = ("slope0", "slope1", "right2", "interleaved1", "interleaved2", "interleaved0", "part3", "da3", "da5", "da7", "dh5")
-XW = 3 * len(HOSTS) * ROOM
+HOSTS = ("gate_rows", "slot_dy0", "part3", "slot_dy1", "interleaved0", "interleaved1", "interleaved2", "da3", "da5", "da7", "dh5")
 
 
 def host(name):
@@ -75,11 +74,11 @@ def tile_moe_rec_mlp_silu_kernel(
             engine.memset(tile[:].bitcast(I32), 0)
             return tile
 
-        def load_planes(tile, planes):
+        def load_planes(tile, planes, engine=nc.sync):
             rows = planes.shape[0] * QUAD_ROWS
             for q in range(QUADS):
                 source = planes[:, QUAD_ROWS * q : QUAD_ROWS * (q + 1), :]
-                nc.sync.dma_start(tile[32 * q : 32 * q + rows, :].bitcast(I32), source.bitcast(I32))
+                engine.dma_start(tile[32 * q : 32 * q + rows, :].bitcast(I32), source.bitcast(I32))
 
         def load_pass(name, words, offset=None):
             tile = placed([P, words.shape[1]], I32, name, offset)
@@ -109,15 +108,15 @@ def tile_moe_rec_mlp_silu_kernel(
         for q in range(QUADS):
             source = x_scales[:, QUAD_ROWS * q : QUAD_ROWS * (q + 1), :].bitcast(I32)
             nc.sync.dma_start(x_plane[32 * q : 32 * (q + 1), :].bitcast(I32), source.to_broadcast([32 // QUAD_ROWS, QUAD_ROWS, T // 4]))
-        gate_rows = keep.tile([P, P], F32, name="gate_rows")
+        xw = load_pass("xw", x_words[0]).bitcast(U32)
+        gate_rows = placed([P, P], F32, "gate_rows", host("gate_rows"))
         nc.sync.dma_start(gate_rows[:], gate[0 : P * P // T, :].rearrange("a (c m) -> (a c) m", m=P))
-        xw = load_pass("xw", x_words[0], XW).bitcast(U32)
         w1 = load_passes("w1_01", w1_words[0:2, 0])
         load_planes(w1_planes, w1_scales[:, 0])
         dyw = [load_pass(f"dyw{s}", dy_words[s]).bitcast(U32) for s in range(DY_PASSES)]
         load_planes(dy_planes, dy_scales)
         w2 = load_passes("w2_0", w2t_words[0])
-        load_planes(w2_planes[0], w2_scale_rows[0:PLANES])
+        load_planes(w2_planes[0], w2_scale_rows[0:PLANES], nc.gpsimd)
         w1.extend(load_passes("w1_23", w1_words[2:4, 0]))
         w2.extend(load_passes("w2_1", w2t_words[1]))
         load_planes(w1t_planes, w1t_scales[:, 0])
@@ -254,34 +253,34 @@ def tile_moe_rec_mlp_silu_kernel(
         gather(slot_x_plane, "slot_x_plane", x_plane[:], U8, (0, 1))
         gather(slot_x, "slot_x", xw, U32, (0, 1))
         gather(slot_x, "slot_x", xw, U32, (2, 3))
-        gather(slot_x_plane, "slot_x_plane", x_plane[:], U8, (2, 3), XW + 4 * T - LAP)
+        gather(slot_x_plane, "slot_x_plane", x_plane[:], U8, (2, 3), above("gate_rows", 4 * P))
         for s in range(DY_PASSES):
-            gather(slot_dy[s], f"slot_dy{s}", dyw[s], U32, (0,))
+            gather(slot_dy[s], f"slot_dy{s}", dyw[s], U32, (0,), host(f"slot_dy{s}"))
         gather(slot_dy_planes, "slot_dy_planes", dy_planes[:], U8, (0,))
         gather(slot_dy_planes, "slot_dy_planes", dy_planes[:], U8, (1, 2, 3))
 
         for j in range(PER_EXPERT):
             factors(j)
             gate_left(j)
-            make_slope(j, host(f"slope{j}"))
-        factors(2, host("right2"))
+            make_slope(j)
+        factors(2)
         gate_left(2)
         factors(3)
         gate_left(3)
         da_on_vector(0, 0)
-        gather(slot_dy[1], "slot_dy1", dyw[1], U32, (1,), above("slope0"))
         da_on_vector(1, 1)
+        gather(slot_dy[1], "slot_dy1", dyw[1], U32, (1,), above("slot_dy0", 4 * C))
         interleaved = interleave(0, 3, host("interleaved0"))
         factors(4)
         gate_left(4)
         factors(5)
-        gather(slot_dy[0], "slot_dy0", dyw[0], U32, (1,), below("slope1", 4 * C))
-        gather(slot_dy[0], "slot_dy0", dyw[0], U32, (2, 3), above("slope1"))
+        gather(slot_dy[0], "slot_dy0", dyw[0], U32, (1,), below("slot_dy1", 4 * C))
+        gather(slot_dy[0], "slot_dy0", dyw[0], U32, (2, 3), above("slot_dy1", 4 * C))
         quantise(0, interleaved)
         gate_left(5, below("interleaved0", ROOM))
         da_on_both(2, 0, None, above("interleaved0"))
-        gather(slot_dy[1], "slot_dy1", dyw[1], U32, (2, 3), above("right2"))
         da_on_both(3, 1, host("part3"), host("da3"))
+        gather(slot_dy[1], "slot_dy1", dyw[1], U32, (2, 3), below("slot_dy1", 4 * C) + LAP - ROOM)
         low, high = make_dx(0, LOW_ROWS, 2, 2), make_dx(0, HIGH_ROWS, 5)
         scatter_dx(0, LOW_ROWS, low)
         make_slope(4, below("part3", ROOM))

@@ -32,9 +32,11 @@ BANK = 2048
 KB = 1024
 
 A_BANKS = (0, 1, 2, 3, 4, 6, 3, 5)
+GATE_BANK = 7
+
 LAP = 64
 ROOM = 2 * KB
-HOSTS = ("gate_rows", "slot_dy0", "part3", "slot_dy1", "interleaved0", "interleaved1", "interleaved2", "da3", "da5", "da7", "dh5")
+HOSTS = ("gate_rows", "slot_dy0", "part3", "slot_dy1", "interleaved0", "interleaved1", "interleaved2", "da3", "da5", "da7", "dh5", "part2")
 
 
 def host(name):
@@ -47,6 +49,10 @@ def below(name, size):
 
 def above(name, host_size=ROOM):
     return host(name) + host_size - LAP
+
+
+def inside(name):
+    return host(name) + ROOM // 4
 
 
 def tile_moe_rec_mlp_silu_kernel(
@@ -80,8 +86,8 @@ def tile_moe_rec_mlp_silu_kernel(
                 source = planes[:, QUAD_ROWS * q : QUAD_ROWS * (q + 1), :]
                 engine.dma_start(tile[32 * q : 32 * q + rows, :].bitcast(I32), source.bitcast(I32))
 
-        def load_pass(name, words, offset=None):
-            tile = placed([P, words.shape[1]], I32, name, offset)
+        def load_pass(name, words):
+            tile = keep.tile([P, words.shape[1]], I32, name=name, align_bytes=MX_ALIGN)
             nc.sync.dma_start(tile[:], words.rearrange("p c d -> p (c d)").bitcast(I32))
             return tile[:]
 
@@ -126,13 +132,13 @@ def tile_moe_rec_mlp_silu_kernel(
         w2.extend(load_passes("w2_3", w2t_words[3]))
         w1t.extend(load_passes("w1t_23", w1t_words[2:4, 0]))
 
-        def bank(shape, name, index):
-            return banks.tile(shape, F32, name=name, offset=index * BANK)
+        def bank(shape, name, bank_index):
+            return banks.tile(shape, F32, name=name, offset=bank_index * BANK)
 
-        gate_ps = bank([P, H], "gate_ps", 7)
+        gate_ps = bank([P, H], "gate_ps", GATE_BANK)
         nc.tensor.transpose(gate_ps[:, 0:P], gate_rows[:], ident[:])
-        half_gate = keep.tile([P, GROUPS], F32, name="half_gate")
-        nc.scalar.activation(half_gate[:], gate_ps[:, 0:GROUPS], ACT.Copy, scale=-0.5)
+        neg_half_gate = keep.tile([P, GROUPS], F32, name="neg_half_gate")
+        nc.scalar.activation(neg_half_gate[:], gate_ps[:, 0:GROUPS], ACT.Copy, scale=-0.5)
 
         slot_x_plane, slot_x, slot_dy_planes = {}, {}, {}
         slot_dy = [{} for s in range(DY_PASSES)]
@@ -144,9 +150,9 @@ def tile_moe_rec_mlp_silu_kernel(
                 into[experts[0] * PER_EXPERT + i] = tile[:, i * P : (i + 1) * P]
 
         windows = [keep.tile([P, T], F32, name=f"window{r}") for r in range(ROW_TILES)]
-        left, right, slope, dh, da, codes, da_plane = {}, {}, {}, {}, {}, {}, {}
+        silu_neg, tanh_half, gated, slope, dh, da, codes, da_plane = {}, {}, {}, {}, {}, {}, {}, {}
 
-        def factors(j, offset=None):
+        def make_factors(j):
             a_ps = bank([P, H], f"a_ps{j}", A_BANKS[j])
             e = j // PER_EXPERT
             nc.tensor.matmul_mx(
@@ -158,24 +164,24 @@ def tile_moe_rec_mlp_silu_kernel(
                 start=True,
                 stop=True,
             )
-            left[j] = keep.tile([P, H], F32, name=f"left{j}")
-            nc.scalar.activation(left[j][:], a_ps[:], ACT.Silu, bias=no_bias[:], scale=-1.0)
-            right[j] = placed([P, H], F32, f"right{j}", offset)
-            nc.scalar.activation(right[j][:], a_ps[:], ACT.Tanh, scale=0.5)
+            silu_neg[j] = keep.tile([P, H], F32, name=f"silu_neg{j}")
+            nc.scalar.activation(silu_neg[j][:], a_ps[:], ACT.Silu, bias=no_bias[:], scale=-1.0)
+            tanh_half[j] = placed([P, H], F32, f"tanh_half{j}", None)
+            nc.scalar.activation(tanh_half[j][:], a_ps[:], ACT.Tanh, scale=0.5)
 
-        def gate_left(j, gated_offset=None):
-            silu_neg = left[j]
-            left[j] = placed([P, H], F32, f"gated{j}", gated_offset)
-            nc.gpsimd.tensor_scalar(left[j][:], silu_neg[:], -1.0, half_gate[:, j : j + 1], ALU.add, ALU.mult)
+        def make_gated(j, offset=None):
+            gated[j] = placed([P, H], F32, f"gated{j}", offset)
+            nc.gpsimd.tensor_scalar(gated[j][:], silu_neg[j][:], -1.0, neg_half_gate[:, j : j + 1], ALU.add, ALU.mult)
 
         def make_slope(j, offset=None):
-            nc.scalar.activation(right[j][:], right[j][:], ACT.Copy, bias=1.0)
+            plus_one = tanh_half[j][:]
+            nc.scalar.activation(plus_one, tanh_half[j][:], ACT.Copy, bias=1.0)
             slope[j] = placed([P, H], F32, f"slope{j}", offset)
-            nc.gpsimd.tensor_tensor(slope[j][:], left[j][:], right[j][:], ALU.mult)
+            nc.gpsimd.tensor_tensor(slope[j][:], gated[j][:], plus_one, ALU.mult)
 
-        def make_dh(j, index):
+        def make_dh(j, bank_index):
             e = j // PER_EXPERT
-            dh_ps = bank([P, H], f"dh_ps{j}", index)
+            dh_ps = bank([P, H], f"dh_ps{j}", bank_index)
             for s in range(DY_PASSES):
                 n = DY_PASSES * e + s
                 nc.tensor.matmul_mx(
@@ -189,20 +195,20 @@ def tile_moe_rec_mlp_silu_kernel(
                 )
             return dh_ps
 
-        def da_on_vector(j, index):
-            dh_ps = make_dh(j, index)
+        def da_on_vector(j, bank_index):
+            dh_ps = make_dh(j, bank_index)
             da[j] = keep.tile([P, H], BF16, name=f"da{j}")
             nc.vector.tensor_tensor(da[j][:], slope[j][:], dh_ps[:], ALU.mult)
 
-        def da_on_both(j, index, part_offset=None, da_offset=None):
-            dh_ps = make_dh(j, index)
+        def da_on_both(j, bank_index, part_offset, da_offset):
+            dh_ps = make_dh(j, bank_index)
             part = placed([P, H], F32, f"part{j}", part_offset)
-            nc.vector.scalar_tensor_tensor(part[:], right[j][:], 1.0, dh_ps[:], ALU.add, ALU.mult)
+            nc.vector.scalar_tensor_tensor(part[:], tanh_half[j][:], 1.0, dh_ps[:], ALU.add, ALU.mult)
             da[j] = placed([P, H], BF16, f"da{j}", da_offset)
-            nc.gpsimd.tensor_tensor(da[j][:], left[j][:], part[:], ALU.mult)
+            nc.gpsimd.tensor_tensor(da[j][:], gated[j][:], part[:], ALU.mult)
 
-        def stage_dh(j, index, offset=None):
-            dh_ps = make_dh(j, index)
+        def stage_dh(j, bank_index, offset=None):
+            dh_ps = make_dh(j, bank_index)
             dh[j] = placed([P, H], F32, f"dh{j}", offset)
             nc.scalar.copy(dh[j][:], dh_ps[:])
 
@@ -210,8 +216,8 @@ def tile_moe_rec_mlp_silu_kernel(
             da[j] = placed([P, H], BF16, f"da{j}", offset)
             nc.gpsimd.tensor_tensor(da[j][:], dh[j][:], slope[j][:], ALU.mult)
 
-        def interleave(e, index, offset=None):
-            turned = bank([P, PER_EXPERT, 2, P], f"turned{e}", index)
+        def interleave(e, bank_index, offset=None):
+            turned = bank([P, PER_EXPERT, 2, P], f"turned{e}", bank_index)
             for c in range(PER_EXPERT):
                 pairs = da[PER_EXPERT * e + c][:].bitcast(F32)
                 for u in range(2):
@@ -227,8 +233,8 @@ def tile_moe_rec_mlp_silu_kernel(
             da_plane[e] = keep.tile([P, C], U8, name=f"da_plane{e}", align_bytes=MX_ALIGN)
             nc.vector.quantize_mx(out=codes[e][:].bitcast(FP8X4), scales=da_plane[e][:], in_=interleaved[:])
 
-        def make_dx(e, row_tiles, index, span=1):
-            dx_ps = bank([P, span * len(row_tiles), C], f"dx_ps{e}_{row_tiles[0]}", index)[:, 0 : len(row_tiles), :]
+        def make_dx(e, row_tiles, bank_index, span=1):
+            dx_ps = bank([P, span * len(row_tiles), C], f"dx_ps{e}_{row_tiles[0]}", bank_index)[:, 0 : len(row_tiles), :]
             for i, r in enumerate(row_tiles):
                 rows = slice(r * P, (r + 1) * P)
                 nc.tensor.matmul_mx(
@@ -259,54 +265,55 @@ def tile_moe_rec_mlp_silu_kernel(
         gather(slot_dy_planes, "slot_dy_planes", dy_planes[:], U8, (0,))
         gather(slot_dy_planes, "slot_dy_planes", dy_planes[:], U8, (1, 2, 3))
 
-        for j in range(PER_EXPERT):
-            factors(j)
-            gate_left(j)
+        for j in (0, 1):
+            make_factors(j)
+            make_gated(j)
             make_slope(j)
-        factors(2)
-        gate_left(2)
-        factors(3)
-        gate_left(3)
+        for j in (2, 3):
+            make_factors(j)
+            make_gated(j)
         da_on_vector(0, 0)
         da_on_vector(1, 1)
         gather(slot_dy[1], "slot_dy1", dyw[1], U32, (1,), above("slot_dy0", 4 * C))
         interleaved = interleave(0, 3, host("interleaved0"))
-        factors(4)
-        gate_left(4)
-        factors(5)
-        gather(slot_dy[0], "slot_dy0", dyw[0], U32, (1,), below("slot_dy1", 4 * C))
+        make_factors(4)
+        make_gated(4)
+        make_factors(5)
+        expert_1_words = below("slot_dy1", 4 * C)
+        gather(slot_dy[0], "slot_dy0", dyw[0], U32, (1,), expert_1_words)
         gather(slot_dy[0], "slot_dy0", dyw[0], U32, (2, 3), above("slot_dy1", 4 * C))
         quantise(0, interleaved)
-        gate_left(5, below("interleaved0", ROOM))
-        da_on_both(2, 0, None, above("interleaved0"))
+
+        da_on_both(2, 0, host("part2"), above("interleaved0"))
         da_on_both(3, 1, host("part3"), host("da3"))
-        gather(slot_dy[1], "slot_dy1", dyw[1], U32, (2, 3), below("slot_dy1", 4 * C) + LAP - ROOM)
-        low, high = make_dx(0, LOW_ROWS, 2, 2), make_dx(0, HIGH_ROWS, 5)
+        gather(slot_dy[1], "slot_dy1", dyw[1], U32, (2, 3), expert_1_words + LAP - ROOM)
+        low, high = make_dx(0, LOW_ROWS, 2, span=2), make_dx(0, HIGH_ROWS, 5)
         scatter_dx(0, LOW_ROWS, low)
         make_slope(4, below("part3", ROOM))
-        factors(6)
-        gate_left(6)
+        make_gated(5, above("part2"))
+        make_factors(6)
+        make_gated(6)
         interleaved = interleave(1, 2, host("interleaved1"))
         scatter_dx(0, HIGH_ROWS, high, above("da3", 2 * H))
         quantise(1, interleaved)
 
         stage_dh(4, 1)
         stage_dh(5, 4, host("dh5"))
-        da_on_gpsimd(4, host("interleaved1") + ROOM // 4)
+        da_on_gpsimd(4, inside("interleaved1"))
         make_slope(5, above("interleaved1"))
         da_on_gpsimd(5, host("da5"))
         make_slope(6, above("dh5"))
-        low, high = make_dx(1, LOW_ROWS, 4, 2), make_dx(1, HIGH_ROWS, 1)
+        low, high = make_dx(1, LOW_ROWS, 4, span=2), make_dx(1, HIGH_ROWS, 1)
         scatter_dx(1, LOW_ROWS, low)
-        factors(7)
-        gate_left(7)
+        make_factors(7)
+        make_gated(7)
         interleaved = interleave(2, 4, host("interleaved2"))
         scatter_dx(1, HIGH_ROWS, high, above("da5", 2 * H))
         quantise(2, interleaved)
 
         stage_dh(6, 4)
         stage_dh(7, 1)
-        da_on_gpsimd(6, host("interleaved2") + ROOM // 4)
+        da_on_gpsimd(6, inside("interleaved2"))
         make_slope(7, above("interleaved2"))
         da_on_gpsimd(7, host("da7"))
         low, high = make_dx(2, LOW_ROWS, 1), make_dx(2, HIGH_ROWS, 4)

@@ -31,12 +31,12 @@ MX_ALIGN = 64
 BANK = 2048
 KB = 1024
 
-A_BANKS = (0, 1, 2, 3, 4, 6, 3, 5)
+A_BANKS = (0, 1, 2, 3, 6, 4, 3, 5)
 GATE_BANK = 7
 
 LAP = 64
 ROOM = 2 * KB
-HOSTS = ("gate_rows", "slot_dy0", "part3", "slot_dy1", "interleaved0", "interleaved1", "interleaved2", "da3", "da5", "da7", "dh5", "part2")
+HOSTS = ("gate_rows", "slot_dy0", "part3", "slot_dy1", "interleaved0", "interleaved1", "interleaved2", "da3", "da5", "da7", "dh5", "part2", "tanh_half1")
 
 
 def host(name):
@@ -150,9 +150,10 @@ def tile_moe_rec_mlp_silu_kernel(
                 into[experts[0] * PER_EXPERT + i] = tile[:, i * P : (i + 1) * P]
 
         windows = [keep.tile([P, T], F32, name=f"window{r}") for r in range(ROW_TILES)]
-        silu_neg, tanh_half, gated, slope, dh, da, codes, da_plane = {}, {}, {}, {}, {}, {}, {}, {}
+        silu_neg, tanh_half, gated, plus_one, slope = {}, {}, {}, {}, {}
+        dh, da, codes, da_plane = {}, {}, {}, {}
 
-        def make_factors(j):
+        def make_factors(j, tanh_offset=None):
             a_ps = bank([P, H], f"a_ps{j}", A_BANKS[j])
             e = j // PER_EXPERT
             nc.tensor.matmul_mx(
@@ -166,18 +167,24 @@ def tile_moe_rec_mlp_silu_kernel(
             )
             silu_neg[j] = keep.tile([P, H], F32, name=f"silu_neg{j}")
             nc.scalar.activation(silu_neg[j][:], a_ps[:], ACT.Silu, bias=no_bias[:], scale=-1.0)
-            tanh_half[j] = placed([P, H], F32, f"tanh_half{j}", None)
+            tanh_half[j] = placed([P, H], F32, f"tanh_half{j}", tanh_offset)
             nc.scalar.activation(tanh_half[j][:], a_ps[:], ACT.Tanh, scale=0.5)
 
         def make_gated(j, offset=None):
             gated[j] = placed([P, H], F32, f"gated{j}", offset)
             nc.gpsimd.tensor_scalar(gated[j][:], silu_neg[j][:], -1.0, neg_half_gate[:, j : j + 1], ALU.add, ALU.mult)
 
+        def add_one_on_scalar(j, offset=None):
+            plus_one[j] = placed([P, H], F32, f"plus_one{j}", offset) if offset else tanh_half[j]
+            nc.scalar.activation(plus_one[j][:], tanh_half[j][:], ACT.Copy, bias=1.0)
+
+        def add_one_on_gpsimd(j):
+            plus_one[j] = placed([P, H], F32, f"plus_one{j}", None)
+            nc.gpsimd.tensor_scalar(plus_one[j][:], tanh_half[j][:], 1.0, 1.0, ALU.mult, ALU.add)
+
         def make_slope(j, offset=None):
-            plus_one = tanh_half[j][:]
-            nc.scalar.activation(plus_one, tanh_half[j][:], ACT.Copy, bias=1.0)
             slope[j] = placed([P, H], F32, f"slope{j}", offset)
-            nc.gpsimd.tensor_tensor(slope[j][:], gated[j][:], plus_one, ALU.mult)
+            nc.gpsimd.tensor_tensor(slope[j][:], gated[j][:], plus_one[j][:], ALU.mult)
 
         def make_dh(j, bank_index):
             e = j // PER_EXPERT
@@ -216,15 +223,15 @@ def tile_moe_rec_mlp_silu_kernel(
             da[j] = placed([P, H], BF16, f"da{j}", offset)
             nc.gpsimd.tensor_tensor(da[j][:], dh[j][:], slope[j][:], ALU.mult)
 
-        def interleave(e, bank_index, offset=None):
-            turned = bank([P, PER_EXPERT, 2, P], f"turned{e}", bank_index)
+        def interleave(e, bank_index, offset=None, span=1):
+            turned = bank([P, span * PER_EXPERT, 2, P], f"turned{e}", bank_index)[:, 0:PER_EXPERT]
             for c in range(PER_EXPERT):
                 pairs = da[PER_EXPERT * e + c][:].bitcast(F32)
                 for u in range(2):
                     nc.tensor.transpose(turned[:, c, u, :], pairs[:, u : H // 2 : 2], ident[:])
             interleaved = placed([P, PER_EXPERT * H], BF16, f"interleaved{e}", offset)
             nc.scalar.copy(
-                interleaved[:].bitcast(F32).rearrange("p (c m u) -> p c m u", c=PER_EXPERT, u=2), turned[:].rearrange("p c u m -> p c m u")
+                interleaved[:].bitcast(F32).rearrange("p (c m u) -> p c m u", c=PER_EXPERT, u=2), turned.rearrange("p c u m -> p c m u")
             )
             return interleaved
 
@@ -265,19 +272,21 @@ def tile_moe_rec_mlp_silu_kernel(
         gather(slot_dy_planes, "slot_dy_planes", dy_planes[:], U8, (0,))
         gather(slot_dy_planes, "slot_dy_planes", dy_planes[:], U8, (1, 2, 3))
 
-        for j in (0, 1):
-            make_factors(j)
+        for j, seat in ((0, None), (1, host("tanh_half1"))):
+            make_factors(j, seat)
             make_gated(j)
+            add_one_on_scalar(j)
             make_slope(j)
-        for j in (2, 3):
+        for j, seat in ((2, below("tanh_half1", ROOM)), (3, above("tanh_half1"))):
             make_factors(j)
-            make_gated(j)
+            make_gated(j, seat)
         da_on_vector(0, 0)
         da_on_vector(1, 1)
         gather(slot_dy[1], "slot_dy1", dyw[1], U32, (1,), above("slot_dy0", 4 * C))
-        interleaved = interleave(0, 3, host("interleaved0"))
+        interleaved = interleave(0, 3, host("interleaved0"), span=2)
         make_factors(4)
         make_gated(4)
+        add_one_on_gpsimd(4)
         make_factors(5)
         expert_1_words = below("slot_dy1", 4 * C)
         gather(slot_dy[0], "slot_dy0", dyw[0], U32, (1,), expert_1_words)
@@ -297,11 +306,13 @@ def tile_moe_rec_mlp_silu_kernel(
         scatter_dx(0, HIGH_ROWS, high, above("da3", 2 * H))
         quantise(1, interleaved)
 
-        stage_dh(4, 1)
-        stage_dh(5, 4, host("dh5"))
+        stage_dh(4, 4)
+        stage_dh(5, 1, host("dh5"))
         da_on_gpsimd(4, inside("interleaved1"))
+        add_one_on_scalar(5, above("interleaved0") + 2 * H - LAP)
         make_slope(5, above("interleaved1"))
         da_on_gpsimd(5, host("da5"))
+        add_one_on_scalar(6)
         make_slope(6, above("dh5"))
         low, high = make_dx(1, LOW_ROWS, 4, span=2), make_dx(1, HIGH_ROWS, 1)
         scatter_dx(1, LOW_ROWS, low)
@@ -314,11 +325,12 @@ def tile_moe_rec_mlp_silu_kernel(
         stage_dh(6, 4)
         stage_dh(7, 1)
         da_on_gpsimd(6, inside("interleaved2"))
+        add_one_on_scalar(7)
         make_slope(7, above("interleaved2"))
         da_on_gpsimd(7, host("da7"))
-        low, high = make_dx(2, LOW_ROWS, 1), make_dx(2, HIGH_ROWS, 4)
+        low, high = make_dx(2, LOW_ROWS, 4), make_dx(2, HIGH_ROWS, 1)
         scatter_dx(2, LOW_ROWS, low)
-        interleaved = interleave(3, 1)
+        interleaved = interleave(3, 4)
         scatter_dx(2, HIGH_ROWS, high, above("da7", 2 * H))
         quantise(3, interleaved)
         low, high = make_dx(3, LOW_ROWS, 0), make_dx(3, HIGH_ROWS, 6)

@@ -20,45 +20,56 @@ P = 128
 PACK = 4
 QUADS = 4
 QUAD_ROWS = 4
-PLANES = 4
 PER_EXPERT = C // P
 GROUPS = E * PER_EXPERT
 ROW_TILES = K // P
-LOW_ROWS, HIGH_ROWS = (0, 1), (2, 3)
+LOW_ROWS, HIGH_ROWS = (0, 2), (1, 3)
+VECTOR_ROWS = (0, 1)
 DY_PASSES = N // (P * PACK)
 STRIPE = 16
 MX_ALIGN = 64
 BANK = 2048
-KB = 1024
-
-A_BANKS = (0, 1, 2, 3, 6, 4, 3, 5)
-GATE_BANK = 7
-
 LAP = 64
-ROOM = 2 * KB
-HOSTS = ("gate_rows", "slot_dy0", "part3", "slot_dy1", "interleaved0", "interleaved1", "interleaved2", "da3", "da5", "da7", "dh5", "part2", "tanh_half1")
+
+WORDS, BYTES_, DA, WIDE, WINDOW = 4 * C, C, 2 * H, 4 * H, 4 * T
+CHAINS = (
+    (("gate_rows", 4 * P), ("slot_x_plane_2", 2 * C)),
+    (("slot_dy0_1", WORDS), ("slot_x_1", WORDS), ("slot_dy1_1", WORDS), ("slot_dy0_2", WORDS), ("codes1", WORDS), ("window0", WINDOW)),
+    (("slot_dy1_2", WORDS), ("interleaved0", WIDE), ("slot_dy1_3", WORDS)),
+    (("silu_neg7", WIDE), ("da1", DA), ("tanh_half7", WIDE)),
+    (("part6", WIDE), ("interleaved1", WIDE), ("part7", WIDE)),
+    (("interleaved2", WIDE), ("window1", WINDOW)),
+    (("da3", DA), ("window3", WINDOW)),
+    (("da5", DA), ("staged1_1", WIDE)),
+    (("da7", DA), ("staged2_0", WIDE)),
+    (("part3", WIDE), ("gated7", WIDE)),
+)
 
 
-def host(name):
-    return (3 * HOSTS.index(name) + 1) * ROOM
+def seat_offsets():
+    offsets, at = {}, 0
+    for chain in CHAINS:
+        for name, size in chain:
+            offsets[name] = at
+            at = at + size - LAP
+        at = at + LAP
+    offsets["slot_dy_planes_2"] = offsets["interleaved0"] + 2 * LAP
+    offsets["slot_dy_planes_3"] = offsets["slot_dy_planes_2"] + BYTES_
+    offsets["slot_dy0_3"] = offsets["slot_dy_planes_3"] + BYTES_
+    return offsets
 
 
-def below(name, size):
-    return host(name) + LAP - size
-
-
-def above(name, host_size=ROOM):
-    return host(name) + host_size - LAP
-
-
-def inside(name):
-    return host(name) + ROOM // 4
+A_BANKS = (0, 1, 2, 3, 0, 1, 2, 3)
+DH_BANKS = (4, 5, 6, 4, 5, 6, 4, 5)
+DX_BANKS = ((0, 1), (2, 3), (0, 1), (2, 3))
+TURN_BANK = 7
 
 
 def tile_moe_rec_mlp_silu_kernel(
     tc, x_words, x_scales, dy_words, dy_scales, w1_words, w1_scales, w2t_words, w2t_scales, w1t_words, w1t_scales, gate, offs, out
 ):
     nc = tc.nc
+    seat = seat_offsets()
     with ExitStack() as ctx:
         keep = ctx.enter_context(tc.tile_pool(name="keep", bufs=1))
         seats = ctx.enter_context(tc.tile_pool(name="seats", bufs=1))
@@ -70,10 +81,10 @@ def tile_moe_rec_mlp_silu_kernel(
         def listed(first_slot, count):
             return offsets[:, first_slot // STRIPE : (first_slot + count) // STRIPE]
 
-        def placed(shape, dtype, name, offset):
-            if offset is None:
-                return keep.tile(shape, dtype, name=name, align_bytes=MX_ALIGN)
-            return seats.tile(shape, dtype, name=name, offset=offset, align_bytes=MX_ALIGN)
+        def placed(shape, dtype, name):
+            if name in seat:
+                return seats.tile(shape, dtype, name=name, offset=seat[name], align_bytes=MX_ALIGN)
+            return keep.tile(shape, dtype, name=name, align_bytes=MX_ALIGN)
 
         def zeroed_planes(name, width, engine):
             tile = keep.tile([P, width], U8, name=name, align_bytes=MX_ALIGN)
@@ -98,9 +109,8 @@ def tile_moe_rec_mlp_silu_kernel(
 
         w1_planes = zeroed_planes("w1_planes", H, nc.gpsimd)
         dy_planes = zeroed_planes("dy_planes", T, nc.gpsimd)
-        w2_planes = [zeroed_planes(f"w2_planes{half}", H, nc.vector) for half in range(E * DY_PASSES // PLANES)]
+        w2_planes = zeroed_planes("w2_planes", E * DY_PASSES * H, nc.vector)
         w1t_planes = zeroed_planes("w1t_planes", K, nc.vector)
-        w2_scale_rows = w2t_scales.rearrange("e s b i -> (e s) b i")
 
         zero = keep.tile([P, 1], F32, name="zero")
         no_bias = keep.tile([P, 1], F32, name="no_bias")
@@ -115,19 +125,24 @@ def tile_moe_rec_mlp_silu_kernel(
             source = x_scales[:, QUAD_ROWS * q : QUAD_ROWS * (q + 1), :].bitcast(I32)
             nc.sync.dma_start(x_plane[32 * q : 32 * (q + 1), :].bitcast(I32), source.to_broadcast([32 // QUAD_ROWS, QUAD_ROWS, T // 4]))
         xw = load_pass("xw", x_words[0]).bitcast(U32)
-        gate_rows = placed([P, P], F32, "gate_rows", host("gate_rows"))
-        nc.sync.dma_start(gate_rows[:], gate[0 : P * P // T, :].rearrange("a (c m) -> (a c) m", m=P))
-        w1 = load_passes("w1_01", w1_words[0:2, 0])
+        w1 = [load_pass("w1_0", w1_words[0, 0])]
         load_planes(w1_planes, w1_scales[:, 0])
-        dyw = [load_pass(f"dyw{s}", dy_words[s]).bitcast(U32) for s in range(DY_PASSES)]
+        dyw = [words.bitcast(U32) for words in load_passes("dyw", dy_words)]
+        gate_rows = placed([P, P], F32, "gate_rows")
+        nc.sync.dma_start(gate_rows[:], gate[0 : P * P // T, :].rearrange("a (c m) -> (a c) m", m=P))
         load_planes(dy_planes, dy_scales)
+        w1.append(load_pass("w1_1", w1_words[1, 0]))
+        w1.append(load_pass("w1_2", w1_words[2, 0]))
         w2 = load_passes("w2_0", w2t_words[0])
-        load_planes(w2_planes[0], w2_scale_rows[0:PLANES], nc.gpsimd)
-        w1.extend(load_passes("w1_23", w1_words[2:4, 0]))
+        w2_scale_rows = w2t_scales.rearrange("e s (q r) i -> r q (e s) i", r=QUAD_ROWS)
+        for r in range(QUAD_ROWS):
+            nc.gpsimd.dma_start(
+                w2_planes[r:P:32, :].bitcast(I32).rearrange("q (j w) -> q j w", j=E * DY_PASSES), w2_scale_rows[r].bitcast(I32)
+            )
+        w1.append(load_pass("w1_3", w1_words[3, 0]))
         w2.extend(load_passes("w2_1", w2t_words[1]))
         load_planes(w1t_planes, w1t_scales[:, 0])
         w1t = load_passes("w1t_01", w1t_words[0:2, 0])
-        load_planes(w2_planes[1], w2_scale_rows[PLANES : 2 * PLANES])
         w2.extend(load_passes("w2_2", w2t_words[2]))
         w2.extend(load_passes("w2_3", w2t_words[3]))
         w1t.extend(load_passes("w1t_23", w1t_words[2:4, 0]))
@@ -135,7 +150,7 @@ def tile_moe_rec_mlp_silu_kernel(
         def bank(shape, name, bank_index):
             return banks.tile(shape, F32, name=name, offset=bank_index * BANK)
 
-        gate_ps = bank([P, H], "gate_ps", GATE_BANK)
+        gate_ps = bank([P, H], "gate_ps", TURN_BANK)
         nc.tensor.transpose(gate_ps[:, 0:P], gate_rows[:], ident[:])
         neg_half_gate = keep.tile([P, GROUPS], F32, name="neg_half_gate")
         nc.scalar.activation(neg_half_gate[:], gate_ps[:, 0:GROUPS], ACT.Copy, scale=-0.5)
@@ -143,17 +158,24 @@ def tile_moe_rec_mlp_silu_kernel(
         slot_x_plane, slot_x, slot_dy_planes = {}, {}, {}
         slot_dy = [{} for s in range(DY_PASSES)]
 
-        def gather(into, name, window, dtype, experts, offset=None):
-            tile = placed([P, len(experts) * C], dtype, f"{name}_{experts[0]}", offset)
+        def gather(into, name, window, dtype, experts):
+            tile = placed([P, len(experts) * C], dtype, f"{name}_{experts[0]}")
             nc.vector.tensor_copy(tile[:], window.indirect(listed(experts[0] * C, len(experts) * C)))
             for i in range(len(experts) * PER_EXPERT):
                 into[experts[0] * PER_EXPERT + i] = tile[:, i * P : (i + 1) * P]
 
-        windows = [keep.tile([P, T], F32, name=f"window{r}") for r in range(ROW_TILES)]
-        silu_neg, tanh_half, gated, plus_one, slope = {}, {}, {}, {}, {}
-        dh, da, codes, da_plane = {}, {}, {}, {}
+        def gather_dy_words(e):
+            for s in range(DY_PASSES):
+                gather(slot_dy[s], f"slot_dy{s}", dyw[s], U32, (e,))
 
-        def make_factors(j, tanh_offset=None):
+        def gather_dy_planes(e):
+            gather(slot_dy_planes, "slot_dy_planes", dy_planes[:], U8, (e,))
+
+        windows, staged = {}, {}
+        silu_neg, tanh_half, gated, slope = {}, {}, {}, {}
+        da, codes, da_plane = {}, {}, {}
+
+        def make_factors(j):
             a_ps = bank([P, H], f"a_ps{j}", A_BANKS[j])
             e = j // PER_EXPERT
             nc.tensor.matmul_mx(
@@ -165,83 +187,68 @@ def tile_moe_rec_mlp_silu_kernel(
                 start=True,
                 stop=True,
             )
-            silu_neg[j] = keep.tile([P, H], F32, name=f"silu_neg{j}")
+            silu_neg[j] = placed([P, H], F32, f"silu_neg{j}")
             nc.scalar.activation(silu_neg[j][:], a_ps[:], ACT.Silu, bias=no_bias[:], scale=-1.0)
-            tanh_half[j] = placed([P, H], F32, f"tanh_half{j}", tanh_offset)
+            tanh_half[j] = placed([P, H], F32, f"tanh_half{j}")
             nc.scalar.activation(tanh_half[j][:], a_ps[:], ACT.Tanh, scale=0.5)
 
-        def make_gated(j, offset=None):
-            gated[j] = placed([P, H], F32, f"gated{j}", offset)
+        def make_gated(j):
+            gated[j] = placed([P, H], F32, f"gated{j}")
             nc.gpsimd.tensor_scalar(gated[j][:], silu_neg[j][:], -1.0, neg_half_gate[:, j : j + 1], ALU.add, ALU.mult)
 
-        def add_one_on_scalar(j, offset=None):
-            plus_one[j] = placed([P, H], F32, f"plus_one{j}", offset) if offset else tanh_half[j]
-            nc.scalar.activation(plus_one[j][:], tanh_half[j][:], ACT.Copy, bias=1.0)
-
-        def add_one_on_gpsimd(j):
-            plus_one[j] = placed([P, H], F32, f"plus_one{j}", None)
-            nc.gpsimd.tensor_scalar(plus_one[j][:], tanh_half[j][:], 1.0, 1.0, ALU.mult, ALU.add)
-
-        def make_slope(j, offset=None):
-            slope[j] = placed([P, H], F32, f"slope{j}", offset)
-            nc.gpsimd.tensor_tensor(slope[j][:], gated[j][:], plus_one[j][:], ALU.mult)
-
-        def make_dh(j, bank_index):
+        def make_dh(j, span=1):
             e = j // PER_EXPERT
-            dh_ps = bank([P, H], f"dh_ps{j}", bank_index)
+            dh_ps = bank([P, span * H], f"dh_ps{j}", DH_BANKS[j])[:, 0:H]
             for s in range(DY_PASSES):
                 n = DY_PASSES * e + s
                 nc.tensor.matmul_mx(
-                    dh_ps[:],
+                    dh_ps,
                     lhsT=slot_dy[s][j].bitcast(FP8X4),
                     lhsT_scale=slot_dy_planes[j][QUAD_ROWS * s :, :],
                     rhs=w2[n].bitcast(FP8X4),
-                    rhs_scale=w2_planes[n // PLANES][QUAD_ROWS * (n % PLANES) :, :],
+                    rhs_scale=w2_planes[:, n * H : (n + 1) * H],
                     start=(s == 0),
                     stop=(s == DY_PASSES - 1),
                 )
             return dh_ps
 
-        def da_on_vector(j, bank_index):
-            dh_ps = make_dh(j, bank_index)
-            da[j] = keep.tile([P, H], BF16, name=f"da{j}")
-            nc.vector.tensor_tensor(da[j][:], slope[j][:], dh_ps[:], ALU.mult)
+        def da_twice_on_vector(j):
+            dh_ps = make_dh(j)
+            part = placed([P, H], F32, f"part{j}")
+            nc.vector.scalar_tensor_tensor(part[:], tanh_half[j][:], 1.0, dh_ps, ALU.add, ALU.mult)
+            da[j] = placed([P, H], BF16, f"da{j}")
+            nc.vector.tensor_tensor(da[j][:], gated[j][:], part[:], ALU.mult)
 
-        def da_on_both(j, bank_index, part_offset, da_offset):
-            dh_ps = make_dh(j, bank_index)
-            part = placed([P, H], F32, f"part{j}", part_offset)
-            nc.vector.scalar_tensor_tensor(part[:], tanh_half[j][:], 1.0, dh_ps[:], ALU.add, ALU.mult)
-            da[j] = placed([P, H], BF16, f"da{j}", da_offset)
+        def da_on_both(j):
+            da_from(j, make_dh(j))
+
+        def da_from(j, dh_ps):
+            part = placed([P, H], F32, f"part{j}")
+            nc.vector.scalar_tensor_tensor(part[:], tanh_half[j][:], 1.0, dh_ps, ALU.add, ALU.mult)
+            da[j] = placed([P, H], BF16, f"da{j}")
             nc.gpsimd.tensor_tensor(da[j][:], gated[j][:], part[:], ALU.mult)
 
-        def stage_dh(j, bank_index, offset=None):
-            dh_ps = make_dh(j, bank_index)
-            dh[j] = placed([P, H], F32, f"dh{j}", offset)
-            nc.scalar.copy(dh[j][:], dh_ps[:])
+        interleaved = {}
 
-        def da_on_gpsimd(j, offset=None):
-            da[j] = placed([P, H], BF16, f"da{j}", offset)
-            nc.gpsimd.tensor_tensor(da[j][:], dh[j][:], slope[j][:], ALU.mult)
-
-        def interleave(e, bank_index, offset=None, span=1):
-            turned = bank([P, span * PER_EXPERT, 2, P], f"turned{e}", bank_index)[:, 0:PER_EXPERT]
+        def interleave(e):
+            turned = bank([P, PER_EXPERT, 2, P], f"turned{e}", TURN_BANK)
             for c in range(PER_EXPERT):
                 pairs = da[PER_EXPERT * e + c][:].bitcast(F32)
                 for u in range(2):
                     nc.tensor.transpose(turned[:, c, u, :], pairs[:, u : H // 2 : 2], ident[:])
-            interleaved = placed([P, PER_EXPERT * H], BF16, f"interleaved{e}", offset)
+            interleaved[e] = placed([P, PER_EXPERT * H], BF16, f"interleaved{e}")
             nc.scalar.copy(
-                interleaved[:].bitcast(F32).rearrange("p (c m u) -> p c m u", c=PER_EXPERT, u=2), turned.rearrange("p c u m -> p c m u")
+                interleaved[e][:].bitcast(F32).rearrange("p (c m u) -> p c m u", c=PER_EXPERT, u=2), turned[:].rearrange("p c u m -> p c m u")
             )
-            return interleaved
 
-        def quantise(e, interleaved):
-            codes[e] = keep.tile([P, C], U32, name=f"codes{e}", align_bytes=MX_ALIGN)
-            da_plane[e] = keep.tile([P, C], U8, name=f"da_plane{e}", align_bytes=MX_ALIGN)
-            nc.vector.quantize_mx(out=codes[e][:].bitcast(FP8X4), scales=da_plane[e][:], in_=interleaved[:])
+        def quantise(e):
+            codes[e] = placed([P, C], U32, f"codes{e}")
+            da_plane[e] = placed([P, C], U8, f"da_plane{e}")
+            nc.vector.quantize_mx(out=codes[e][:].bitcast(FP8X4), scales=da_plane[e][:], in_=interleaved[e][:])
 
-        def make_dx(e, row_tiles, bank_index, span=1):
-            dx_ps = bank([P, span * len(row_tiles), C], f"dx_ps{e}_{row_tiles[0]}", bank_index)[:, 0 : len(row_tiles), :]
+        def make_dx(e, half):
+            row_tiles = (LOW_ROWS, HIGH_ROWS)[half]
+            dx_ps = bank([P, len(row_tiles), C], f"dx_ps{e}_{half}", DX_BANKS[e][half])
             for i, r in enumerate(row_tiles):
                 rows = slice(r * P, (r + 1) * P)
                 nc.tensor.matmul_mx(
@@ -255,84 +262,94 @@ def tile_moe_rec_mlp_silu_kernel(
                 )
             return dx_ps
 
-        def scatter_dx(e, row_tiles, dx_ps, offset=None):
-            staged = placed([P, len(row_tiles), C], F32, f"staged{e}_{row_tiles[0]}", offset)
-            nc.scalar.copy(staged[:], dx_ps)
+        def stage(e, half, dx_ps, on_vector=False):
+            row_tiles = (LOW_ROWS, HIGH_ROWS)[half]
+            tile = placed([P, len(row_tiles), C], F32, f"staged{e}_{row_tiles[0]}")
+            if on_vector:
+                nc.vector.tensor_copy(tile[:], dx_ps[:])
+            else:
+                nc.scalar.copy(tile[:], dx_ps[:])
             for i, r in enumerate(row_tiles):
-                nc.vector.tensor_copy(windows[r][:].indirect(listed(e * C, C)), staged[:, i, :])
-                if e == E - 1:
-                    nc.sync.dma_start(out[r * P : (r + 1) * P, :], windows[r][:])
+                staged[r, e] = tile[:, i, :]
+
+        done = {r: 0 for r in range(ROW_TILES)}
+
+        def scatter(r, e):
+            if r not in windows:
+                windows[r] = placed([P, T], F32, f"window{r}")
+            into = windows[r][:].indirect(listed(e * C, C))
+            if r in VECTOR_ROWS:
+                nc.vector.tensor_copy(into, staged[r, e])
+            else:
+                nc.scalar.activation(into, staged[r, e], ACT.Copy)
+            done[r] = done[r] + 1
+            if done[r] == E:
+                nc.sync.dma_start(out[r * P : (r + 1) * P, :], windows[r][:])
 
         gather(slot_x_plane, "slot_x_plane", x_plane[:], U8, (0, 1))
-        gather(slot_x, "slot_x", xw, U32, (0, 1))
+        gather(slot_x, "slot_x", xw, U32, (0,))
+        gather(slot_x, "slot_x", xw, U32, (1,))
         gather(slot_x, "slot_x", xw, U32, (2, 3))
-        gather(slot_x_plane, "slot_x_plane", x_plane[:], U8, (2, 3), above("gate_rows", 4 * P))
-        for s in range(DY_PASSES):
-            gather(slot_dy[s], f"slot_dy{s}", dyw[s], U32, (0,), host(f"slot_dy{s}"))
-        gather(slot_dy_planes, "slot_dy_planes", dy_planes[:], U8, (0,))
-        gather(slot_dy_planes, "slot_dy_planes", dy_planes[:], U8, (1, 2, 3))
-
-        for j, seat in ((0, None), (1, host("tanh_half1"))):
-            make_factors(j, seat)
-            make_gated(j)
-            add_one_on_scalar(j)
-            make_slope(j)
-        for j, seat in ((2, below("tanh_half1", ROOM)), (3, above("tanh_half1"))):
+        gather_dy_words(0)
+        gather(slot_x_plane, "slot_x_plane", x_plane[:], U8, (2, 3))
+        for j in range(7):
             make_factors(j)
-            make_gated(j, seat)
-        da_on_vector(0, 0)
-        da_on_vector(1, 1)
-        gather(slot_dy[1], "slot_dy1", dyw[1], U32, (1,), above("slot_dy0", 4 * C))
-        interleaved = interleave(0, 3, host("interleaved0"), span=2)
-        make_factors(4)
-        make_gated(4)
-        add_one_on_gpsimd(4)
-        make_factors(5)
-        expert_1_words = below("slot_dy1", 4 * C)
-        gather(slot_dy[0], "slot_dy0", dyw[0], U32, (1,), expert_1_words)
-        gather(slot_dy[0], "slot_dy0", dyw[0], U32, (2, 3), above("slot_dy1", 4 * C))
-        quantise(0, interleaved)
+            make_gated(j)
 
-        da_on_both(2, 0, host("part2"), above("interleaved0"))
-        da_on_both(3, 1, host("part3"), host("da3"))
-        gather(slot_dy[1], "slot_dy1", dyw[1], U32, (2, 3), expert_1_words + LAP - ROOM)
-        low, high = make_dx(0, LOW_ROWS, 2, span=2), make_dx(0, HIGH_ROWS, 5)
-        scatter_dx(0, LOW_ROWS, low)
-        make_slope(4, below("part3", ROOM))
-        make_gated(5, above("part2"))
-        make_factors(6)
-        make_gated(6)
-        interleaved = interleave(1, 2, host("interleaved1"))
-        scatter_dx(0, HIGH_ROWS, high, above("da3", 2 * H))
-        quantise(1, interleaved)
-
-        stage_dh(4, 4)
-        stage_dh(5, 1, host("dh5"))
-        da_on_gpsimd(4, inside("interleaved1"))
-        add_one_on_scalar(5, above("interleaved0") + 2 * H - LAP)
-        make_slope(5, above("interleaved1"))
-        da_on_gpsimd(5, host("da5"))
-        add_one_on_scalar(6)
-        make_slope(6, above("dh5"))
-        low, high = make_dx(1, LOW_ROWS, 4, span=2), make_dx(1, HIGH_ROWS, 1)
-        scatter_dx(1, LOW_ROWS, low)
+        gather_dy_planes(0)
+        gather_dy_planes(1)
+        gather_dy_words(1)
+        da_twice_on_vector(0)
+        da_twice_on_vector(1)
+        da_on_both(2)
+        dh_ps = make_dh(3)
+        gather(slot_dy[0], "slot_dy0", dyw[0], U32, (2,))
+        da_from(3, dh_ps)
+        interleave(0)
         make_factors(7)
         make_gated(7)
-        interleaved = interleave(2, 4, host("interleaved2"))
-        scatter_dx(1, HIGH_ROWS, high, above("da5", 2 * H))
-        quantise(2, interleaved)
+        quantise(0)
+        gather_dy_planes(2)
+        gather(slot_dy[1], "slot_dy1", dyw[1], U32, (2,))
+        gather_dy_planes(3)
+        gather_dy_words(3)
+        low, high = make_dx(0, 0), make_dx(0, 1)
+        stage(0, 0, low)
+        stage(0, 1, high)
+        scatter(2, 0)
 
-        stage_dh(6, 4)
-        stage_dh(7, 1)
-        da_on_gpsimd(6, inside("interleaved2"))
-        add_one_on_scalar(7)
-        make_slope(7, above("interleaved2"))
-        da_on_gpsimd(7, host("da7"))
-        low, high = make_dx(2, LOW_ROWS, 4), make_dx(2, HIGH_ROWS, 1)
-        scatter_dx(2, LOW_ROWS, low)
-        interleaved = interleave(3, 4)
-        scatter_dx(2, HIGH_ROWS, high, above("da7", 2 * H))
-        quantise(3, interleaved)
-        low, high = make_dx(3, LOW_ROWS, 0), make_dx(3, HIGH_ROWS, 6)
-        scatter_dx(3, LOW_ROWS, low)
-        scatter_dx(3, HIGH_ROWS, high)
+        da_on_both(4)
+        da_on_both(5)
+        interleave(1)
+        scatter(3, 0)
+        quantise(1)
+        da_on_both(6)
+        da_on_both(7)
+        low, high = make_dx(1, 0), make_dx(1, 1)
+        stage(1, 0, low)
+        scatter(0, 0)
+        scatter(0, 1)
+        scatter(2, 1)
+
+        interleave(2)
+        stage(1, 1, high)
+        scatter(3, 1)
+        quantise(2)
+        scatter(1, 0)
+        scatter(1, 1)
+        low, high = make_dx(2, 0), make_dx(2, 1)
+        stage(2, 1, high)
+
+        interleave(3)
+        stage(2, 0, low)
+        quantise(3)
+        scatter(0, 2)
+        scatter(2, 2)
+        low, high = make_dx(3, 0), make_dx(3, 1)
+        stage(3, 0, low)
+        stage(3, 1, high)
+        scatter(0, 3)
+        scatter(2, 3)
+        for e in (3, 2):
+            scatter(1, e)
+            scatter(3, e)

@@ -24,7 +24,6 @@ PER_EXPERT = C // P
 GROUPS = E * PER_EXPERT
 ROW_TILES = K // P
 LOW_ROWS, HIGH_ROWS = (0, 2), (1, 3)
-VECTOR_ROWS = (0, 1)
 DY_PASSES = N // (P * PACK)
 STRIPE = 16
 MX_ALIGN = 64
@@ -34,15 +33,15 @@ LAP = 64
 WORDS, BYTES_, DA, WIDE, WINDOW = 4 * C, C, 2 * H, 4 * H, 4 * T
 CHAINS = (
     (("gate_rows", 4 * P), ("slot_x_plane_2", 2 * C)),
-    (("slot_dy0_1", WORDS), ("slot_x_1", WORDS), ("slot_dy1_1", WORDS), ("slot_dy0_2", WORDS), ("codes1", WORDS), ("window0", WINDOW)),
-    (("slot_dy1_2", WORDS), ("interleaved0", WIDE), ("slot_dy1_3", WORDS)),
+    (("slot_dy0_1", WORDS), ("slot_x_1", WORDS), ("slot_dy1_1", WORDS), ("slot_dy0_2", WORDS)),
+    (("slot_dy1_2", WORDS), ("interleaved0", WIDE)),
     (("silu_neg7", WIDE), ("da1", DA), ("tanh_half7", WIDE)),
     (("part6", WIDE), ("interleaved1", WIDE), ("part7", WIDE)),
-    (("interleaved2", WIDE), ("window1", WINDOW)),
-    (("da3", DA), ("window3", WINDOW)),
-    (("da5", DA), ("staged1_1", WIDE)),
-    (("da7", DA), ("staged2_0", WIDE)),
+    (("tanh_half4", WIDE), ("slot_dy1_3", WORDS)),
+    (("window0", WINDOW), ("da5", DA), ("window1", WINDOW)),
+    (("da7", DA), ("codes2", WORDS)),
     (("part3", WIDE), ("gated7", WIDE)),
+    (("tanh_half1", WIDE), ("da0", DA)),
 )
 
 
@@ -60,9 +59,10 @@ def seat_offsets():
 
 
 A_BANKS = (0, 1, 2, 3, 0, 1, 2, 3)
-DH_BANKS = (4, 5, 6, 4, 5, 6, 4, 5)
+DH_BANKS = (4, 5, 6, 4, 5, 6, 4, 0)
 DX_BANKS = ((0, 1), (2, 3), (0, 1), (2, 3))
-TURN_BANK = 7
+TURN_BANKS = (7, 5, 7, 4)
+GATE_BANK = 7
 
 
 def tile_moe_rec_mlp_silu_kernel(
@@ -107,9 +107,9 @@ def tile_moe_rec_mlp_silu_kernel(
             nc.sync.dma_start(tile[:], words.rearrange("j p c d -> p j (c d)").bitcast(I32))
             return [tile[:, j, :] for j in range(words.shape[0])]
 
-        w1_planes = zeroed_planes("w1_planes", H, nc.gpsimd)
-        dy_planes = zeroed_planes("dy_planes", T, nc.gpsimd)
         w2_planes = zeroed_planes("w2_planes", E * DY_PASSES * H, nc.vector)
+        w1_planes = zeroed_planes("w1_planes", H, nc.vector)
+        dy_planes = zeroed_planes("dy_planes", T, nc.vector)
         w1t_planes = zeroed_planes("w1t_planes", K, nc.vector)
 
         zero = keep.tile([P, 1], F32, name="zero")
@@ -127,9 +127,9 @@ def tile_moe_rec_mlp_silu_kernel(
         xw = load_pass("xw", x_words[0]).bitcast(U32)
         w1 = [load_pass("w1_0", w1_words[0, 0])]
         load_planes(w1_planes, w1_scales[:, 0])
-        dyw = [words.bitcast(U32) for words in load_passes("dyw", dy_words)]
         gate_rows = placed([P, P], F32, "gate_rows")
         nc.sync.dma_start(gate_rows[:], gate[0 : P * P // T, :].rearrange("a (c m) -> (a c) m", m=P))
+        dyw = [words.bitcast(U32) for words in load_passes("dyw", dy_words)]
         load_planes(dy_planes, dy_scales)
         w1.append(load_pass("w1_1", w1_words[1, 0]))
         w1.append(load_pass("w1_2", w1_words[2, 0]))
@@ -150,7 +150,7 @@ def tile_moe_rec_mlp_silu_kernel(
         def bank(shape, name, bank_index):
             return banks.tile(shape, F32, name=name, offset=bank_index * BANK)
 
-        gate_ps = bank([P, H], "gate_ps", TURN_BANK)
+        gate_ps = bank([P, H], "gate_ps", GATE_BANK)
         nc.tensor.transpose(gate_ps[:, 0:P], gate_rows[:], ident[:])
         neg_half_gate = keep.tile([P, GROUPS], F32, name="neg_half_gate")
         nc.scalar.activation(neg_half_gate[:], gate_ps[:, 0:GROUPS], ACT.Copy, scale=-0.5)
@@ -171,7 +171,7 @@ def tile_moe_rec_mlp_silu_kernel(
         def gather_dy_planes(e):
             gather(slot_dy_planes, "slot_dy_planes", dy_planes[:], U8, (e,))
 
-        windows, staged = {}, {}
+        windows = {}
         silu_neg, tanh_half, gated, slope = {}, {}, {}, {}
         da, codes, da_plane = {}, {}, {}
 
@@ -212,12 +212,14 @@ def tile_moe_rec_mlp_silu_kernel(
                 )
             return dh_ps
 
-        def da_twice_on_vector(j):
-            dh_ps = make_dh(j)
-            part = placed([P, H], F32, f"part{j}")
-            nc.vector.scalar_tensor_tensor(part[:], tanh_half[j][:], 1.0, dh_ps, ALU.add, ALU.mult)
-            da[j] = placed([P, H], BF16, f"da{j}")
-            nc.vector.tensor_tensor(da[j][:], gated[j][:], part[:], ALU.mult)
+        def first_expert_on_vector():
+            parts = []
+            for j in range(PER_EXPERT):
+                parts.append(placed([P, H], F32, f"part{j}"))
+                nc.vector.scalar_tensor_tensor(parts[j][:], tanh_half[j][:], 1.0, make_dh(j), ALU.add, ALU.mult)
+            for j in range(PER_EXPERT):
+                da[j] = placed([P, H], BF16, f"da{j}")
+                nc.vector.tensor_tensor(da[j][:], gated[j][:], parts[j][:], ALU.mult)
 
         def da_on_both(j):
             da_from(j, make_dh(j))
@@ -230,68 +232,74 @@ def tile_moe_rec_mlp_silu_kernel(
 
         interleaved = {}
 
-        def interleave(e):
-            turned = bank([P, PER_EXPERT, 2, P], f"turned{e}", TURN_BANK)
+        def turn(e):
+            turned = bank([P, PER_EXPERT, 2, P], f"turned{e}", TURN_BANKS[e])
             for c in range(PER_EXPERT):
                 pairs = da[PER_EXPERT * e + c][:].bitcast(F32)
                 for u in range(2):
                     nc.tensor.transpose(turned[:, c, u, :], pairs[:, u : H // 2 : 2], ident[:])
+            return turned
+
+        def weave(e, turned, copy):
             interleaved[e] = placed([P, PER_EXPERT * H], BF16, f"interleaved{e}")
-            nc.scalar.copy(
+            copy(
                 interleaved[e][:].bitcast(F32).rearrange("p (c m u) -> p c m u", c=PER_EXPERT, u=2), turned[:].rearrange("p c u m -> p c m u")
             )
+
+        def interleave(e, copy):
+            weave(e, turn(e), copy)
 
         def quantise(e):
             codes[e] = placed([P, C], U32, f"codes{e}")
             da_plane[e] = placed([P, C], U8, f"da_plane{e}")
             nc.vector.quantize_mx(out=codes[e][:].bitcast(FP8X4), scales=da_plane[e][:], in_=interleaved[e][:])
 
+        def dx_rows(e, r, dx_ps):
+            rows = slice(r * P, (r + 1) * P)
+            nc.tensor.matmul_mx(
+                dx_ps,
+                lhsT=w1t[e][:, rows].bitcast(FP8X4),
+                lhsT_scale=w1t_planes[QUAD_ROWS * e :, rows],
+                rhs=codes[e][:].bitcast(FP8X4),
+                rhs_scale=da_plane[e][:],
+                start=True,
+                stop=True,
+            )
+
         def make_dx(e, half):
             row_tiles = (LOW_ROWS, HIGH_ROWS)[half]
             dx_ps = bank([P, len(row_tiles), C], f"dx_ps{e}_{half}", DX_BANKS[e][half])
             for i, r in enumerate(row_tiles):
-                rows = slice(r * P, (r + 1) * P)
-                nc.tensor.matmul_mx(
-                    dx_ps[:, i, :],
-                    lhsT=w1t[e][:, rows].bitcast(FP8X4),
-                    lhsT_scale=w1t_planes[QUAD_ROWS * e :, rows],
-                    rhs=codes[e][:].bitcast(FP8X4),
-                    rhs_scale=da_plane[e][:],
-                    start=True,
-                    stop=True,
-                )
+                dx_rows(e, r, dx_ps[:, i, :])
             return dx_ps
 
-        def stage(e, half, dx_ps, on_vector=False):
-            row_tiles = (LOW_ROWS, HIGH_ROWS)[half]
-            tile = placed([P, len(row_tiles), C], F32, f"staged{e}_{row_tiles[0]}")
-            if on_vector:
-                nc.vector.tensor_copy(tile[:], dx_ps[:])
-            else:
-                nc.scalar.copy(tile[:], dx_ps[:])
-            for i, r in enumerate(row_tiles):
-                staged[r, e] = tile[:, i, :]
+        staged = [keep.tile([P, len(LOW_ROWS), T], F32, name=f"staged{half}") for half in range(2)]
 
-        done = {r: 0 for r in range(ROW_TILES)}
+        def stage(e, half, dx_ps, copy):
+            copy(staged[half][:, :, e * C : (e + 1) * C], dx_ps[:])
 
-        def scatter(r, e):
+        def scatter(r, experts, engine):
             if r not in windows:
                 windows[r] = placed([P, T], F32, f"window{r}")
-            into = windows[r][:].indirect(listed(e * C, C))
-            if r in VECTOR_ROWS:
-                nc.vector.tensor_copy(into, staged[r, e])
+            first, count = experts[0] * C, len(experts) * C
+            into = windows[r][:].indirect(listed(first, count))
+            source = staged[r % 2][:, r // 2, first : first + count]
+            if engine == "vector":
+                nc.vector.tensor_copy(into, source)
             else:
-                nc.scalar.activation(into, staged[r, e], ACT.Copy)
-            done[r] = done[r] + 1
-            if done[r] == E:
-                nc.sync.dma_start(out[r * P : (r + 1) * P, :], windows[r][:])
+                nc.scalar.activation(into, source, ACT.Copy)
+
+        def store(r, engine):
+            engine.dma_start(out[r * P : (r + 1) * P, :], windows[r][:])
+
+        on_scalar, on_vector = nc.scalar.copy, nc.vector.tensor_copy
 
         gather(slot_x_plane, "slot_x_plane", x_plane[:], U8, (0, 1))
         gather(slot_x, "slot_x", xw, U32, (0,))
         gather(slot_x, "slot_x", xw, U32, (1,))
         gather(slot_x, "slot_x", xw, U32, (2, 3))
-        gather_dy_words(0)
         gather(slot_x_plane, "slot_x_plane", x_plane[:], U8, (2, 3))
+        gather_dy_words(0)
         for j in range(7):
             make_factors(j)
             make_gated(j)
@@ -299,57 +307,65 @@ def tile_moe_rec_mlp_silu_kernel(
         gather_dy_planes(0)
         gather_dy_planes(1)
         gather_dy_words(1)
-        da_twice_on_vector(0)
-        da_twice_on_vector(1)
+        first_expert_on_vector()
         da_on_both(2)
         dh_ps = make_dh(3)
         gather(slot_dy[0], "slot_dy0", dyw[0], U32, (2,))
         da_from(3, dh_ps)
-        interleave(0)
+        interleave(0, on_scalar)
         make_factors(7)
         make_gated(7)
         quantise(0)
         gather_dy_planes(2)
         gather(slot_dy[1], "slot_dy1", dyw[1], U32, (2,))
         gather_dy_planes(3)
-        gather_dy_words(3)
+        gather(slot_dy[0], "slot_dy0", dyw[0], U32, (3,))
         low, high = make_dx(0, 0), make_dx(0, 1)
-        stage(0, 0, low)
-        stage(0, 1, high)
-        scatter(2, 0)
+        stage(0, 0, low, on_scalar)
+        stage(0, 1, high, on_scalar)
+        scatter(2, (0,), "scalar")
+        scatter(3, (0,), "scalar")
 
         da_on_both(4)
+        gather(slot_dy[1], "slot_dy1", dyw[1], U32, (3,))
+        turned = turn(1)
         da_on_both(5)
-        interleave(1)
-        scatter(3, 0)
+        weave(1, turned, on_vector)
         quantise(1)
         da_on_both(6)
         da_on_both(7)
         low, high = make_dx(1, 0), make_dx(1, 1)
-        stage(1, 0, low)
-        scatter(0, 0)
-        scatter(0, 1)
-        scatter(2, 1)
+        stage(1, 0, low, on_scalar)
+        stage(1, 1, high, on_scalar)
+        scatter(2, (1,), "scalar")
+        scatter(3, (1,), "scalar")
+        turned = turn(2)
+        scatter(0, (0,), "vector")
+        weave(2, turned, on_vector)
+        scatter(1, (0,), "vector")
+        scatter(1, (1,), "scalar")
 
-        interleave(2)
-        stage(1, 1, high)
-        scatter(3, 1)
+        turned = turn(3)
         quantise(2)
-        scatter(1, 0)
-        scatter(1, 1)
-        low, high = make_dx(2, 0), make_dx(2, 1)
-        stage(2, 1, high)
-
-        interleave(3)
-        stage(2, 0, low)
+        weave(3, turned, on_vector)
+        stage(2, 0, make_dx(2, 0), on_vector)
         quantise(3)
-        scatter(0, 2)
-        scatter(2, 2)
-        low, high = make_dx(3, 0), make_dx(3, 1)
-        stage(3, 0, low)
-        stage(3, 1, high)
-        scatter(0, 3)
-        scatter(2, 3)
-        for e in (3, 2):
-            scatter(1, e)
-            scatter(3, e)
+        late = {r: bank([P, 2 * C], f"dx_late{r}", DX_BANKS[e][1]) for e, r in ((2, 3), (3, 1))}
+        for r in late:
+            dx_rows(2, r, late[r][:, 0:C])
+        scatter(0, (1, 2), "vector")
+        scatter(2, (2,), "scalar")
+        stage(3, 0, make_dx(3, 0), on_scalar)
+        for r in late:
+            dx_rows(3, r, late[r][:, C : 2 * C])
+        nc.scalar.copy(staged[1][:, 1, 2 * C : 4 * C], late[3][:])
+        scatter(0, (3,), "vector")
+        store(0, nc.sync)
+        scatter(2, (3,), "scalar")
+        store(2, nc.sync)
+        nc.scalar.copy(staged[1][:, 0, 2 * C : 4 * C], late[1][:])
+        scatter(1, (2, 3), "vector")
+        store(1, nc.sync)
+        scatter(3, (2,), "scalar")
+        scatter(3, (3,), "scalar")
+        store(3, nc.sync)

@@ -33,15 +33,14 @@ LAP = 64
 WORDS, BYTES_, DA, WIDE, WINDOW = 4 * C, C, 2 * H, 4 * H, 4 * T
 CHAINS = (
     (("gate_rows", 4 * P), ("slot_x_plane_2", 2 * C)),
-    (("slot_dy0_1", WORDS), ("slot_x_1", WORDS), ("slot_dy1_1", WORDS), ("slot_dy0_2", WORDS)),
+    (("slot_dy0_1", WORDS), ("slot_x_1", WORDS), ("slot_dy1_1", WORDS)),
+    (("tanh_half2", WIDE), ("slot_dy0_2", WORDS)),
     (("slot_dy1_2", WORDS), ("interleaved0", WIDE)),
-    (("silu_neg7", WIDE), ("da1", DA), ("tanh_half7", WIDE)),
+    (("silu_neg7", WIDE), ("da1", DA), ("tanh_half7", WIDE), ("window0", WINDOW)),
     (("part6", WIDE), ("interleaved1", WIDE), ("part7", WIDE)),
     (("tanh_half4", WIDE), ("slot_dy1_3", WORDS)),
-    (("window0", WINDOW), ("da5", DA), ("window1", WINDOW)),
     (("da7", DA), ("codes2", WORDS)),
     (("part3", WIDE), ("gated7", WIDE)),
-    (("tanh_half1", WIDE), ("da0", DA)),
 )
 
 
@@ -154,6 +153,8 @@ def tile_moe_rec_mlp_silu_kernel(
         nc.tensor.transpose(gate_ps[:, 0:P], gate_rows[:], ident[:])
         neg_half_gate = keep.tile([P, GROUPS], F32, name="neg_half_gate")
         nc.scalar.activation(neg_half_gate[:], gate_ps[:, 0:GROUPS], ACT.Copy, scale=-0.5)
+        half_gate = keep.tile([P, PER_EXPERT], F32, name="half_gate")
+        nc.scalar.activation(half_gate[:], gate_ps[:, 0:PER_EXPERT], ACT.Copy, scale=0.5)
 
         slot_x_plane, slot_x, slot_dy_planes = {}, {}, {}
         slot_dy = [{} for s in range(DY_PASSES)]
@@ -194,7 +195,10 @@ def tile_moe_rec_mlp_silu_kernel(
 
         def make_gated(j):
             gated[j] = placed([P, H], F32, f"gated{j}")
-            nc.gpsimd.tensor_scalar(gated[j][:], silu_neg[j][:], -1.0, neg_half_gate[:, j : j + 1], ALU.add, ALU.mult)
+            if j < PER_EXPERT:
+                nc.scalar.activation(gated[j][:], silu_neg[j][:], ACT.Identity, bias=half_gate[:, j : j + 1], scale=neg_half_gate[:, j : j + 1])
+            else:
+                nc.gpsimd.tensor_scalar(gated[j][:], silu_neg[j][:], -1.0, neg_half_gate[:, j : j + 1], ALU.add, ALU.mult)
 
         def make_dh(j, span=1):
             e = j // PER_EXPERT
@@ -212,14 +216,15 @@ def tile_moe_rec_mlp_silu_kernel(
                 )
             return dh_ps
 
-        def first_expert_on_vector():
-            parts = []
-            for j in range(PER_EXPERT):
-                parts.append(placed([P, H], F32, f"part{j}"))
-                nc.vector.scalar_tensor_tensor(parts[j][:], tanh_half[j][:], 1.0, make_dh(j), ALU.add, ALU.mult)
-            for j in range(PER_EXPERT):
-                da[j] = placed([P, H], BF16, f"da{j}")
-                nc.vector.tensor_tensor(da[j][:], gated[j][:], parts[j][:], ALU.mult)
+        def make_slope(j):
+            plus_one = placed([P, H], F32, f"plus_one{j}")
+            nc.gpsimd.tensor_scalar(plus_one[:], tanh_half[j][:], 1.0, 1.0, ALU.mult, ALU.add)
+            slope[j] = placed([P, H], F32, f"slope{j}")
+            nc.gpsimd.tensor_tensor(slope[j][:], gated[j][:], plus_one[:], ALU.mult)
+
+        def da_by_slope(j):
+            da[j] = placed([P, H], BF16, f"da{j}")
+            nc.vector.tensor_tensor(da[j][:], slope[j][:], make_dh(j), ALU.mult)
 
         def da_on_both(j):
             da_from(j, make_dh(j))
@@ -303,16 +308,18 @@ def tile_moe_rec_mlp_silu_kernel(
         for j in range(7):
             make_factors(j)
             make_gated(j)
+            if j < PER_EXPERT:
+                make_slope(j)
 
         gather_dy_planes(0)
         gather_dy_planes(1)
         gather_dy_words(1)
-        first_expert_on_vector()
+        da_by_slope(0)
+        da_by_slope(1)
         da_on_both(2)
-        dh_ps = make_dh(3)
-        gather(slot_dy[0], "slot_dy0", dyw[0], U32, (2,))
-        da_from(3, dh_ps)
         interleave(0, on_scalar)
+        gather(slot_dy[0], "slot_dy0", dyw[0], U32, (2,))
+        da_on_both(3)
         make_factors(7)
         make_gated(7)
         quantise(0)
@@ -325,6 +332,7 @@ def tile_moe_rec_mlp_silu_kernel(
         stage(0, 1, high, on_scalar)
         scatter(2, (0,), "scalar")
         scatter(3, (0,), "scalar")
+        scatter(1, (0,), "scalar")
 
         da_on_both(4)
         gather(slot_dy[1], "slot_dy1", dyw[1], U32, (3,))
@@ -339,33 +347,28 @@ def tile_moe_rec_mlp_silu_kernel(
         stage(1, 1, high, on_scalar)
         scatter(2, (1,), "scalar")
         scatter(3, (1,), "scalar")
-        turned = turn(2)
         scatter(0, (0,), "vector")
-        weave(2, turned, on_vector)
-        scatter(1, (0,), "vector")
-        scatter(1, (1,), "scalar")
+        interleave(2, on_vector)
+        scatter(1, (1,), "vector")
 
         turned = turn(3)
         quantise(2)
         weave(3, turned, on_vector)
-        stage(2, 0, make_dx(2, 0), on_vector)
         quantise(3)
-        late = {r: bank([P, 2 * C], f"dx_late{r}", DX_BANKS[e][1]) for e, r in ((2, 3), (3, 1))}
-        for r in late:
-            dx_rows(2, r, late[r][:, 0:C])
+        low, high = make_dx(2, 0), make_dx(2, 1)
+        stage(2, 0, low, on_scalar)
+        stage(2, 1, high, on_scalar)
         scatter(0, (1, 2), "vector")
         scatter(2, (2,), "scalar")
-        stage(3, 0, make_dx(3, 0), on_scalar)
-        for r in late:
-            dx_rows(3, r, late[r][:, C : 2 * C])
-        nc.scalar.copy(staged[1][:, 1, 2 * C : 4 * C], late[3][:])
+        low, high = make_dx(3, 0), make_dx(3, 1)
+        stage(3, 0, low, on_scalar)
+        stage(3, 1, high, on_vector)
         scatter(0, (3,), "vector")
         store(0, nc.sync)
+        scatter(3, (2,), "scalar")
         scatter(2, (3,), "scalar")
         store(2, nc.sync)
-        nc.scalar.copy(staged[1][:, 0, 2 * C : 4 * C], late[1][:])
+        scatter(3, (3,), "scalar")
+        store(3, nc.scalar)
         scatter(1, (2, 3), "vector")
         store(1, nc.sync)
-        scatter(3, (2,), "scalar")
-        scatter(3, (3,), "scalar")
-        store(3, nc.sync)

@@ -32,7 +32,7 @@ LAP = 64
 
 WORDS, BYTES_, DA, WIDE, WINDOW = 4 * C, C, 2 * H, 4 * H, 4 * T
 CHAINS = (
-    (("gate_rows", 4 * P), ("slot_x_plane_2", 2 * C)),
+    (("xw", WINDOW), ("slot_x_plane_2", 2 * C)),
     (("slot_dy0_1", WORDS), ("slot_x_1", WORDS), ("slot_dy1_1", WORDS)),
     (("tanh_half2", WIDE), ("slot_dy0_2", WORDS)),
     (("slot_dy1_2", WORDS), ("interleaved0", WIDE)),
@@ -97,7 +97,7 @@ def tile_moe_rec_mlp_silu_kernel(
                 engine.dma_start(tile[32 * q : 32 * q + rows, :].bitcast(I32), source.bitcast(I32))
 
         def load_pass(name, words):
-            tile = keep.tile([P, words.shape[1]], I32, name=name, align_bytes=MX_ALIGN)
+            tile = placed([P, words.shape[1]], I32, name)
             nc.sync.dma_start(tile[:], words.rearrange("p c d -> p (c d)").bitcast(I32))
             return tile[:]
 

@@ -19,29 +19,36 @@ ALU = mybir.AluOpType
 P = 128
 PACK = 4
 QUADS = 4
+QUAD = P // QUADS
 QUAD_ROWS = 4
 PER_EXPERT = C // P
 GROUPS = E * PER_EXPERT
-ROW_TILES = K // P
-LOW_ROWS, HIGH_ROWS = (0, 2), (1, 3)
+LOW, HIGH = 0, 1
+HALF_ROWS = ((0, 2), (1, 3))
 DY_PASSES = N // (P * PACK)
 STRIPE = 16
 MX_ALIGN = 64
 BANK = 2048
 LAP = 64
 
-WORDS, BYTES_, DA, WIDE, WINDOW = 4 * C, C, 2 * H, 4 * H, 4 * T
+WORDS = PACK * C
+SCALES = C
+DA = 2 * H
+WIDE = PACK * H
+TOKENS = PACK * T
+
 CHAINS = (
-    (("xw", WINDOW), ("slot_x_plane_2", 2 * C)),
+    (("xw", TOKENS), ("slot_x_plane_2", 2 * SCALES)),
     (("slot_dy0_1", WORDS), ("slot_x_1", WORDS), ("slot_dy1_1", WORDS)),
     (("tanh_half2", WIDE), ("slot_dy0_2", WORDS)),
     (("slot_dy1_2", WORDS), ("interleaved0", WIDE)),
-    (("silu_neg7", WIDE), ("da1", DA), ("tanh_half7", WIDE), ("window0", WINDOW)),
+    (("silu_neg7", WIDE), ("da1", DA), ("tanh_half7", WIDE), ("window0", TOKENS)),
     (("part6", WIDE), ("interleaved1", WIDE), ("part7", WIDE)),
     (("tanh_half4", WIDE), ("slot_dy1_3", WORDS)),
     (("da7", DA), ("codes2", WORDS)),
     (("part3", WIDE), ("gated7", WIDE)),
 )
+WITHIN_INTERLEAVED0 = (("slot_dy_planes_2", SCALES), ("slot_dy_planes_3", SCALES), ("slot_dy0_3", WORDS))
 
 
 def seat_offsets():
@@ -51,13 +58,14 @@ def seat_offsets():
             offsets[name] = at
             at = at + size - LAP
         at = at + LAP
-    offsets["slot_dy_planes_2"] = offsets["interleaved0"] + 2 * LAP
-    offsets["slot_dy_planes_3"] = offsets["slot_dy_planes_2"] + BYTES_
-    offsets["slot_dy0_3"] = offsets["slot_dy_planes_3"] + BYTES_
+    at = offsets["interleaved0"] + 2 * LAP
+    for name, size in WITHIN_INTERLEAVED0:
+        offsets[name] = at
+        at = at + size
     return offsets
 
 
-A_BANKS = (0, 1, 2, 3, 0, 1, 2, 3)
+A_BANKS = (0, 1, 2, 3, 0, 1, 7, 3)
 DH_BANKS = (4, 5, 6, 4, 5, 6, 4, 0)
 DX_BANKS = ((0, 1), (2, 3), (0, 1), (2, 3))
 TURN_BANKS = (7, 5, 7, 4)
@@ -85,16 +93,19 @@ def tile_moe_rec_mlp_silu_kernel(
                 return seats.tile(shape, dtype, name=name, offset=seat[name], align_bytes=MX_ALIGN)
             return keep.tile(shape, dtype, name=name, align_bytes=MX_ALIGN)
 
-        def zeroed_planes(name, width, engine):
+        def bank(shape, name, bank_index):
+            return banks.tile(shape, F32, name=name, offset=bank_index * BANK)
+
+        def zeroed_planes(name, width):
             tile = keep.tile([P, width], U8, name=name, align_bytes=MX_ALIGN)
-            engine.memset(tile[:].bitcast(I32), 0)
+            nc.vector.memset(tile[:].bitcast(I32), 0)
             return tile
 
-        def load_planes(tile, planes, engine=nc.sync):
+        def load_planes(tile, planes):
             rows = planes.shape[0] * QUAD_ROWS
             for q in range(QUADS):
                 source = planes[:, QUAD_ROWS * q : QUAD_ROWS * (q + 1), :]
-                engine.dma_start(tile[32 * q : 32 * q + rows, :].bitcast(I32), source.bitcast(I32))
+                nc.sync.dma_start(tile[QUAD * q : QUAD * q + rows, :].bitcast(I32), source.bitcast(I32))
 
         def load_pass(name, words):
             tile = placed([P, words.shape[1]], I32, name)
@@ -106,10 +117,10 @@ def tile_moe_rec_mlp_silu_kernel(
             nc.sync.dma_start(tile[:], words.rearrange("j p c d -> p j (c d)").bitcast(I32))
             return [tile[:, j, :] for j in range(words.shape[0])]
 
-        w2_planes = zeroed_planes("w2_planes", E * DY_PASSES * H, nc.vector)
-        w1_planes = zeroed_planes("w1_planes", H, nc.vector)
-        dy_planes = zeroed_planes("dy_planes", T, nc.vector)
-        w1t_planes = zeroed_planes("w1t_planes", K, nc.vector)
+        w2_planes = zeroed_planes("w2_planes", E * DY_PASSES * H)
+        w1_planes = zeroed_planes("w1_planes", H)
+        dy_planes = zeroed_planes("dy_planes", T)
+        w1t_planes = zeroed_planes("w1t_planes", K)
 
         zero = keep.tile([P, 1], F32, name="zero")
         no_bias = keep.tile([P, 1], F32, name="no_bias")
@@ -122,12 +133,12 @@ def tile_moe_rec_mlp_silu_kernel(
         x_plane = keep.tile([P, T], U8, name="x_plane", align_bytes=MX_ALIGN)
         for q in range(QUADS):
             source = x_scales[:, QUAD_ROWS * q : QUAD_ROWS * (q + 1), :].bitcast(I32)
-            nc.sync.dma_start(x_plane[32 * q : 32 * (q + 1), :].bitcast(I32), source.to_broadcast([32 // QUAD_ROWS, QUAD_ROWS, T // 4]))
+            nc.sync.dma_start(x_plane[QUAD * q : QUAD * (q + 1), :].bitcast(I32), source.to_broadcast([QUAD // QUAD_ROWS, QUAD_ROWS, T // PACK]))
         xw = load_pass("xw", x_words[0]).bitcast(U32)
         w1 = [load_pass("w1_0", w1_words[0, 0])]
         load_planes(w1_planes, w1_scales[:, 0])
         gate_rows = placed([P, P], F32, "gate_rows")
-        nc.sync.dma_start(gate_rows[:], gate[0 : P * P // T, :].rearrange("a (c m) -> (a c) m", m=P))
+        nc.sync.dma_start(gate_rows[:], gate[0 : P // GROUPS, :].rearrange("a (c m) -> (a c) m", m=P))
         dyw = [words.bitcast(U32) for words in load_passes("dyw", dy_words)]
         load_planes(dy_planes, dy_scales)
         w1.append(load_pass("w1_1", w1_words[1, 0]))
@@ -136,7 +147,7 @@ def tile_moe_rec_mlp_silu_kernel(
         w2_scale_rows = w2t_scales.rearrange("e s (q r) i -> r q (e s) i", r=QUAD_ROWS)
         for r in range(QUAD_ROWS):
             nc.gpsimd.dma_start(
-                w2_planes[r:P:32, :].bitcast(I32).rearrange("q (j w) -> q j w", j=E * DY_PASSES), w2_scale_rows[r].bitcast(I32)
+                w2_planes[r:P:QUAD, :].bitcast(I32).rearrange("q (j w) -> q j w", j=E * DY_PASSES), w2_scale_rows[r].bitcast(I32)
             )
         w1.append(load_pass("w1_3", w1_words[3, 0]))
         w2.extend(load_passes("w2_1", w2t_words[1]))
@@ -145,9 +156,6 @@ def tile_moe_rec_mlp_silu_kernel(
         w2.extend(load_passes("w2_2", w2t_words[2]))
         w2.extend(load_passes("w2_3", w2t_words[3]))
         w1t.extend(load_passes("w1t_23", w1t_words[2:4, 0]))
-
-        def bank(shape, name, bank_index):
-            return banks.tile(shape, F32, name=name, offset=bank_index * BANK)
 
         gate_ps = bank([P, H], "gate_ps", GATE_BANK)
         nc.tensor.transpose(gate_ps[:, 0:P], gate_rows[:], ident[:])
@@ -159,22 +167,26 @@ def tile_moe_rec_mlp_silu_kernel(
         slot_x_plane, slot_x, slot_dy_planes = {}, {}, {}
         slot_dy = [{} for s in range(DY_PASSES)]
 
-        def gather(into, name, window, dtype, experts):
+        def gather(by_group, name, window, dtype, experts):
             tile = placed([P, len(experts) * C], dtype, f"{name}_{experts[0]}")
             nc.vector.tensor_copy(tile[:], window.indirect(listed(experts[0] * C, len(experts) * C)))
-            for i in range(len(experts) * PER_EXPERT):
-                into[experts[0] * PER_EXPERT + i] = tile[:, i * P : (i + 1) * P]
+            for c in range(len(experts) * PER_EXPERT):
+                by_group[experts[0] * PER_EXPERT + c] = tile[:, c * P : (c + 1) * P]
 
-        def gather_dy_words(e):
-            for s in range(DY_PASSES):
-                gather(slot_dy[s], f"slot_dy{s}", dyw[s], U32, (e,))
+        def gather_x_plane(experts):
+            gather(slot_x_plane, "slot_x_plane", x_plane[:], U8, experts)
+
+        def gather_x_words(experts):
+            gather(slot_x, "slot_x", xw, U32, experts)
 
         def gather_dy_planes(e):
             gather(slot_dy_planes, "slot_dy_planes", dy_planes[:], U8, (e,))
 
-        windows = {}
-        silu_neg, tanh_half, gated, slope = {}, {}, {}, {}
-        da, codes, da_plane = {}, {}, {}
+        def gather_dy_words(e, s):
+            gather(slot_dy[s], f"slot_dy{s}", dyw[s], U32, (e,))
+
+        silu_neg, tanh_half, gated, slope, da = {}, {}, {}, {}, {}
+        interleaved, codes, da_plane, windows = {}, {}, {}, {}
 
         def make_factors(j):
             a_ps = bank([P, H], f"a_ps{j}", A_BANKS[j])
@@ -195,47 +207,42 @@ def tile_moe_rec_mlp_silu_kernel(
 
         def make_gated(j):
             gated[j] = placed([P, H], F32, f"gated{j}")
-            if j < PER_EXPERT:
-                nc.scalar.activation(gated[j][:], silu_neg[j][:], ACT.Identity, bias=half_gate[:, j : j + 1], scale=neg_half_gate[:, j : j + 1])
-            else:
-                nc.gpsimd.tensor_scalar(gated[j][:], silu_neg[j][:], -1.0, neg_half_gate[:, j : j + 1], ALU.add, ALU.mult)
-
-        def make_dh(j, span=1):
-            e = j // PER_EXPERT
-            dh_ps = bank([P, span * H], f"dh_ps{j}", DH_BANKS[j])[:, 0:H]
-            for s in range(DY_PASSES):
-                n = DY_PASSES * e + s
-                nc.tensor.matmul_mx(
-                    dh_ps,
-                    lhsT=slot_dy[s][j].bitcast(FP8X4),
-                    lhsT_scale=slot_dy_planes[j][QUAD_ROWS * s :, :],
-                    rhs=w2[n].bitcast(FP8X4),
-                    rhs_scale=w2_planes[:, n * H : (n + 1) * H],
-                    start=(s == 0),
-                    stop=(s == DY_PASSES - 1),
-                )
-            return dh_ps
+            nc.gpsimd.tensor_scalar(gated[j][:], silu_neg[j][:], -1.0, neg_half_gate[:, j : j + 1], ALU.add, ALU.mult)
 
         def make_slope(j):
+            gated[j] = placed([P, H], F32, f"gated{j}")
+            nc.scalar.activation(gated[j][:], silu_neg[j][:], ACT.Identity, bias=half_gate[:, j : j + 1], scale=neg_half_gate[:, j : j + 1])
             plus_one = placed([P, H], F32, f"plus_one{j}")
             nc.gpsimd.tensor_scalar(plus_one[:], tanh_half[j][:], 1.0, 1.0, ALU.mult, ALU.add)
             slope[j] = placed([P, H], F32, f"slope{j}")
             nc.gpsimd.tensor_tensor(slope[j][:], gated[j][:], plus_one[:], ALU.mult)
 
+        def make_dh(j):
+            e = j // PER_EXPERT
+            dh_ps = bank([P, H], f"dh_ps{j}", DH_BANKS[j])
+            for s in range(DY_PASSES):
+                w2_pass = DY_PASSES * e + s
+                nc.tensor.matmul_mx(
+                    dh_ps[:],
+                    lhsT=slot_dy[s][j].bitcast(FP8X4),
+                    lhsT_scale=slot_dy_planes[j][QUAD_ROWS * s :, :],
+                    rhs=w2[w2_pass].bitcast(FP8X4),
+                    rhs_scale=w2_planes[:, w2_pass * H : (w2_pass + 1) * H],
+                    start=(s == 0),
+                    stop=(s == DY_PASSES - 1),
+                )
+            return dh_ps
+
         def da_by_slope(j):
             da[j] = placed([P, H], BF16, f"da{j}")
-            nc.vector.tensor_tensor(da[j][:], slope[j][:], make_dh(j), ALU.mult)
+            nc.vector.tensor_tensor(da[j][:], slope[j][:], make_dh(j)[:], ALU.mult)
 
-        def da_on_both(j):
-            da_from(j, make_dh(j))
-
-        def da_from(j, dh_ps):
+        def da_by_part(j):
+            dh_ps = make_dh(j)
             part = placed([P, H], F32, f"part{j}")
-            nc.vector.scalar_tensor_tensor(part[:], tanh_half[j][:], 1.0, dh_ps, ALU.add, ALU.mult)
+            nc.vector.scalar_tensor_tensor(part[:], tanh_half[j][:], 1.0, dh_ps[:], ALU.add, ALU.mult)
             da[j] = placed([P, H], BF16, f"da{j}")
             nc.gpsimd.tensor_tensor(da[j][:], gated[j][:], part[:], ALU.mult)
-
-        interleaved = {}
 
         def turn(e):
             turned = bank([P, PER_EXPERT, 2, P], f"turned{e}", TURN_BANKS[e])
@@ -251,124 +258,123 @@ def tile_moe_rec_mlp_silu_kernel(
                 interleaved[e][:].bitcast(F32).rearrange("p (c m u) -> p c m u", c=PER_EXPERT, u=2), turned[:].rearrange("p c u m -> p c m u")
             )
 
-        def interleave(e, copy):
-            weave(e, turn(e), copy)
-
         def quantise(e):
             codes[e] = placed([P, C], U32, f"codes{e}")
             da_plane[e] = placed([P, C], U8, f"da_plane{e}")
             nc.vector.quantize_mx(out=codes[e][:].bitcast(FP8X4), scales=da_plane[e][:], in_=interleaved[e][:])
 
-        def dx_rows(e, r, dx_ps):
-            rows = slice(r * P, (r + 1) * P)
-            nc.tensor.matmul_mx(
-                dx_ps,
-                lhsT=w1t[e][:, rows].bitcast(FP8X4),
-                lhsT_scale=w1t_planes[QUAD_ROWS * e :, rows],
-                rhs=codes[e][:].bitcast(FP8X4),
-                rhs_scale=da_plane[e][:],
-                start=True,
-                stop=True,
-            )
+        def make_dx(e):
+            halves = []
+            for half in (LOW, HIGH):
+                dx_ps = bank([P, len(HALF_ROWS[half]), C], f"dx_ps{e}_{half}", DX_BANKS[e][half])
+                for place, r in enumerate(HALF_ROWS[half]):
+                    rows = slice(r * P, (r + 1) * P)
+                    nc.tensor.matmul_mx(
+                        dx_ps[:, place, :],
+                        lhsT=w1t[e][:, rows].bitcast(FP8X4),
+                        lhsT_scale=w1t_planes[QUAD_ROWS * e :, rows],
+                        rhs=codes[e][:].bitcast(FP8X4),
+                        rhs_scale=da_plane[e][:],
+                        start=True,
+                        stop=True,
+                    )
+                halves.append(dx_ps)
+            return halves
 
-        def make_dx(e, half):
-            row_tiles = (LOW_ROWS, HIGH_ROWS)[half]
-            dx_ps = bank([P, len(row_tiles), C], f"dx_ps{e}_{half}", DX_BANKS[e][half])
-            for i, r in enumerate(row_tiles):
-                dx_rows(e, r, dx_ps[:, i, :])
-            return dx_ps
+        staged = [keep.tile([P, len(HALF_ROWS[half]), T], F32, name=f"staged{half}") for half in (LOW, HIGH)]
 
-        staged = [keep.tile([P, len(LOW_ROWS), T], F32, name=f"staged{half}") for half in range(2)]
+        def stage(e, half, dx, copy):
+            copy(staged[half][:, :, e * C : (e + 1) * C], dx[half][:])
 
-        def stage(e, half, dx_ps, copy):
-            copy(staged[half][:, :, e * C : (e + 1) * C], dx_ps[:])
-
-        def scatter(r, experts, engine):
+        def scatter(r, experts, copy):
             if r not in windows:
                 windows[r] = placed([P, T], F32, f"window{r}")
             first, count = experts[0] * C, len(experts) * C
-            into = windows[r][:].indirect(listed(first, count))
-            source = staged[r % 2][:, r // 2, first : first + count]
-            if engine == "vector":
-                nc.vector.tensor_copy(into, source)
-            else:
-                nc.scalar.activation(into, source, ACT.Copy)
+            half = LOW if r in HALF_ROWS[LOW] else HIGH
+            copy(windows[r][:].indirect(listed(first, count)), staged[half][:, HALF_ROWS[half].index(r), first : first + count])
+
+        def scalar_scatter(window, values):
+            nc.scalar.activation(window, values, ACT.Copy)
 
         def store(r, engine):
             engine.dma_start(out[r * P : (r + 1) * P, :], windows[r][:])
 
-        on_scalar, on_vector = nc.scalar.copy, nc.vector.tensor_copy
+        scalar_copy, vector_copy = nc.scalar.copy, nc.vector.tensor_copy
 
-        gather(slot_x_plane, "slot_x_plane", x_plane[:], U8, (0, 1))
-        gather(slot_x, "slot_x", xw, U32, (0,))
-        gather(slot_x, "slot_x", xw, U32, (1,))
-        gather(slot_x, "slot_x", xw, U32, (2, 3))
-        gather(slot_x_plane, "slot_x_plane", x_plane[:], U8, (2, 3))
-        gather_dy_words(0)
-        for j in range(7):
+        gather_x_plane((0, 1))
+        gather_x_words((0,))
+        gather_x_words((1,))
+        gather_x_words((2, 3))
+        gather_x_plane((2, 3))
+        for s in range(DY_PASSES):
+            gather_dy_words(0, s)
+        for j in range(PER_EXPERT):
+            make_factors(j)
+            make_slope(j)
+        for j in range(PER_EXPERT, GROUPS - PER_EXPERT):
             make_factors(j)
             make_gated(j)
-            if j < PER_EXPERT:
-                make_slope(j)
 
         gather_dy_planes(0)
         gather_dy_planes(1)
-        gather_dy_words(1)
+        for s in range(DY_PASSES):
+            gather_dy_words(1, s)
         da_by_slope(0)
         da_by_slope(1)
-        da_on_both(2)
-        interleave(0, on_scalar)
-        gather(slot_dy[0], "slot_dy0", dyw[0], U32, (2,))
-        da_on_both(3)
+        da_by_part(2)
+        weave(0, turn(0), scalar_copy)
+        gather_dy_words(2, 0)
+        da_by_part(3)
         make_factors(7)
+        make_factors(6)
+        make_gated(6)
         make_gated(7)
         quantise(0)
         gather_dy_planes(2)
-        gather(slot_dy[1], "slot_dy1", dyw[1], U32, (2,))
+        gather_dy_words(2, 1)
         gather_dy_planes(3)
-        gather(slot_dy[0], "slot_dy0", dyw[0], U32, (3,))
-        low, high = make_dx(0, 0), make_dx(0, 1)
-        stage(0, 0, low, on_scalar)
-        stage(0, 1, high, on_scalar)
-        scatter(2, (0,), "scalar")
-        scatter(3, (0,), "scalar")
-        scatter(1, (0,), "scalar")
+        gather_dy_words(3, 0)
+        dx = make_dx(0)
+        stage(0, LOW, dx, scalar_copy)
+        stage(0, HIGH, dx, scalar_copy)
+        for r in (2, 3, 1):
+            scatter(r, (0,), scalar_scatter)
 
-        da_on_both(4)
-        gather(slot_dy[1], "slot_dy1", dyw[1], U32, (3,))
+        da_by_part(4)
+        gather_dy_words(3, 1)
         turned = turn(1)
-        da_on_both(5)
-        weave(1, turned, on_vector)
+        da_by_part(5)
+        weave(1, turned, vector_copy)
         quantise(1)
-        da_on_both(6)
-        da_on_both(7)
-        low, high = make_dx(1, 0), make_dx(1, 1)
-        stage(1, 0, low, on_scalar)
-        stage(1, 1, high, on_scalar)
-        scatter(2, (1,), "scalar")
-        scatter(3, (1,), "scalar")
-        scatter(0, (0,), "vector")
-        interleave(2, on_vector)
-        scatter(1, (1,), "vector")
+        da_by_part(6)
+        da_by_part(7)
+        dx = make_dx(1)
+        stage(1, LOW, dx, scalar_copy)
+        stage(1, HIGH, dx, scalar_copy)
+        for r in (2, 3):
+            scatter(r, (1,), scalar_scatter)
+        scatter(0, (0,), vector_copy)
+        weave(2, turn(2), vector_copy)
+        scatter(1, (1,), vector_copy)
 
         turned = turn(3)
         quantise(2)
-        weave(3, turned, on_vector)
+        weave(3, turned, vector_copy)
         quantise(3)
-        low, high = make_dx(2, 0), make_dx(2, 1)
-        stage(2, 0, low, on_scalar)
-        stage(2, 1, high, on_scalar)
-        scatter(0, (1, 2), "vector")
-        scatter(2, (2,), "scalar")
-        low, high = make_dx(3, 0), make_dx(3, 1)
-        stage(3, 0, low, on_scalar)
-        stage(3, 1, high, on_vector)
-        scatter(0, (3,), "vector")
+        dx = make_dx(2)
+        stage(2, LOW, dx, scalar_copy)
+        stage(2, HIGH, dx, scalar_copy)
+        scatter(0, (1, 2), vector_copy)
+        scatter(2, (2,), scalar_scatter)
+        dx = make_dx(3)
+        stage(3, LOW, dx, scalar_copy)
+        stage(3, HIGH, dx, vector_copy)
+        scatter(0, (3,), vector_copy)
         store(0, nc.sync)
-        scatter(3, (2,), "scalar")
-        scatter(2, (3,), "scalar")
+        scatter(3, (2,), scalar_scatter)
+        scatter(2, (3,), scalar_scatter)
         store(2, nc.sync)
-        scatter(3, (3,), "scalar")
+        scatter(3, (3,), scalar_scatter)
         store(3, nc.scalar)
-        scatter(1, (2, 3), "vector")
+        scatter(1, (2, 3), vector_copy)
         store(1, nc.sync)

@@ -23,13 +23,13 @@ QUAD = P // QUADS
 QUAD_ROWS = 4
 PER_EXPERT = C // P
 GROUPS = E * PER_EXPERT
-LOW, HIGH = 0, 1
+EARLY, LATE = 0, 1
 HALF_ROWS = ((0, 2), (1, 3))
 DY_PASSES = N // (P * PACK)
 STRIPE = 16
 MX_ALIGN = 64
 BANK = 2048
-LAP = 64
+ITEM_BYTES = {F32: 4, I32: 4, U32: 4, BF16: 2, U8: 1}
 
 WORDS = PACK * C
 SCALES = C
@@ -37,38 +37,49 @@ DA = 2 * H
 WIDE = PACK * H
 TOKENS = PACK * T
 
-CHAINS = (
-    (("xw", TOKENS), ("slot_x_plane_2", 2 * SCALES)),
-    (("slot_dy0_1", WORDS), ("slot_x_1", WORDS), ("slot_dy1_1", WORDS)),
-    (("tanh_half2", WIDE), ("slot_dy0_2", WORDS)),
-    (("slot_dy1_2", WORDS), ("interleaved0", WIDE)),
-    (("silu_neg7", WIDE), ("da1", DA), ("tanh_half7", WIDE), ("window0", TOKENS)),
-    (("part6", WIDE), ("interleaved1", WIDE), ("part7", WIDE)),
-    (("tanh_half4", WIDE), ("slot_dy1_3", WORDS)),
-    (("da7", DA), ("codes2", WORDS)),
-    (("part3", WIDE), ("gated7", WIDE)),
+GUESTS = {
+    "slot_x_0": (("slot_x_plane_4", 2 * SCALES),),
+    "tanh_half2": (("slot_dy0_4", WORDS), ("gated3", WIDE),),
+    "slot_dy1_2": (("slot_dy1_4", WORDS),),
+    "da0": (("slot_dy_planes_4", SCALES), ("slot_dy_planes_6", SCALES), ("part3", WIDE), ("silu_neg7", WIDE), ("tanh_half7", WIDE), ("gated5", WIDE),),
+    "interleaved0": (("part4", WIDE), ("part5", WIDE), ("slot_dy0_6", WORDS), ("slot_dy1_6", WORDS), ("da3", DA), ("gated4", WIDE),),
+    "slot_dy0_6": (("codes1", WORDS),),
+    "slot_dy1_6": (("window0", TOKENS),),
+    "interleaved1": (("da5", DA), ("gated6", WIDE),),
+    "da4": (("window1", TOKENS), ("part7", WIDE),),
+    "da6": (("staged2_row0", WORDS),),
+}
+HOSTS = (
+    ("slot_x_0", WORDS // 2),
+    ("tanh_half2", WIDE),
+    ("slot_dy1_2", WORDS),
+    ("da0", DA),
+    ("interleaved0", WIDE),
+    ("interleaved1", WIDE),
+    ("da4", DA),
+    ("da6", DA),
 )
-WITHIN_INTERLEAVED0 = (("slot_dy_planes_2", SCALES), ("slot_dy_planes_3", SCALES), ("slot_dy0_3", WORDS))
 
 
-def seat_offsets():
-    offsets, at = {}, 0
-    for chain in CHAINS:
-        for name, size in chain:
-            offsets[name] = at
-            at = at + size - LAP
-        at = at + LAP
-    at = offsets["interleaved0"] + 2 * LAP
-    for name, size in WITHIN_INTERLEAVED0:
-        offsets[name] = at
-        at = at + size
-    return offsets
+def lay_out(name, size, at, seats):
+    end = at
+    for guest, guest_size in GUESTS.get(name, ()):
+        end = end + lay_out(guest, guest_size, end, seats)
+    seats[name] = (at, max(size, end - at))
+    return seats[name][1]
 
 
-A_BANKS = (0, 1, 2, 3, 0, 1, 7, 3)
-DH_BANKS = (4, 5, 6, 4, 5, 6, 4, 0)
-DX_BANKS = ((0, 1), (2, 3), (0, 1), (2, 3))
-TURN_BANKS = (7, 5, 7, 4)
+def seat_plan():
+    seats, at = {}, 0
+    for name, size in HOSTS:
+        at = at + lay_out(name, size, at, seats)
+    return seats
+
+
+A_BANKS = (0, 1, 2, 3, 0, 1, 2, 3)
+DH_BANKS = (4, 5, 6, 7, 4, 5, 1, 7)
+DX_BANKS = ((0, 1), (2, 3), (6, 0), (4, 5))
+TURN_BANKS = (6, 0, 1, 7)
 GATE_BANK = 7
 
 
@@ -76,7 +87,7 @@ def tile_moe_rec_mlp_silu_kernel(
     tc, x_words, x_scales, dy_words, dy_scales, w1_words, w1_scales, w2t_words, w2t_scales, w1t_words, w1t_scales, gate, offs, out
 ):
     nc = tc.nc
-    seat = seat_offsets()
+    seat = seat_plan()
     with ExitStack() as ctx:
         keep = ctx.enter_context(tc.tile_pool(name="keep", bufs=1))
         seats = ctx.enter_context(tc.tile_pool(name="seats", bufs=1))
@@ -88,10 +99,11 @@ def tile_moe_rec_mlp_silu_kernel(
         def listed(first_slot, count):
             return offsets[:, first_slot // STRIPE : (first_slot + count) // STRIPE]
 
-        def placed(shape, dtype, name):
-            if name in seat:
-                return seats.tile(shape, dtype, name=name, offset=seat[name], align_bytes=MX_ALIGN)
-            return keep.tile(shape, dtype, name=name, align_bytes=MX_ALIGN)
+        def placed(width, dtype, name):
+            if name not in seat:
+                return keep.tile([P, width], dtype, name=name, align_bytes=MX_ALIGN)[:]
+            offset, size = seat[name]
+            return seats.tile([P, size // ITEM_BYTES[dtype]], dtype, name=name, offset=offset, align_bytes=MX_ALIGN)[:, 0:width]
 
         def bank(shape, name, bank_index):
             return banks.tile(shape, F32, name=name, offset=bank_index * BANK)
@@ -108,7 +120,7 @@ def tile_moe_rec_mlp_silu_kernel(
                 nc.sync.dma_start(tile[QUAD * q : QUAD * q + rows, :].bitcast(I32), source.bitcast(I32))
 
         def load_pass(name, words):
-            tile = placed([P, words.shape[1]], I32, name)
+            tile = placed(words.shape[1], I32, name)
             nc.sync.dma_start(tile[:], words.rearrange("p c d -> p (c d)").bitcast(I32))
             return tile[:]
 
@@ -117,15 +129,15 @@ def tile_moe_rec_mlp_silu_kernel(
             nc.sync.dma_start(tile[:], words.rearrange("j p c d -> p j (c d)").bitcast(I32))
             return [tile[:, j, :] for j in range(words.shape[0])]
 
-        w2_planes = zeroed_planes("w2_planes", E * DY_PASSES * H)
-        w1_planes = zeroed_planes("w1_planes", H)
-        dy_planes = zeroed_planes("dy_planes", T)
-        w1t_planes = zeroed_planes("w1t_planes", K)
-
         zero = keep.tile([P, 1], F32, name="zero")
         no_bias = keep.tile([P, 1], F32, name="no_bias")
         nc.vector.memset(zero[:], 0.0)
         nc.scalar.activation(no_bias[:], zero[:], ACT.Silu)
+
+        w1_planes = zeroed_planes("w1_planes", H)
+        w2_planes = zeroed_planes("w2_planes", E * DY_PASSES * H)
+        dy_planes = zeroed_planes("dy_planes", T)
+        w1t_planes = zeroed_planes("w1t_planes", K)
 
         ident = keep.tile([P, P], F32, name="ident")
         make_identity(nc, ident[:])
@@ -137,62 +149,63 @@ def tile_moe_rec_mlp_silu_kernel(
         xw = load_pass("xw", x_words[0]).bitcast(U32)
         w1 = [load_pass("w1_0", w1_words[0, 0])]
         load_planes(w1_planes, w1_scales[:, 0])
-        gate_rows = placed([P, P], F32, "gate_rows")
+        gate_rows = placed(P, F32, "gate_rows")
         nc.sync.dma_start(gate_rows[:], gate[0 : P // GROUPS, :].rearrange("a (c m) -> (a c) m", m=P))
-        dyw = [words.bitcast(U32) for words in load_passes("dyw", dy_words)]
+        dyw = [load_pass(f"dyw{s}", dy_words[s]).bitcast(U32) for s in range(DY_PASSES)]
         load_planes(dy_planes, dy_scales)
         w1.append(load_pass("w1_1", w1_words[1, 0]))
         w1.append(load_pass("w1_2", w1_words[2, 0]))
-        w2 = load_passes("w2_0", w2t_words[0])
         w2_scale_rows = w2t_scales.rearrange("e s (q r) i -> r q (e s) i", r=QUAD_ROWS)
         for r in range(QUAD_ROWS):
-            nc.gpsimd.dma_start(
+            nc.sync.dma_start(
                 w2_planes[r:P:QUAD, :].bitcast(I32).rearrange("q (j w) -> q j w", j=E * DY_PASSES), w2_scale_rows[r].bitcast(I32)
             )
+        w2 = load_passes("w2_0", w2t_words[0])
         w1.append(load_pass("w1_3", w1_words[3, 0]))
         w2.extend(load_passes("w2_1", w2t_words[1]))
-        load_planes(w1t_planes, w1t_scales[:, 0])
-        w1t = load_passes("w1t_01", w1t_words[0:2, 0])
         w2.extend(load_passes("w2_2", w2t_words[2]))
+        load_planes(w1t_planes, w1t_scales[:, 0])
+        w1t = load_passes("w1t", w1t_words[:, 0])
         w2.extend(load_passes("w2_3", w2t_words[3]))
-        w1t.extend(load_passes("w1t_23", w1t_words[2:4, 0]))
 
         gate_ps = bank([P, H], "gate_ps", GATE_BANK)
         nc.tensor.transpose(gate_ps[:, 0:P], gate_rows[:], ident[:])
         neg_half_gate = keep.tile([P, GROUPS], F32, name="neg_half_gate")
         nc.scalar.activation(neg_half_gate[:], gate_ps[:, 0:GROUPS], ACT.Copy, scale=-0.5)
-        half_gate = keep.tile([P, PER_EXPERT], F32, name="half_gate")
-        nc.scalar.activation(half_gate[:], gate_ps[:, 0:PER_EXPERT], ACT.Copy, scale=0.5)
+        half_gate = keep.tile([P, GROUPS], F32, name="half_gate")
+        nc.scalar.activation(half_gate[:], gate_ps[:, 0:GROUPS], ACT.Copy, scale=0.5)
 
         slot_x_plane, slot_x, slot_dy_planes = {}, {}, {}
         slot_dy = [{} for s in range(DY_PASSES)]
 
-        def gather(by_group, name, window, dtype, experts):
-            tile = placed([P, len(experts) * C], dtype, f"{name}_{experts[0]}")
-            nc.vector.tensor_copy(tile[:], window.indirect(listed(experts[0] * C, len(experts) * C)))
-            for c in range(len(experts) * PER_EXPERT):
-                by_group[experts[0] * PER_EXPERT + c] = tile[:, c * P : (c + 1) * P]
+        def gather(by_group, name, window, dtype, first, count):
+            tile = placed(count * P, dtype, f"{name}_{first}")
+            nc.vector.tensor_copy(tile[:], window.indirect(listed(first * P, count * P)))
+            for c in range(count):
+                by_group[first + c] = tile[:, c * P : (c + 1) * P]
 
-        def gather_x_plane(experts):
-            gather(slot_x_plane, "slot_x_plane", x_plane[:], U8, experts)
+        def gather_x_plane(first, count):
+            gather(slot_x_plane, "slot_x_plane", x_plane[:], U8, first, count)
 
-        def gather_x_words(experts):
-            gather(slot_x, "slot_x", xw, U32, experts)
+        def gather_x_words(first, count):
+            gather(slot_x, "slot_x", xw, U32, first, count)
 
         def gather_dy_planes(e):
-            gather(slot_dy_planes, "slot_dy_planes", dy_planes[:], U8, (e,))
+            gather(slot_dy_planes, "slot_dy_planes", dy_planes[:], U8, e * PER_EXPERT, PER_EXPERT)
 
         def gather_dy_words(e, s):
-            gather(slot_dy[s], f"slot_dy{s}", dyw[s], U32, (e,))
+            gather(slot_dy[s], f"slot_dy{s}", dyw[s], U32, e * PER_EXPERT, PER_EXPERT)
 
         silu_neg, tanh_half, gated, slope, da = {}, {}, {}, {}, {}
         interleaved, codes, da_plane, windows = {}, {}, {}, {}
 
-        def make_factors(j):
-            a_ps = bank([P, H], f"a_ps{j}", A_BANKS[j])
+        a_ps, dh_ps, part, staged = {}, {}, {}, {}
+
+        def make_a(j):
+            a_ps[j] = bank([P, H], f"a_ps{j}", A_BANKS[j])
             e = j // PER_EXPERT
             nc.tensor.matmul_mx(
-                a_ps[:],
+                a_ps[j][:],
                 lhsT=slot_x[j].bitcast(FP8X4),
                 lhsT_scale=slot_x_plane[j],
                 rhs=w1[e].bitcast(FP8X4),
@@ -200,30 +213,36 @@ def tile_moe_rec_mlp_silu_kernel(
                 start=True,
                 stop=True,
             )
-            silu_neg[j] = placed([P, H], F32, f"silu_neg{j}")
-            nc.scalar.activation(silu_neg[j][:], a_ps[:], ACT.Silu, bias=no_bias[:], scale=-1.0)
-            tanh_half[j] = placed([P, H], F32, f"tanh_half{j}")
-            nc.scalar.activation(tanh_half[j][:], a_ps[:], ACT.Tanh, scale=0.5)
+
+        def make_silu(j):
+            silu_neg[j] = placed(H, F32, f"silu_neg{j}")
+            nc.scalar.activation(silu_neg[j][:], a_ps[j][:], ACT.Silu, bias=no_bias[:], scale=-1.0)
+
+        def make_tanh(j):
+            tanh_half[j] = placed(H, F32, f"tanh_half{j}")
+            nc.scalar.activation(tanh_half[j][:], a_ps[j][:], ACT.Tanh, scale=0.5)
 
         def make_gated(j):
-            gated[j] = placed([P, H], F32, f"gated{j}")
+            gated[j] = placed(H, F32, f"gated{j}")
             nc.gpsimd.tensor_scalar(gated[j][:], silu_neg[j][:], -1.0, neg_half_gate[:, j : j + 1], ALU.add, ALU.mult)
 
-        def make_slope(j):
-            gated[j] = placed([P, H], F32, f"gated{j}")
+        def make_gated_on_scalar(j):
+            gated[j] = placed(H, F32, f"gated{j}")
             nc.scalar.activation(gated[j][:], silu_neg[j][:], ACT.Identity, bias=half_gate[:, j : j + 1], scale=neg_half_gate[:, j : j + 1])
-            plus_one = placed([P, H], F32, f"plus_one{j}")
+
+        def make_slope(j):
+            plus_one = placed(H, F32, f"plus_one{j}")
             nc.gpsimd.tensor_scalar(plus_one[:], tanh_half[j][:], 1.0, 1.0, ALU.mult, ALU.add)
-            slope[j] = placed([P, H], F32, f"slope{j}")
+            slope[j] = placed(H, F32, f"slope{j}")
             nc.gpsimd.tensor_tensor(slope[j][:], gated[j][:], plus_one[:], ALU.mult)
 
         def make_dh(j):
             e = j // PER_EXPERT
-            dh_ps = bank([P, H], f"dh_ps{j}", DH_BANKS[j])
+            dh_ps[j] = bank([P, H], f"dh_ps{j}", DH_BANKS[j])
             for s in range(DY_PASSES):
                 w2_pass = DY_PASSES * e + s
                 nc.tensor.matmul_mx(
-                    dh_ps[:],
+                    dh_ps[j][:],
                     lhsT=slot_dy[s][j].bitcast(FP8X4),
                     lhsT_scale=slot_dy_planes[j][QUAD_ROWS * s :, :],
                     rhs=w2[w2_pass].bitcast(FP8X4),
@@ -231,41 +250,41 @@ def tile_moe_rec_mlp_silu_kernel(
                     start=(s == 0),
                     stop=(s == DY_PASSES - 1),
                 )
-            return dh_ps
 
         def da_by_slope(j):
-            da[j] = placed([P, H], BF16, f"da{j}")
-            nc.vector.tensor_tensor(da[j][:], slope[j][:], make_dh(j)[:], ALU.mult)
+            da[j] = placed(H, BF16, f"da{j}")
+            nc.vector.tensor_tensor(da[j][:], slope[j][:], dh_ps[j][:], ALU.mult)
 
-        def da_by_part(j):
-            dh_ps = make_dh(j)
-            part = placed([P, H], F32, f"part{j}")
-            nc.vector.scalar_tensor_tensor(part[:], tanh_half[j][:], 1.0, dh_ps[:], ALU.add, ALU.mult)
-            da[j] = placed([P, H], BF16, f"da{j}")
-            nc.gpsimd.tensor_tensor(da[j][:], gated[j][:], part[:], ALU.mult)
+        def make_part(j):
+            part[j] = placed(H, F32, f"part{j}")
+            nc.vector.scalar_tensor_tensor(part[j][:], tanh_half[j][:], 1.0, dh_ps[j][:], ALU.add, ALU.mult)
 
-        def turn(e):
+        def da_by_part(j, engine):
+            da[j] = placed(H, BF16, f"da{j}")
+            engine.tensor_tensor(da[j][:], gated[j][:], part[j][:], ALU.mult)
+
+        def turn(e, order):
             turned = bank([P, PER_EXPERT, 2, P], f"turned{e}", TURN_BANKS[e])
-            for c in range(PER_EXPERT):
+            for c in order:
                 pairs = da[PER_EXPERT * e + c][:].bitcast(F32)
                 for u in range(2):
                     nc.tensor.transpose(turned[:, c, u, :], pairs[:, u : H // 2 : 2], ident[:])
             return turned
 
         def weave(e, turned, copy):
-            interleaved[e] = placed([P, PER_EXPERT * H], BF16, f"interleaved{e}")
+            interleaved[e] = placed(PER_EXPERT * H, BF16, f"interleaved{e}")
             copy(
                 interleaved[e][:].bitcast(F32).rearrange("p (c m u) -> p c m u", c=PER_EXPERT, u=2), turned[:].rearrange("p c u m -> p c m u")
             )
 
         def quantise(e):
-            codes[e] = placed([P, C], U32, f"codes{e}")
-            da_plane[e] = placed([P, C], U8, f"da_plane{e}")
+            codes[e] = placed(C, U32, f"codes{e}")
+            da_plane[e] = placed(C, U8, f"da_plane{e}")
             nc.vector.quantize_mx(out=codes[e][:].bitcast(FP8X4), scales=da_plane[e][:], in_=interleaved[e][:])
 
         def make_dx(e):
             halves = []
-            for half in (LOW, HIGH):
+            for half in (EARLY, LATE):
                 dx_ps = bank([P, len(HALF_ROWS[half]), C], f"dx_ps{e}_{half}", DX_BANKS[e][half])
                 for place, r in enumerate(HALF_ROWS[half]):
                     rows = slice(r * P, (r + 1) * P)
@@ -281,100 +300,135 @@ def tile_moe_rec_mlp_silu_kernel(
                 halves.append(dx_ps)
             return halves
 
-        staged = [keep.tile([P, len(HALF_ROWS[half]), T], F32, name=f"staged{half}") for half in (LOW, HIGH)]
+        staged_late = keep.tile([P, len(HALF_ROWS[LATE]), T], F32, name="staged_late")
 
-        def stage(e, half, dx, copy):
-            copy(staged[half][:, :, e * C : (e + 1) * C], dx[half][:])
+        def stage_late(e, dx, copy):
+            copy(staged_late[:, :, e * C : (e + 1) * C], dx[LATE][:])
 
-        def scatter(r, experts, copy):
+        def stage_early(e, dx, copy):
+            tile = placed(len(HALF_ROWS[EARLY]) * C, F32, f"staged_early{e}").rearrange("p (r c) -> p r c", c=C)
+            copy(tile, dx[EARLY][:])
+            for place, r in enumerate(HALF_ROWS[EARLY]):
+                staged[r, e] = tile[:, place, :]
+
+        def stage_row(e, r, dx, copy):
+            tile = placed(C, F32, f"staged{e}_row{r}")
+            copy(tile[:], dx[EARLY][:, HALF_ROWS[EARLY].index(r), :])
+            staged[r, e] = tile[:]
+
+        def window(r, first, count):
             if r not in windows:
-                windows[r] = placed([P, T], F32, f"window{r}")
-            first, count = experts[0] * C, len(experts) * C
-            half = LOW if r in HALF_ROWS[LOW] else HIGH
-            copy(windows[r][:].indirect(listed(first, count)), staged[half][:, HALF_ROWS[half].index(r), first : first + count])
+                windows[r] = placed(T, F32, f"window{r}")
+            return windows[r][:].indirect(listed(first, count))
 
-        def scalar_scatter(window, values):
-            nc.scalar.activation(window, values, ACT.Copy)
+        def scatter_early(r, e, copy):
+            copy(window(r, e * C, C), staged[r, e])
+
+        def scatter_late(r, first, count, copy):
+            copy(window(r, first, count), staged_late[:, HALF_ROWS[LATE].index(r), first : first + count])
+
+        def scalar_scatter(target, values):
+            nc.scalar.activation(target, values, ACT.Copy)
 
         def store(r, engine):
             engine.dma_start(out[r * P : (r + 1) * P, :], windows[r][:])
 
         scalar_copy, vector_copy = nc.scalar.copy, nc.vector.tensor_copy
 
-        gather_x_plane((0, 1))
-        gather_x_words((0,))
-        gather_x_words((1,))
-        gather_x_words((2, 3))
-        gather_x_plane((2, 3))
-        for s in range(DY_PASSES):
-            gather_dy_words(0, s)
-        for j in range(PER_EXPERT):
-            make_factors(j)
-            make_slope(j)
-        for j in range(PER_EXPERT, GROUPS - PER_EXPERT):
-            make_factors(j)
-            make_gated(j)
-
-        gather_dy_planes(0)
-        gather_dy_planes(1)
-        for s in range(DY_PASSES):
-            gather_dy_words(1, s)
-        da_by_slope(0)
+        gather_x_plane(0, 4)
+        gather_x_words(0, 1)
+        gather_x_words(1, 3)
+        gather_x_words(4, 4)
+        gather_x_plane(4, 4)
+        for e in range(2):
+            for s in range(DY_PASSES):
+                gather_dy_words(e, s)
+            gather_dy_planes(e)
+        for j in range(6):
+            make_a(j)
+            make_silu(j)
+            make_tanh(j)
+        make_gated(0)
+        make_gated(1)
+        make_slope(1)
+        make_gated(2)
+        make_dh(0)
+        make_dh(1)
+        make_a(6)
+        make_a(7)
+        make_silu(6)
+        make_tanh(6)
+        make_dh(2)
+        make_dh(3)
+        make_part(0)
         da_by_slope(1)
-        da_by_part(2)
-        weave(0, turn(0), scalar_copy)
-        gather_dy_words(2, 0)
-        da_by_part(3)
-        make_factors(7)
-        make_factors(6)
-        make_gated(6)
-        make_gated(7)
-        quantise(0)
-        gather_dy_planes(2)
+        make_part(2)
+        da_by_part(0, nc.gpsimd)
+        da_by_part(2, nc.gpsimd)
+        make_gated(3)
         gather_dy_words(2, 1)
+        gather_dy_words(2, 0)
+        weave(0, turn(0, (1, 0)), scalar_copy)
+        gather_dy_planes(2)
+        make_part(3)
         gather_dy_planes(3)
+        make_silu(7)
+        make_tanh(7)
+        make_gated_on_scalar(5)
+        make_gated_on_scalar(7)
+        make_dh(4)
+        make_dh(5)
+        quantise(0)
+        make_part(4)
         gather_dy_words(3, 0)
-        dx = make_dx(0)
-        stage(0, LOW, dx, scalar_copy)
-        stage(0, HIGH, dx, scalar_copy)
-        for r in (2, 3, 1):
-            scatter(r, (0,), scalar_scatter)
-
-        da_by_part(4)
         gather_dy_words(3, 1)
-        turned = turn(1)
-        da_by_part(5)
+        make_part(5)
+        dx = make_dx(0)
+        stage_early(0, dx, scalar_copy)
+        stage_late(0, dx, scalar_copy)
+        scatter_early(2, 0, scalar_scatter)
+        scatter_late(3, 0, C, scalar_scatter)
+        da_by_part(3, nc.gpsimd)
+        make_gated(4)
+        turned = turn(1, (1, 0))
+        make_dh(6)
+        make_dh(7)
         weave(1, turned, vector_copy)
+        make_part(6)
         quantise(1)
-        da_by_part(6)
-        da_by_part(7)
+        scatter_early(0, 0, vector_copy)
+        da_by_part(4, nc.gpsimd)
+        da_by_part(5, nc.gpsimd)
+        make_gated(6)
+        da_by_part(6, nc.gpsimd)
         dx = make_dx(1)
-        stage(1, LOW, dx, scalar_copy)
-        stage(1, HIGH, dx, scalar_copy)
-        for r in (2, 3):
-            scatter(r, (1,), scalar_scatter)
-        scatter(0, (0,), vector_copy)
-        weave(2, turn(2), vector_copy)
-        scatter(1, (1,), vector_copy)
-
-        turned = turn(3)
+        stage_early(1, dx, scalar_copy)
+        stage_late(1, dx, vector_copy)
+        scatter_early(2, 1, scalar_scatter)
+        scatter_early(0, 1, scalar_scatter)
+        scatter_late(3, C, C, scalar_scatter)
+        weave(2, turn(2, (1, 0)), vector_copy)
+        make_part(7)
         quantise(2)
-        weave(3, turned, vector_copy)
+        scatter_late(1, 0, 3 * P, vector_copy)
+        da_by_part(7, nc.gpsimd)
+        dx2 = make_dx(2)
+        stage_row(2, 2, dx2, scalar_copy)
+        stage_late(2, dx2, scalar_copy)
+        scatter_early(2, 2, scalar_scatter)
+        scatter_late(3, 2 * C, P, scalar_scatter)
+        weave(3, turn(3, (1, 0)), vector_copy)
+        stage_row(2, 0, dx2, vector_copy)
         quantise(3)
-        dx = make_dx(2)
-        stage(2, LOW, dx, scalar_copy)
-        stage(2, HIGH, dx, scalar_copy)
-        scatter(0, (1, 2), vector_copy)
-        scatter(2, (2,), scalar_scatter)
+        scatter_early(0, 2, vector_copy)
         dx = make_dx(3)
-        stage(3, LOW, dx, scalar_copy)
-        stage(3, HIGH, dx, vector_copy)
-        scatter(0, (3,), vector_copy)
+        stage_early(3, dx, vector_copy)
+        stage_late(3, dx, scalar_copy)
+        scatter_early(0, 3, vector_copy)
         store(0, nc.sync)
-        scatter(3, (2,), scalar_scatter)
-        scatter(2, (3,), scalar_scatter)
+        scatter_early(2, 3, scalar_scatter)
         store(2, nc.sync)
-        scatter(3, (3,), scalar_scatter)
+        scatter_late(3, 2 * C + P, 3 * P, scalar_scatter)
         store(3, nc.scalar)
-        scatter(1, (2, 3), vector_copy)
+        scatter_late(1, 3 * P, T - 3 * P, vector_copy)
         store(1, nc.sync)

@@ -39,8 +39,8 @@ TOKENS = PACK * T
 
 GUESTS = {
     "slot_x_0": (("slot_x_plane_4", 2 * SCALES),),
-    "tanh_half2": (("slot_dy0_4", WORDS), ("gated3", WIDE),),
-    "slot_dy1_2": (("slot_dy1_4", WORDS),),
+    "tanh_half2": (("gated3", WIDE),),
+    "slot_dy1_2": (("slot_dy1_4", WORDS), ("slot_dy0_4", WORDS),),
     "da0": (("slot_dy_planes_4", SCALES), ("slot_dy_planes_6", SCALES), ("part3", WIDE), ("silu_neg7", WIDE), ("tanh_half7", WIDE), ("gated5", WIDE),),
     "interleaved0": (("part4", WIDE), ("part5", WIDE), ("slot_dy0_6", WORDS), ("slot_dy1_6", WORDS), ("da3", DA), ("gated4", WIDE),),
     "slot_dy0_6": (("codes1", WORDS),),
@@ -78,8 +78,15 @@ def seat_plan():
 
 A_BANKS = (0, 1, 2, 3, 0, 1, 2, 3)
 DH_BANKS = (4, 5, 6, 7, 4, 5, 1, 7)
-DX_BANKS = ((0, 1), (2, 3), (6, 0), (4, 5))
+DX_PLACES = (
+    ((0, 0), (1, 0), (0, 1), (1, 1)),
+    ((2, 0), (3, 0), (2, 1), (3, 1)),
+    ((2, 0), (0, 0), (6, 0), (0, 1)),
+    ((4, 0), (5, 0), (4, 1), (5, 1)),
+)
+DX_ORDER = ((0, 2, 1, 3), (0, 2, 1, 3), (0, 2, 1, 3), (0, 2, 1, 3))
 TURN_BANKS = (6, 0, 1, 7)
+FIRST_PIECE = 448
 GATE_BANK = 7
 
 
@@ -155,12 +162,12 @@ def tile_moe_rec_mlp_silu_kernel(
         load_planes(dy_planes, dy_scales)
         w1.append(load_pass("w1_1", w1_words[1, 0]))
         w1.append(load_pass("w1_2", w1_words[2, 0]))
+        w2 = load_passes("w2_0", w2t_words[0])
         w2_scale_rows = w2t_scales.rearrange("e s (q r) i -> r q (e s) i", r=QUAD_ROWS)
         for r in range(QUAD_ROWS):
-            nc.sync.dma_start(
+            nc.gpsimd.dma_start(
                 w2_planes[r:P:QUAD, :].bitcast(I32).rearrange("q (j w) -> q j w", j=E * DY_PASSES), w2_scale_rows[r].bitcast(I32)
             )
-        w2 = load_passes("w2_0", w2t_words[0])
         w1.append(load_pass("w1_3", w1_words[3, 0]))
         w2.extend(load_passes("w2_1", w2t_words[1]))
         w2.extend(load_passes("w2_2", w2t_words[2]))
@@ -214,13 +221,19 @@ def tile_moe_rec_mlp_silu_kernel(
                 stop=True,
             )
 
+        def by_halves(sums):
+            return sums.rearrange("q (p u e) -> q u p e", u=2, e=2)
+
+        def in_halves(values):
+            return values.rearrange("q (u p e) -> q u p e", u=2, e=2)
+
         def make_silu(j):
             silu_neg[j] = placed(H, F32, f"silu_neg{j}")
-            nc.scalar.activation(silu_neg[j][:], a_ps[j][:], ACT.Silu, bias=no_bias[:], scale=-1.0)
+            nc.scalar.activation(in_halves(silu_neg[j]), by_halves(a_ps[j][:]), ACT.Silu, bias=no_bias[:], scale=-1.0)
 
         def make_tanh(j):
             tanh_half[j] = placed(H, F32, f"tanh_half{j}")
-            nc.scalar.activation(tanh_half[j][:], a_ps[j][:], ACT.Tanh, scale=0.5)
+            nc.scalar.activation(in_halves(tanh_half[j]), by_halves(a_ps[j][:]), ACT.Tanh, scale=0.5)
 
         def make_gated(j):
             gated[j] = placed(H, F32, f"gated{j}")
@@ -253,11 +266,14 @@ def tile_moe_rec_mlp_silu_kernel(
 
         def da_by_slope(j):
             da[j] = placed(H, BF16, f"da{j}")
-            nc.vector.tensor_tensor(da[j][:], slope[j][:], dh_ps[j][:], ALU.mult)
+            nc.vector.tensor_tensor(in_halves(da[j]), in_halves(slope[j]), by_halves(dh_ps[j][:]), ALU.mult)
 
         def make_part(j):
             part[j] = placed(H, F32, f"part{j}")
-            nc.vector.scalar_tensor_tensor(part[j][:], tanh_half[j][:], 1.0, dh_ps[j][:], ALU.add, ALU.mult)
+            for u in range(2):
+                nc.vector.scalar_tensor_tensor(
+                    in_halves(part[j])[:, u], in_halves(tanh_half[j])[:, u], 1.0, by_halves(dh_ps[j][:])[:, u], ALU.add, ALU.mult
+                )
 
         def da_by_part(j, engine):
             da[j] = placed(H, BF16, f"da{j}")
@@ -268,7 +284,7 @@ def tile_moe_rec_mlp_silu_kernel(
             for c in order:
                 pairs = da[PER_EXPERT * e + c][:].bitcast(F32)
                 for u in range(2):
-                    nc.tensor.transpose(turned[:, c, u, :], pairs[:, u : H // 2 : 2], ident[:])
+                    nc.tensor.transpose(turned[:, c, u, :], pairs[:, u * P : (u + 1) * P], ident[:])
             return turned
 
         def weave(e, turned, copy):
@@ -283,37 +299,38 @@ def tile_moe_rec_mlp_silu_kernel(
             nc.vector.quantize_mx(out=codes[e][:].bitcast(FP8X4), scales=da_plane[e][:], in_=interleaved[e][:])
 
         def make_dx(e):
-            halves = []
-            for half in (EARLY, LATE):
-                dx_ps = bank([P, len(HALF_ROWS[half]), C], f"dx_ps{e}_{half}", DX_BANKS[e][half])
-                for place, r in enumerate(HALF_ROWS[half]):
-                    rows = slice(r * P, (r + 1) * P)
-                    nc.tensor.matmul_mx(
-                        dx_ps[:, place, :],
-                        lhsT=w1t[e][:, rows].bitcast(FP8X4),
-                        lhsT_scale=w1t_planes[QUAD_ROWS * e :, rows],
-                        rhs=codes[e][:].bitcast(FP8X4),
-                        rhs_scale=da_plane[e][:],
-                        start=True,
-                        stop=True,
-                    )
-                halves.append(dx_ps)
-            return halves
+            tiles, rows_of = {}, {}
+            for r in DX_ORDER[e]:
+                bank_index, place = DX_PLACES[e][r]
+                if bank_index not in tiles:
+                    tiles[bank_index] = bank([P, 2, C], f"dx_ps{e}_{bank_index}", bank_index)
+                rows = slice(r * P, (r + 1) * P)
+                nc.tensor.matmul_mx(
+                    tiles[bank_index][:, place, :],
+                    lhsT=w1t[e][:, rows].bitcast(FP8X4),
+                    lhsT_scale=w1t_planes[QUAD_ROWS * e :, rows],
+                    rhs=codes[e][:].bitcast(FP8X4),
+                    rhs_scale=da_plane[e][:],
+                    start=True,
+                    stop=True,
+                )
+                rows_of[r] = tiles[bank_index]
+            return rows_of
 
         staged_late = keep.tile([P, len(HALF_ROWS[LATE]), T], F32, name="staged_late")
 
         def stage_late(e, dx, copy):
-            copy(staged_late[:, :, e * C : (e + 1) * C], dx[LATE][:])
+            copy(staged_late[:, :, e * C : (e + 1) * C], dx[HALF_ROWS[LATE][0]][:])
 
         def stage_early(e, dx, copy):
             tile = placed(len(HALF_ROWS[EARLY]) * C, F32, f"staged_early{e}").rearrange("p (r c) -> p r c", c=C)
-            copy(tile, dx[EARLY][:])
+            copy(tile, dx[HALF_ROWS[EARLY][0]][:])
             for place, r in enumerate(HALF_ROWS[EARLY]):
                 staged[r, e] = tile[:, place, :]
 
         def stage_row(e, r, dx, copy):
             tile = placed(C, F32, f"staged{e}_row{r}")
-            copy(tile[:], dx[EARLY][:, HALF_ROWS[EARLY].index(r), :])
+            copy(tile[:], dx[r][:, DX_PLACES[e][r][1], :])
             staged[r, e] = tile[:]
 
         def window(r, first, count):
@@ -374,8 +391,8 @@ def tile_moe_rec_mlp_silu_kernel(
         gather_dy_planes(3)
         make_silu(7)
         make_tanh(7)
-        make_gated_on_scalar(5)
         make_gated_on_scalar(7)
+        make_gated_on_scalar(5)
         make_dh(4)
         make_dh(5)
         quantise(0)
@@ -405,12 +422,12 @@ def tile_moe_rec_mlp_silu_kernel(
         stage_early(1, dx, scalar_copy)
         stage_late(1, dx, vector_copy)
         scatter_early(2, 1, scalar_scatter)
-        scatter_early(0, 1, scalar_scatter)
         scatter_late(3, C, C, scalar_scatter)
+        scatter_early(0, 1, scalar_scatter)
         weave(2, turn(2, (1, 0)), vector_copy)
         make_part(7)
         quantise(2)
-        scatter_late(1, 0, 3 * P, vector_copy)
+        scatter_late(1, 0, FIRST_PIECE, vector_copy)
         da_by_part(7, nc.gpsimd)
         dx2 = make_dx(2)
         stage_row(2, 2, dx2, scalar_copy)
@@ -430,5 +447,5 @@ def tile_moe_rec_mlp_silu_kernel(
         store(2, nc.sync)
         scatter_late(3, 2 * C + P, 3 * P, scalar_scatter)
         store(3, nc.scalar)
-        scatter_late(1, 3 * P, T - 3 * P, vector_copy)
+        scatter_late(1, FIRST_PIECE, T - FIRST_PIECE, vector_copy)
         store(1, nc.sync)

from contextlib import ExitStack

import concourse.mybir as mybir
from concourse.masks import make_identity

K, T, E, C, H, N = 512, 1024, 4, 256, 512, 1024
FLOPS = 2 * E * C * (K * H + N * H + H * K)

F32 = mybir.dt.float32
BF16 = mybir.dt.bfloat16
I32 = mybir.dt.int32
U32 = mybir.dt.uint32
U16 = mybir.dt.uint16
U8 = mybir.dt.uint8
FP8X4 = mybir.dt.float8_e4m3fn_x4
ACT = mybir.ActivationFunctionType
ALU = mybir.AluOpType

P = 128
PACK = 4
QUADS = 4
QUAD = P // QUADS
QUAD_ROWS = 4
PER_EXPERT = C // P
GROUPS = E * PER_EXPERT
EARLY, LATE = 0, 1
HALF_ROWS = ((0, 2), (1, 3))
DY_PASSES = N // (P * PACK)
STRIPE = 16
MX_ALIGN = 64
BANK = 2048
ITEM_BYTES = {F32: 4, I32: 4, U32: 4, BF16: 2, U8: 1}

WORDS = PACK * C
SCALES = C
DA = 2 * H
WIDE = PACK * H
TOKENS = PACK * T

GUESTS = {
    "slot_x_0": (("slot_x_plane_4", 2 * SCALES),),
    "tanh_half2": (("gated3", WIDE),),
    "slot_dy1_2": (("slot_dy1_4", WORDS), ("slot_dy0_4", WORDS),),
    "da0": (("slot_dy_planes_4", SCALES), ("slot_dy_planes_6", SCALES), ("part3", WIDE), ("silu_neg7", WIDE), ("tanh_half7", WIDE), ("gated5", WIDE),),
    "interleaved0": (("part4", WIDE), ("part5", WIDE), ("slot_dy0_6", WORDS), ("slot_dy1_6", WORDS), ("da3", DA), ("gated4", WIDE),),
    "slot_dy0_6": (("codes1", WORDS),),
    "slot_dy1_6": (("window0", TOKENS),),
    "interleaved1": (("da5", DA), ("gated6", WIDE),),
    "da4": (("window1", TOKENS), ("part7", WIDE),),
    "da6": (("staged2_row0", WORDS),),
}
HOSTS = (
    ("slot_x_0", WORDS // 2),
    ("tanh_half2", WIDE),
    ("slot_dy1_2", WORDS),
    ("da0", DA),
    ("interleaved0", WIDE),
    ("interleaved1", WIDE),
    ("da4", DA),
    ("da6", DA),
)


def lay_out(name, size, at, seats):
    end = at
    for guest, guest_size in GUESTS.get(name, ()):
        end = end + lay_out(guest, guest_size, end, seats)
    seats[name] = (at, max(size, end - at))
    return seats[name][1]


def seat_plan():
    seats, at = {}, 0
    for name, size in HOSTS:
        at = at + lay_out(name, size, at, seats)
    return seats


A_BANKS = (0, 1, 2, 3, 0, 1, 2, 3)
DH_BANKS = (4, 5, 6, 7, 4, 5, 1, 7)
DX_PLACES = (
    ((0, 0), (1, 0), (0, 1), (1, 1)),
    ((2, 0), (3, 0), (2, 1), (3, 1)),
    ((2, 0), (0, 0), (6, 0), (0, 1)),
    ((4, 0), (5, 0), (4, 1), (5, 1)),
)
DX_ORDER = ((0, 2, 1, 3), (0, 2, 1, 3), (0, 2, 1, 3), (0, 2, 1, 3))
TURN_BANKS = (6, 0, 1, 7)
FIRST_PIECE = 448
GATE_BANK = 7


def tile_moe_rec_mlp_silu_kernel(
    tc, x_words, x_scales, dy_words, dy_scales, w1_words, w1_scales, w2t_words, w2t_scales, w1t_words, w1t_scales, gate, offs, out
):
    nc = tc.nc
    seat = seat_plan()
    with ExitStack() as ctx:
        keep = ctx.enter_context(tc.tile_pool(name="keep", bufs=1))
        seats = ctx.enter_context(tc.tile_pool(name="seats", bufs=1))
        banks = ctx.enter_context(tc.psum_pool(name="banks", bufs=1))

        offsets = keep.tile([P, T // STRIPE], U16, name="offsets")
        nc.sync.dma_start(offsets[:], offs)

        def listed(first_slot, count):
            return offsets[:, first_slot // STRIPE : (first_slot + count) // STRIPE]

        def placed(width, dtype, name):
            if name not in seat:
                return keep.tile([P, width], dtype, name=name, align_bytes=MX_ALIGN)[:]
            offset, size = seat[name]
            return seats.tile([P, size // ITEM_BYTES[dtype]], dtype, name=name, offset=offset, align_bytes=MX_ALIGN)[:, 0:width]

        def bank(shape, name, bank_index):
            return banks.tile(shape, F32, name=name, offset=bank_index * BANK)

        def zeroed_planes(name, width):
            tile = keep.tile([P, width], U8, name=name, align_bytes=MX_ALIGN)
            nc.vector.memset(tile[:].bitcast(I32), 0)
            return tile

        def load_planes(tile, planes):
            rows = planes.shape[0] * QUAD_ROWS
            for q in range(QUADS):
                source = planes[:, QUAD_ROWS * q : QUAD_ROWS * (q + 1), :]
                nc.sync.dma_start(tile[QUAD * q : QUAD * q + rows, :].bitcast(I32), source.bitcast(I32))

        def load_pass(name, words):
            tile = placed(words.shape[1], I32, name)
            nc.sync.dma_start(tile[:], words.rearrange("p c d -> p (c d)").bitcast(I32))
            return tile[:]

        def load_passes(name, words):
            tile = keep.tile([P, words.shape[0], words.shape[2]], I32, name=name, align_bytes=MX_ALIGN)
            nc.sync.dma_start(tile[:], words.rearrange("j p c d -> p j (c d)").bitcast(I32))
            return [tile[:, j, :] for j in range(words.shape[0])]

        zero = keep.tile([P, 1], F32, name="zero")
        no_bias = keep.tile([P, 1], F32, name="no_bias")
        nc.vector.memset(zero[:], 0.0)
        nc.scalar.activation(no_bias[:], zero[:], ACT.Silu)

        w1_planes = zeroed_planes("w1_planes", H)
        w2_planes = zeroed_planes("w2_planes", E * DY_PASSES * H)
        dy_planes = zeroed_planes("dy_planes", T)
        w1t_planes = zeroed_planes("w1t_planes", K)

        ident = keep.tile([P, P], F32, name="ident")
        make_identity(nc, ident[:])

        x_plane = keep.tile([P, T], U8, name="x_plane", align_bytes=MX_ALIGN)
        for q in range(QUADS):
            source = x_scales[:, QUAD_ROWS * q : QUAD_ROWS * (q + 1), :].bitcast(I32)
            nc.sync.dma_start(x_plane[QUAD * q : QUAD * (q + 1), :].bitcast(I32), source.to_broadcast([QUAD // QUAD_ROWS, QUAD_ROWS, T // PACK]))
        xw = load_pass("xw", x_words[0]).bitcast(U32)
        w1 = [load_pass("w1_0", w1_words[0, 0])]
        load_planes(w1_planes, w1_scales[:, 0])
        gate_rows = placed(P, F32, "gate_rows")
        nc.sync.dma_start(gate_rows[:], gate[0 : P // GROUPS, :].rearrange("a (c m) -> (a c) m", m=P))
        dyw = [load_pass(f"dyw{s}", dy_words[s]).bitcast(U32) for s in range(DY_PASSES)]
        load_planes(dy_planes, dy_scales)
        w1.append(load_pass("w1_1", w1_words[1, 0]))
        w1.append(load_pass("w1_2", w1_words[2, 0]))
        w2 = load_passes("w2_0", w2t_words[0])
        w2_scale_rows = w2t_scales.rearrange("e s (q r) i -> r q (e s) i", r=QUAD_ROWS)
        for r in range(QUAD_ROWS):
            nc.gpsimd.dma_start(
                w2_planes[r:P:QUAD, :].bitcast(I32).rearrange("q (j w) -> q j w", j=E * DY_PASSES), w2_scale_rows[r].bitcast(I32)
            )
        w1.append(load_pass("w1_3", w1_words[3, 0]))
        w2.extend(load_passes("w2_1", w2t_words[1]))
        w2.extend(load_passes("w2_2", w2t_words[2]))
        load_planes(w1t_planes, w1t_scales[:, 0])
        w1t = load_passes("w1t", w1t_words[:, 0])
        w2.extend(load_passes("w2_3", w2t_words[3]))

        gate_ps = bank([P, H], "gate_ps", GATE_BANK)
        nc.tensor.transpose(gate_ps[:, 0:P], gate_rows[:], ident[:])
        neg_half_gate = keep.tile([P, GROUPS], F32, name="neg_half_gate")
        nc.scalar.activation(neg_half_gate[:], gate_ps[:, 0:GROUPS], ACT.Copy, scale=-0.5)
        half_gate = keep.tile([P, GROUPS], F32, name="half_gate")
        nc.scalar.activation(half_gate[:], gate_ps[:, 0:GROUPS], ACT.Copy, scale=0.5)

        slot_x_plane, slot_x, slot_dy_planes = {}, {}, {}
        slot_dy = [{} for s in range(DY_PASSES)]

        def gather(by_group, name, window, dtype, first, count):
            tile = placed(count * P, dtype, f"{name}_{first}")
            nc.vector.tensor_copy(tile[:], window.indirect(listed(first * P, count * P)))
            for c in range(count):
                by_group[first + c] = tile[:, c * P : (c + 1) * P]

        def gather_x_plane(first, count):
            gather(slot_x_plane, "slot_x_plane", x_plane[:], U8, first, count)

        def gather_x_words(first, count):
            gather(slot_x, "slot_x", xw, U32, first, count)

        def gather_dy_planes(e):
            gather(slot_dy_planes, "slot_dy_planes", dy_planes[:], U8, e * PER_EXPERT, PER_EXPERT)

        def gather_dy_words(e, s):
            gather(slot_dy[s], f"slot_dy{s}", dyw[s], U32, e * PER_EXPERT, PER_EXPERT)

        silu_neg, tanh_half, gated, slope, da = {}, {}, {}, {}, {}
        interleaved, codes, da_plane, windows = {}, {}, {}, {}

        a_ps, dh_ps, part, staged = {}, {}, {}, {}

        def make_a(j):
            a_ps[j] = bank([P, H], f"a_ps{j}", A_BANKS[j])
            e = j // PER_EXPERT
            nc.tensor.matmul_mx(
                a_ps[j][:],
                lhsT=slot_x[j].bitcast(FP8X4),
                lhsT_scale=slot_x_plane[j],
                rhs=w1[e].bitcast(FP8X4),
                rhs_scale=w1_planes[QUAD_ROWS * e :, :],
                start=True,
                stop=True,
            )

        def by_halves(sums):
            return sums.rearrange("q (p u e) -> q u p e", u=2, e=2)

        def in_halves(values):
            return values.rearrange("q (u p e) -> q u p e", u=2, e=2)

        def make_silu(j):
            silu_neg[j] = placed(H, F32, f"silu_neg{j}")
            nc.scalar.activation(in_halves(silu_neg[j]), by_halves(a_ps[j][:]), ACT.Silu, bias=no_bias[:], scale=-1.0)

        def make_tanh(j):
            tanh_half[j] = placed(H, F32, f"tanh_half{j}")
            nc.scalar.activation(in_halves(tanh_half[j]), by_halves(a_ps[j][:]), ACT.Tanh, scale=0.5)

        def make_gated(j):
            gated[j] = placed(H, F32, f"gated{j}")
            nc.gpsimd.tensor_scalar(gated[j][:], silu_neg[j][:], -1.0, neg_half_gate[:, j : j + 1], ALU.add, ALU.mult)

        def make_gated_on_scalar(j):
            gated[j] = placed(H, F32, f"gated{j}")
            nc.scalar.activation(gated[j][:], silu_neg[j][:], ACT.Identity, bias=half_gate[:, j : j + 1], scale=neg_half_gate[:, j : j + 1])

        def make_slope(j):
            plus_one = placed(H, F32, f"plus_one{j}")
            nc.gpsimd.tensor_scalar(plus_one[:], tanh_half[j][:], 1.0, 1.0, ALU.mult, ALU.add)
            slope[j] = placed(H, F32, f"slope{j}")
            nc.gpsimd.tensor_tensor(slope[j][:], gated[j][:], plus_one[:], ALU.mult)

        def make_dh(j):
            e = j // PER_EXPERT
            dh_ps[j] = bank([P, H], f"dh_ps{j}", DH_BANKS[j])
            for s in range(DY_PASSES):
                w2_pass = DY_PASSES * e + s
                nc.tensor.matmul_mx(
                    dh_ps[j][:],
                    lhsT=slot_dy[s][j].bitcast(FP8X4),
                    lhsT_scale=slot_dy_planes[j][QUAD_ROWS * s :, :],
                    rhs=w2[w2_pass].bitcast(FP8X4),
                    rhs_scale=w2_planes[:, w2_pass * H : (w2_pass + 1) * H],
                    start=(s == 0),
                    stop=(s == DY_PASSES - 1),
                )

        def da_by_slope(j):
            da[j] = placed(H, BF16, f"da{j}")
            nc.vector.tensor_tensor(in_halves(da[j]), in_halves(slope[j]), by_halves(dh_ps[j][:]), ALU.mult)

        def make_part(j):
            part[j] = placed(H, F32, f"part{j}")
            for u in range(2):
                nc.vector.scalar_tensor_tensor(
                    in_halves(part[j])[:, u], in_halves(tanh_half[j])[:, u], 1.0, by_halves(dh_ps[j][:])[:, u], ALU.add, ALU.mult
                )

        def da_by_part(j, engine):
            da[j] = placed(H, BF16, f"da{j}")
            engine.tensor_tensor(da[j][:], gated[j][:], part[j][:], ALU.mult)

        def turn(e, order):
            turned = bank([P, PER_EXPERT, 2, P], f"turned{e}", TURN_BANKS[e])
            for c in order:
                pairs = da[PER_EXPERT * e + c][:].bitcast(F32)
                for u in range(2):
                    nc.tensor.transpose(turned[:, c, u, :], pairs[:, u * P : (u + 1) * P], ident[:])
            return turned

        def weave(e, turned, copy):
            interleaved[e] = placed(PER_EXPERT * H, BF16, f"interleaved{e}")
            copy(
                interleaved[e][:].bitcast(F32).rearrange("p (c m u) -> p c m u", c=PER_EXPERT, u=2), turned[:].rearrange("p c u m -> p c m u")
            )

        def quantise(e):
            codes[e] = placed(C, U32, f"codes{e}")
            da_plane[e] = placed(C, U8, f"da_plane{e}")
            nc.vector.quantize_mx(out=codes[e][:].bitcast(FP8X4), scales=da_plane[e][:], in_=interleaved[e][:])

        def make_dx(e):
            tiles, rows_of = {}, {}
            for r in DX_ORDER[e]:
                bank_index, place = DX_PLACES[e][r]
                if bank_index not in tiles:
                    tiles[bank_index] = bank([P, 2, C], f"dx_ps{e}_{bank_index}", bank_index)
                rows = slice(r * P, (r + 1) * P)
                nc.tensor.matmul_mx(
                    tiles[bank_index][:, place, :],
                    lhsT=w1t[e][:, rows].bitcast(FP8X4),
                    lhsT_scale=w1t_planes[QUAD_ROWS * e :, rows],
                    rhs=codes[e][:].bitcast(FP8X4),
                    rhs_scale=da_plane[e][:],
                    start=True,
                    stop=True,
                )
                rows_of[r] = tiles[bank_index]
            return rows_of

        staged_late = keep.tile([P, len(HALF_ROWS[LATE]), T], F32, name="staged_late")

        def stage_late(e, dx, copy):
            copy(staged_late[:, :, e * C : (e + 1) * C], dx[HALF_ROWS[LATE][0]][:])

        def stage_early(e, dx, copy):
            tile = placed(len(HALF_ROWS[EARLY]) * C, F32, f"staged_early{e}").rearrange("p (r c) -> p r c", c=C)
            copy(tile, dx[HALF_ROWS[EARLY][0]][:])
            for place, r in enumerate(HALF_ROWS[EARLY]):
                staged[r, e] = tile[:, place, :]

        def stage_row(e, r, dx, copy):
            tile = placed(C, F32, f"staged{e}_row{r}")
            copy(tile[:], dx[r][:, DX_PLACES[e][r][1], :])
            staged[r, e] = tile[:]

        def window(r, first, count):
            if r not in windows:
                windows[r] = placed(T, F32, f"window{r}")
            return windows[r][:].indirect(listed(first, count))

        def scatter_early(r, e, copy):
            copy(window(r, e * C, C), staged[r, e])

        def scatter_late(r, first, count, copy):
            copy(window(r, first, count), staged_late[:, HALF_ROWS[LATE].index(r), first : first + count])

        def scalar_scatter(target, values):
            nc.scalar.activation(target, values, ACT.Copy)

        def store(r, engine):
            engine.dma_start(out[r * P : (r + 1) * P, :], windows[r][:])

        scalar_copy, vector_copy = nc.scalar.copy, nc.vector.tensor_copy

        gather_x_plane(0, 4)
        gather_x_words(0, 1)
        gather_x_words(1, 3)
        gather_x_words(4, 4)
        gather_x_plane(4, 4)
        for e in range(2):
            for s in range(DY_PASSES):
                gather_dy_words(e, s)
            gather_dy_planes(e)
        for j in range(6):
            make_a(j)
            make_silu(j)
            make_tanh(j)
        make_gated(0)
        make_gated(1)
        make_slope(1)
        make_gated(2)
        make_dh(0)
        make_dh(1)
        make_a(6)
        make_a(7)
        make_silu(6)
        make_tanh(6)
        make_dh(2)
        make_dh(3)
        make_part(0)
        da_by_slope(1)
        make_part(2)
        da_by_part(0, nc.gpsimd)
        da_by_part(2, nc.gpsimd)
        make_gated(3)
        gather_dy_words(2, 1)
        gather_dy_words(2, 0)
        weave(0, turn(0, (1, 0)), scalar_copy)
        gather_dy_planes(2)
        make_part(3)
        gather_dy_planes(3)
        make_silu(7)
        make_tanh(7)
        make_gated_on_scalar(7)
        make_gated_on_scalar(5)
        make_dh(4)
        make_dh(5)
        quantise(0)
        make_part(4)
        gather_dy_words(3, 0)
        gather_dy_words(3, 1)
        make_part(5)
        dx = make_dx(0)
        stage_early(0, dx, scalar_copy)
        stage_late(0, dx, scalar_copy)
        scatter_early(2, 0, scalar_scatter)
        scatter_late(3, 0, C, scalar_scatter)
        da_by_part(3, nc.gpsimd)
        make_gated(4)
        turned = turn(1, (1, 0))
        make_dh(6)
        make_dh(7)
        weave(1, turned, vector_copy)
        make_part(6)
        quantise(1)
        scatter_early(0, 0, vector_copy)
        da_by_part(4, nc.gpsimd)
        da_by_part(5, nc.gpsimd)
        make_gated(6)
        da_by_part(6, nc.gpsimd)
        dx = make_dx(1)
        stage_early(1, dx, scalar_copy)
        stage_late(1, dx, vector_copy)
        scatter_early(2, 1, scalar_scatter)
        scatter_late(3, C, C, scalar_scatter)
        scatter_early(0, 1, scalar_scatter)
        weave(2, turn(2, (1, 0)), vector_copy)
        make_part(7)
        quantise(2)
        scatter_late(1, 0, FIRST_PIECE, vector_copy)
        da_by_part(7, nc.gpsimd)
        dx2 = make_dx(2)
        stage_row(2, 2, dx2, scalar_copy)
        stage_late(2, dx2, scalar_copy)
        scatter_early(2, 2, scalar_scatter)
        scatter_late(3, 2 * C, P, scalar_scatter)
        weave(3, turn(3, (1, 0)), vector_copy)
        stage_row(2, 0, dx2, vector_copy)
        quantise(3)
        scatter_early(0, 2, vector_copy)
        dx = make_dx(3)
        stage_early(3, dx, vector_copy)
        stage_late(3, dx, scalar_copy)
        scatter_early(0, 3, vector_copy)
        store(0, nc.sync)
        scatter_early(2, 3, scalar_scatter)
        store(2, nc.sync)
        scatter_late(3, 2 * C + P, 3 * P, scalar_scatter)
        store(3, nc.scalar)
        scatter_late(1, FIRST_PIECE, T - FIRST_PIECE, vector_copy)
        store(1, nc.sync)
